import numpy as np, ml_dtypes
CORES = [56,57,58,59,60,61,62]
N = 7
BF = ml_dtypes.bfloat16
W, H, LG = 4096, 2048, 12
B, I, RO, A, C, DS = 16, 224, 5, 3, 3, (1, 3)
def pick(p, x):
    return np.take_along_axis(p, x, 3)
def swap(p, s, t):
    p = np.array(p); a = np.array(p[..., t:B * I:B])
    m = np.array(np.broadcast_to(B * np.arange(I) + (s[:, :, :1] & (B - 1)), a.shape))
    b = np.take_along_axis(p, m, 3); np.put_along_axis(p, m, a, 3); p[..., t:B * I:B] = b
    return p
def shuffled(rng):
    return rng.permuted(np.tile(np.arange(W), (N, 8, 16, 1)), axis=3)
def lanes(rng):
    return rng.integers(0, W, (N, 8, 16, I))
def join(p, s, t):
    return {"pm": (p[..., :H] + W * p[..., H:]).reshape(N, 128, H).astype(np.int32), "sa": s.reshape(N, 128, I).astype(np.int32), "ta": t.reshape(N, 128, I).astype(np.int32)}
def halves(pm):
    w = np.asarray(pm).astype(np.int64); return np.concatenate([w & (W - 1), w >> LG], axis=-1)
def setup_inputs(rng):
    return join(shuffled(rng), lanes(rng), lanes(rng))
def setup_inputs_spread(rng):
    size = np.exp2(rng.integers(0, 14, (N, 8, 16, 1)))
    p = np.argsort(np.arange(W) + size * rng.random((N, 8, 16, W)), axis=3)
    s, t = [(np.exp2(LG * rng.random((N, 8, 1, I))) * rng.random((N, 8, 16, I))).astype(np.int64) for _ in range(2)]
    return join(p, s, t)
def setup_inputs_ends(rng):
    ty = (np.arange(8)[:, None] + 1 + ((np.arange(16) + 1) % 16) // 4) % 2
    p = np.zeros((N, 8, 16, W), np.int64); end, low, n = B * (I - 1), 2 * B, len(DS)
    for v in (0, 1):
        big, small = (end, low) if v == 0 else (low, end)
        at = {big: W - 1, small: 0, end - H: W - 2 if v == 0 else 1}
        x = [W - 2 - j for j in range(n + 2)]; y = [0] + [j + 2 for j in range(n + 1)]
        at.update(zip(x, x[1:] + [big - 1])); at.update(zip(y, y[1:] + [small - 1]))
        a = np.array([c for c in at]); b = np.array([at[c] for c in at])
        ra = np.setdiff1d(np.arange(W), a); rb = np.setdiff1d(np.arange(W), b); q = np.zeros((N * int(np.count_nonzero(ty == v)), W), np.int64)
        q[:, a] = b; q[:, ra] = rng.permuted(np.tile(rb, (len(q), 1)), axis=1)
        p[:, ty == v] = q.reshape(N, -1, W)
    s = (W - 1) * rng.integers(0, 2, (N, 8, 16, I)); t = (W - 1) * rng.integers(0, 2, (N, 8, 16, I)); top = (W - 1) * (ty == 0)
    s[..., I - 1] = top; t[..., I - 1] = top; s[..., 2] = W - 1 - top; t[..., 2] = W - 1 - top
    return join(p, s, t)
def setup_inputs_corners(rng):
    p = shuffled(rng); x = np.arange(W)
    for r in range(N):
        kind = rng.permutation(8)
        for g in range(8):
            c = kind[g]
            if c == 5: p[r, g] = rng.permuted(x.reshape(W // B, B), axis=1).reshape(W)
            elif c == 6: p[r, g] = np.array(p[r, g, 0])
            elif c < 5: p[r, g] = (x, W - 1 - x, (x + 1) & (W - 1), (x - 1) & (W - 1), x ^ 1)[c]
    u = p[..., 0:B * I:B]; z = rng.integers(0, 4, (N, 8, 16, I))
    aim = np.where(z == 0, 0, np.where(z == 1, W - 1, np.where(z == 2, B * np.arange(I), lanes(rng))))
    mode = ((np.arange(N)[:, None] + np.arange(8)) % 4)[:, :, None]
    dig = np.where(mode == 0, 0, np.where(mode == 1, B - 1, np.where(mode == 2, 1, rng.integers(0, B, (N, 8, I)))))
    back = np.argsort(p[:, :, 0], axis=2)
    aim[:, :, 0] = np.take_along_axis(back, B * rng.integers(0, W // B, (N, 8, I)) + dig, 2)
    return join(p, (aim - u) & (W - 1), rng.choice(np.array([0, 1, W - 2, W - 1]), (N, 8, 16, I)))
def setup_inputs_crowd(rng):
    p = shuffled(rng); place = rng.integers(0, W, (N, 8, 16, 1)); aim = np.array(np.broadcast_to(place, (N, 8, 16, I)))
    i = int(rng.integers(0, I)); aim[:, 1::4, :, i] = (aim[:, 1::4, :, i] + 1) & (W - 1)
    aim[:, 2::4] = (W - 1) * rng.integers(0, 2, (N, 2, 16, I)); aim[:, 3::4] = place[:, 3::4, :1]
    t = np.array(np.broadcast_to(rng.integers(0, W, (N, 8, 1, 1)), (N, 8, 16, I)))
    return join(p, (aim - p[..., 0:B * I:B]) & (W - 1), t)
def setup_inputs_calm(rng):
    p = shuffled(rng); s = lanes(rng); n = W // B
    a = B * rng.permuted(np.tile(np.arange(n), (N, 8, B, 1)), axis=3) + rng.permuted(np.tile(np.arange(B), (N, 8, 1)), axis=2)[..., None]
    p[:, :, 0] = a.swapaxes(2, 3).reshape(N, 8, W)
    lone = np.arange(I) == rng.integers(0, I, (N, 8, 1))
    s[:, :, 0] = B * (s[:, :, 0] // B) + rng.integers(0, B, (N, 8, 1))
    s[:, 1::2, 0] ^= lone[:, 1::2].astype(np.int64)
    q, w, hist, back = p, s, [], []
    for t in range(RO):
        if t: w = np.roll(w, (A, C), axis=(0, 1))
        h = np.roll(q, (-A * t, -C * t), axis=(0, 1)); x = np.zeros_like(h)
        np.put_along_axis(x, h, np.broadcast_to(np.arange(W), h.shape), 3); hist.append(h); back.append(x)
        if t < RO - 1: w = pick(q, (w + q[..., t:B * I:B]) & (W - 1)); q = swap(q, w, t)
    g = np.arange(8)[:, None, None]; r = np.arange(N)[:, None, None, None]; j = (g >> 1) + 4 * r
    full = (g & 1) == 1; top = (W - 1) * (j & 1); few = (g + r) & 3
    when = np.array(np.broadcast_to(np.where(full, 1 + (j >> 1) % (RO - 1), 1 + np.arange(I) % (RO - 1)), (N, 8, 16, I)))
    want = np.where(rng.random((N, 8, 16, I)) < 0.5, few, W - 1 - (few & 1))
    for t in range(1, RO):
        e = hist[t][..., t:B * I:B]
        for v in (0, W - 1):
            m = (e == v) & ~full; when = np.where(m, t - 1, when); want = np.where(m, v, want)
    when = np.where(full & ((r & 1) == 1) & lone[:, :, None, :], RO, when)
    b = lanes(rng)
    for t in range(RO - 1, -1, -1):
        y = (pick(back[t], np.array(np.broadcast_to(top, (N, 8, 16, 1)))) - 1) & (W - 1)
        for d in DS[::-1]:
            y = pick(np.roll(back[t], -d, axis=0), y)
        y = pick(back[t], y)
        b = np.where(when == t, np.where(full, y, want), b)
        b = (pick(back[t], b) - hist[t][..., t:B * I:B]) & (W - 1)
    b[:, :, 0] = s[:, :, 0]
    w, zs = b, []
    for t in range(RO):
        w = pick(hist[t], (w + hist[t][..., t:B * I:B]) & (W - 1)); v = pick(hist[t], w)
        for d in DS:
            v = pick(np.roll(hist[t], -d, axis=0), v)
        zs.append(pick(hist[t], (v + 1) & (W - 1)))
    c = lanes(rng)
    for t in range(RO - 1, -1, -1):
        u = pick(back[t], c) - zs[t]; c = lanes(rng)
        for k in range(15, 0, -1):
            c[:, :, k] = (u[:, :, k] - c[:, :, (k + 1) & 15]) & (W - 1)
        c = np.where(full & (when == t), top, c)
    return join(p, b, np.where(full, c, rng.integers(0, 4, (N, 8, 16, I))))
def check_inputs(d):
    bad = []
    for k, lo, hi in (("pm", 1, W * W - 2), ("sa", 0, W - 1), ("ta", 0, W - 1)):
        if np.min(d[k]) < lo or np.max(d[k]) > hi: bad.append("range of " + k)
    if np.any(np.sort(halves(d["pm"]), axis=-1) != np.arange(W)): bad.append("permutations in pm")
    return bad
def reference(pm, sa, ta):
    P = halves(pm).reshape(N, 8, 16, W); S = sa.astype(np.int64).reshape(N, 8, 16, I); T = ta.astype(np.int64).reshape(N, 8, 16, I)
    for t in range(RO):
        if t:
            S = np.roll(S, (A, C), axis=(0, 1)); T = np.roll(T, (A, C), axis=(0, 1))
        S = pick(P, (S + P[..., t:B * I:B]) & (W - 1))
        z = pick(P, S)
        for a in DS:
            z = pick(np.roll(P, -a, axis=0), z)
        z = pick(P, (z + 1) & (W - 1))
        T = pick(P, (T + np.roll(T, -1, axis=2) + z) & (W - 1))
        if t < RO - 1: P = swap(P, S, t)
    return {"ys": S.reshape(N, 128, I).astype(np.float32), "yt": T.reshape(N, 128, I).astype(np.float32)}

@@ -1,0 +1,544 @@
+from concourse.mybir import AluOpType, ActivationFunctionType
+A = AluOpType
+F = ActivationFunctionType
+
+NR, RO, I, W, H = 7, 5, 224, 4096, 2048
+NG, NB = 8, 8
+XW = W + 8
+MAGIC = 1.5 * 2.0 ** 35
+BIG = 1.5 * 2.0 ** 19
+CH = [(0, 256), (256, 768), (768, 1280), (1280, 1792), (1792, 2048)]
+U_A, U_S, U_1, U_2, U_3, U_T = range(6)
+L_S, L_1, L_2, L_3 = range(4)
+
+SCRATCH = {
+    "pw": ("sbuf", [128, H], "int32"), "bp": ("sbuf", [128, H], "float32"),
+    "si": ("sbuf", [128, I], "int32"), "ti": ("sbuf", [128, I], "int32"),
+    "U": ("sbuf", [128, 6 * RO * I], "uint16"), "L": ("sbuf", [128, 4 * RO * I], "uint16"),
+    "s16": ("sbuf", [128, RO * I], "float16"), "tin": ("sbuf", [128, RO * I], "float16"),
+    "tout": ("sbuf", [128, RO * I], "float16"), "hn": ("sbuf", [128, RO * I], "bfloat16"),
+    "ia": ("sbuf", [128, RO * I], "int32"), "ib": ("sbuf", [128, RO * I], "int32"),
+    "la": ("sbuf", [128, 64], "int32"), "lb": ("sbuf", [128, 64], "int32"), "lc": ("sbuf", [128, 64], "int32"),
+    "lx": ("sbuf", [128, 64], "uint16"),
+    "ja": ("sbuf", [128, 16], "int32"), "jb": ("sbuf", [128, 16], "int32"), "jc": ("sbuf", [128, 16], "int32"),
+    "jd": ("sbuf", [128, 16], "int32"),
+    "one": ("sbuf", [128, 2048], "bfloat16"), "onef": ("sbuf", [128, 128], "float32"),
+    "D": ("sbuf", [128, 2048], "bfloat16"), "II": ("sbuf", [128, 256], "bfloat16"), "TT": ("sbuf", [128, 256], "bfloat16"),
+    "EW": ("sbuf", [128, 144], "bfloat16"), "IF": ("sbuf", [128, 128], "float32"),
+    "ysf": ("sbuf", [128, I], "float32"), "ytf": ("sbuf", [128, I], "float32"),
+}
+for _t in range(RO):
+    SCRATCH["X%d" % _t] = ("sbuf", [128, XW], "float32")
+for _t in range(NG):
+    SCRATCH["G%d" % _t] = ("sbuf", [128, 16 * I], "float16")
+for _t in range(NB):
+    SCRATCH["ps%d" % _t] = ("psum", [128, 512], "float32")
+
+WHOLE, HALF = [(0, I)], [(0, I // 2), (I // 2, I)]
+PARTS = [WHOLE, HALF, [(0, 84), (84, 168), (168, I)], [(0, 140), (140, I)]]
+PAR = {
+    "first_copy": [(0, 768, "G"), (H, H + 768, "G"), (768, 1280, "G"), (H + 768, H + 1280, "G"), (1280, H, "G"), (H + 1280, W, "G")],
+    "tails": "G", "first_sum": [(0, 112), (128, I), (112, 128)], "s0half": 1,
+    "gx": 0, "gp": 512, "dp": 3584, "pace": 0, "prio": {},
+    "unit": 28, "ph": {}, "si_at": 2,
+    "split": {("s", 0): 1, ("p", 4): 1, ("T", 4): 1},
+    "pe_half": 0,
+    "seed": 0, "noise": 0.0,
+    "model": {"f": 1.25, "c": 1.56, "sc": 3.8, "pe": 0.417, "pef": 0, "lat": 120, "fix": 60, "hop": 2600, "iss": 500,
+              "first": 2500, "dst": 1800, "bw": 300.0, "fifo": 1},
+}
+PAR.update({
+    'prio': {('T', 4): -6300.0, ('1', 1): 36300.0, ('T', 2): 32800.0, ('p', 3): -6300.0, ('s', 2): 46800.0, ('1', 3): -1700.0, ('s', 1): 51800.0, ('3', 4): -39900.0, ('2', 2): 200.0, ('2', 4): -9100.0, ('3', 0): 19900.0, ('3', 2): 1100.0, ('T', 3): 34600.0, ('p', 2): -2800.0, ('2', 1): 1000.0, ('p', 1): -1300.0, ('p', 0): 3900.0, ('2', 0): 18800.0, ('T', 1): 500.0, ('2', 3): -100.0, ('s', 0): 55200.0, ('1', 2): 400.0, ('3', 3): -4400.0, ('p', 4): -1200.0, ('T', 0): -500.0, ('3', 1): -500.0, ('s', 4): -400.0, ('1', 4): -3400.0, ('1', 0): 35100.0, ('s', 3): 3700.0},
+    'split': {('s', 0): 1, ('1', 0): 1, ('p', 4): 2, ('T', 4): 2, ('s', 2): 3, ('3', 3): 1, ('2', 4): 2, ('T', 3): 2, ('a', 1): 1, ('2', 1): 1, ('3', 4): 2, ('p', 1): 1, ('2', 2): 3, ('1', 1): 1, ('2', 0): 3, ('1', 2): 1},
+    'eps': 1, 'gw': 4, 'gx': 1792, 'gp': 448, 'dp': 896, 'pace': 1, 'pe_half': 1, 'ph': {('s', 3): 0},
+    "first_copy": [(0, 768, "G"), (H, H + 768, "G"), (768, 1280, "G"), (H + 768, H + 1280, "G"), (1280, H, "Y"), (H + 1280, W, "Y")],
+    "tails": "Y", "si_at": 1, "first_sum": [(0, 112), (128, 224), (112, 128)]})
+
+
+def build_ops(par):
+    ops, wr, names = [], {}, []
+
+    def add(kind, eng, n, rd, wt, **kw):
+        o = {"ix": len(ops), "kind": kind, "eng": eng, "n": n, "deps": set(), "virt": [], "sem": None}
+        o.update(kw)
+        for (b, lo, hi) in rd:
+            if b[0] == "ps":
+                wt = wt + [(b, 0, 512)]
+                continue
+            for (j, l2, h2) in wr.get(b, []):
+                if l2 < hi and lo < h2:
+                    o["deps"].add(j)
+        for (b, lo, hi) in wt:
+            if b[0] == "ps":
+                lo, hi = 0, 512
+            for (j, l2, h2) in wr.get(b, []):
+                if l2 < hi and lo < h2:
+                    o["deps"].add(j)
+            wr.setdefault(b, []).append((o["ix"], lo, hi))
+        for (b, lo, hi) in rd + wt:
+            if b[0] in ("ps", "G") and b not in o["virt"]:
+                o["virt"].append(b)
+        if kind in ("load", "copyx", "store", "send"):
+            o["sem"] = "d%d" % len(names)
+            names.append(o["sem"])
+        ops.append(o)
+        return o
+
+    def rg(b, lo, hi):
+        return ((b,), lo, hi)
+
+    def X(t, lo, hi):
+        return (("X", t), lo, hi)
+
+    for j, (lo, hi) in enumerate(CH):
+        add("load", "Y", 4 * (hi - lo), [], [rg("pw", lo, hi)], src="pm", dst="pw", lo=lo, hi=hi)
+        if j == par["si_at"]:
+            add("load", "Y", 4 * I, [], [rg("si", 0, I)], src="sa", dst="si", lo=0, hi=I)
+    add("load", "Y", 4 * I, [], [rg("ti", 0, I)], src="ta", dst="ti", lo=0, hi=I)
+    add("ones", "V", 128, [], [rg("onef", 0, 128)], buf="onef")
+    add("ones", "V", 1024, [], [rg("one", 0, 2048)], buf="one")
+    add("iota", "G", 16, [], [rg("ja", 0, 16)], buf="ja", pat=[[0, 16]], cm=16)
+    add("iota", "G", 16, [], [rg("jb", 0, 16)], buf="jb", pat=[[256, 16]], cm=0)
+    add("sel", "G", 128, [rg("onef", 0, 128)], [rg("IF", 0, 128)], which="IF")
+    add("sel", "G", 256, [rg("one", 0, 256)], [rg("II", 0, 256)], which="II")
+    add("sel", "G", 2048, [rg("one", 0, 2048)], [rg("D", 0, 2048)], which="D")
+    add("sel", "G", 144, [rg("one", 0, 144)], [rg("EW", 0, 144)], which="EW")
+    add("sel", "G", 256, [rg("II", 0, 256)], [rg("TT", 0, 256)], which="T1")
+    add("sel", "G", 16, [], [rg("TT", 0, 256)], which="T2")
+    add("sel", "G", 16, [], [rg("TT", 0, 256)], which="T3")
+    add("jand", "V", 16, [rg("ja", 0, 16)], [rg("jc", 0, 16)])
+    add("jadd", "V", 32, [rg("jb", 0, 16), rg("jc", 0, 16)], [rg("jd", 0, 16)])
+    add("cv0", "V", I, [rg("si", 0, I)], [rg("s16", 0, I)], src="si", dst="s16")
+    add("cv0", "V", I, [rg("ti", 0, I)], [rg("tin", 0, I)], src="ti", dst="tin")
+    for j, (lo, hi) in enumerate(CH):
+        add("un1", "V", hi - lo, [rg("pw", lo, hi)], [rg("bp", lo, hi)], lo=lo, hi=hi)
+        add("un2", "S", hi - lo, [rg("bp", lo, hi)], [(("ps", "u", j), 0, 512)], lo=lo, hi=hi)
+        add("un3", "S", hi - lo, [rg("bp", lo, hi)], [X(0, H + lo, H + hi)], lo=lo, hi=hi)
+    for j, (lo, hi) in enumerate(CH):
+        add("un4", "V", hi - lo, [rg("pw", lo, hi), (("ps", "u", j), 0, 512)], [X(0, lo, hi)], lo=lo, hi=hi)
+
+    def uc(k, t):
+        return (k * RO + t) * I
+
+    def send(t, buf, c0, dbuf, d0, lo, hi, dist):
+        add("send", "G", 2 * (hi - lo), [rg(buf, c0 + lo, c0 + hi)], [rg(dbuf, d0 + lo, d0 + hi)],
+            src=buf, s0=c0 + lo, dst=dbuf, d0=d0 + lo, w=hi - lo, dist=dist)
+
+    def stage(name, t, obuf, o0, width):
+        gb = ("G", name, t)
+        parts = PARTS[par["split"].get((name, t), 0)]
+        u = par["unit"]
+        for (lo, hi) in parts:
+            for c in range(lo, hi, u):
+                add("gath", "VS", 16 * u, [X(t, 0, width), rg(obuf, o0 + c, o0 + c + u)], [(gb, c, c + u)],
+                    t=t, obuf=obuf, o0=o0, lo=c, hi=c + u, width=width, stage=(name, t, lo))
+        res = []
+        for (lo, hi) in parts:
+            bank = ("ps", name, t, lo)
+            subs = HALF if (par["ph"].get((name, t), par["pe_half"]) and len(parts) == 1) else [(lo, hi)]
+            for (l2, h2) in subs:
+                rd = [(gb, l2, h2), rg("D", 0, 2048)]
+                extra = name == "p"
+                add("pick", "P", 16 * max(64, h2 - l2), rd, [(bank, 0, 512)], t=t, lo=l2, hi=h2, extra=extra,
+                    nmm=16, g=gb, bank=bank)
+                if extra:
+                    add("tadd", "P", max(64, h2 - l2), [rg("tin", t * I + l2, t * I + h2), rg("TT", 0, 256)], [(bank, 0, 512)],
+                        t=t, lo=l2, hi=h2, nmm=1, bank=bank)
+            res.append((lo, hi, bank))
+        return res
+
+    def conv(bank, lo, hi, k, t, c):
+        add("conv", "V", hi - lo, [(bank, 0, 512)], [rg("U", uc(k, t) + lo, uc(k, t) + hi)], bank=bank, lo=lo, hi=hi, o0=uc(k, t), c=c)
+
+    for t in range(RO):
+        add("wrap", "G", 1, [X(t, 0, 1)], [X(t, W, W + 1)], t=t)
+        if t == 0:
+            for (lo, hi, e) in par["first_copy"]:
+                if e == "Y":
+                    add("copyx", "Y", 4 * (hi - lo), [X(0, lo, hi)], [X(1, lo, hi)], t=0, to=1, lo=lo, hi=hi)
+                else:
+                    add("copyg", "G", hi - lo, [X(0, lo, hi)], [X(1, lo, hi)], t=0, to=1, lo=lo, hi=hi)
+            for to in range(2, RO):
+                if par["tails"] == "Y":
+                    add("copyx", "Y", 4 * (W - 16 * I), [X(0, 16 * I, W)], [X(to, 16 * I, W)], t=0, to=to, lo=16 * I, hi=W)
+                else:
+                    add("copyg", "G", W - 16 * I, [X(0, 16 * I, W)], [X(to, 16 * I, W)], t=0, to=to, lo=16 * I, hi=W)
+        elif t < RO - 1:
+            gx, gp, dp = par["gx"], par["gp"], par["dp"]
+            for lo in range(0, gx, gp):
+                hi = min(gx, lo + gp)
+                add("copyg", "G", hi - lo, [X(t, lo, hi)], [X(t + 1, lo, hi)], t=t, to=t + 1, lo=lo, hi=hi)
+            prev = []
+            for lo in range(gx, 16 * I, dp):
+                hi = min(16 * I, lo + dp)
+                o = add("copyx", "Y", 4 * (hi - lo), [X(t, lo, hi)], [X(t + 1, lo, hi)], t=t, to=t + 1, lo=lo, hi=hi)
+                if par["pace"] and len(prev) >= par["pace"]:
+                    o["deps"].add(prev[-par["pace"]])
+                prev.append(o["ix"])
+        if t:
+            add("cvs", "V", I // 2, [rg("L", uc(L_S, t), uc(L_S, t) + I)], [rg("s16", t * I, t * I + I)], t=t)
+        parts = par["first_sum"] if t == 0 else PARTS[par["split"].get(("a", t), 0)]
+        for (lo, hi) in parts:
+            n = max(64, hi - lo)
+            rd = [rg("s16", t * I + lo, t * I + hi), X(t, 16 * lo, 16 * hi), rg("II", 0, 256), rg("IF", 0, 128)]
+            b1, b2 = ("ps", "a1", t, lo), ("ps", "a2", t, lo)
+            add("sum", "P", 5 * n, rd, [(b1, 0, 512)], t=t, lo=lo, hi=hi, second=0, nmm=2, bank=b1)
+            add("high", "VS", hi - lo, [(b1, 0, 512)], [rg("hn", t * I + lo, t * I + hi)], t=t, lo=lo, hi=hi, bank=b1)
+            add("sum", "P", 6 * n, rd + [rg("hn", t * I + lo, t * I + hi)], [(b2, 0, 512)], t=t, lo=lo, hi=hi, second=1, nmm=3, bank=b2)
+            conv(b2, lo, hi, U_A, t, BIG + 2048.0)
+        res = stage("s", t, "U", uc(U_A, t), W)
+        for (lo, hi, bank) in res:
+            conv(bank, lo, hi, U_S, t, 2048.0)
+            if t == RO - 1:
+                add("out", "VS", hi - lo, [(bank, 0, 512)], [rg("ysf", lo, hi)], bank=bank, lo=lo, hi=hi, dst="ysf", d0=0, c=2048.0)
+                add("store", "Y", 4 * (hi - lo), [rg("ysf", lo, hi)], [], src="ysf", dst="ys", lo=lo, hi=hi)
+        if t < RO - 1:
+            for (lo, hi) in (HALF if t == 0 and par["s0half"] else WHOLE):
+                send(t, "U", uc(U_S, t), "L", uc(L_S, t + 1), lo, hi, 3)
+            bl = ("ps", "l", t)
+            c = 16 * t
+            add("list", "P", 16 * 64, [(("G", "s", t), 0, I), rg("EW", 0, 144)], [(bl, 0, 512)], t=t, nmm=16, g=("G", "s", t), bank=bl)
+            add("l1", "V", 14, [(bl, 0, 512)], [rg("la", c, c + 14)], t=t, bank=bl)
+            add("l2", "V", 14, [rg("la", c, c + 14)], [rg("lb", c, c + 14)], t=t)
+            add("l3", "V", 28, [rg("lb", c, c + 14), rg("jd", 0, 16)], [rg("lc", c, c + 14)], t=t)
+            add("l4", "V", 14, [rg("lc", c, c + 14)], [rg("lx", c, c + 14)], t=t)
+            add("xg", "VS", I, [rg("lx", c, c + 14), X(t, 0, W)], [X(t + 1, 0, 16 * I)], t=t)
+            add("xs", "V", I, [rg("lx", c, c + 14), X(t, 0, W)], [X(t + 1, 0, 16 * I)], t=t)
+        for (name, obuf, o0, k, c, lk, dist) in (("1", "U", uc(U_S, t), U_1, 2048.0, L_1, 1), ("2", "L", uc(L_1, t), U_2, 2048.0, L_2, 2),
+                                                 ("3", "L", uc(L_2, t), U_3, 2049.0, L_3, -3)):
+            for (lo, hi, bank) in stage(name, t, obuf, o0, W):
+                conv(bank, lo, hi, k, t, c)
+                send(t, "U", uc(k, t), "L", uc(lk, t), lo, hi, dist)
+        for (lo, hi, bank) in stage("p", t, "L", uc(L_3, t), W + 1):
+            c = t * I
+            add("m1", "V", hi - lo, [(bank, 0, 512)], [rg("ia", c + lo, c + hi)], bank=bank, t=t, lo=lo, hi=hi)
+            add("m2", "V", hi - lo, [rg("ia", c + lo, c + hi)], [rg("ib", c + lo, c + hi)], t=t, lo=lo, hi=hi)
+            add("m3", "V", hi - lo, [rg("ib", c + lo, c + hi)], [rg("U", uc(U_T, t) + lo, uc(U_T, t) + hi)], t=t, lo=lo, hi=hi)
+        for (lo, hi, bank) in stage("T", t, "U", uc(U_T, t), W):
+            if t < RO - 1:
+                add("out", "VS", hi - lo, [(bank, 0, 512)], [rg("tout", t * I + lo, t * I + hi)], bank=bank, lo=lo, hi=hi, dst="tout", d0=t * I, c=0.0)
+                send(t, "tout", t * I, "tin", (t + 1) * I, lo, hi, 3)
+            else:
+                add("out", "VS", hi - lo, [(bank, 0, 512)], [rg("ytf", lo, hi)], bank=bank, lo=lo, hi=hi, dst="ytf", d0=0, c=2048.0)
+                add("store", "Y", 4 * (hi - lo), [rg("ytf", lo, hi)], [], src="ytf", dst="yt", lo=lo, hi=hi)
+    return ops, names
+
+
+DMAS = ("load", "copyx", "store", "send")
+
+
+def cost(o, e, m):
+    k, n, cy = o["kind"], o["n"], 0.83 * m["f"]
+    if k in DMAS:
+        rows = 8 * (60 + n / (m["bw"] / 16.0))
+        return (m["iss"] if k == "send" else 100), rows
+    if k in ("gath", "xg"):
+        return ((50 if e == "V" else 65) + n * m["c"] * 0.83) * m["f"], None
+    if k == "xs":
+        return (50 + n * m["sc"] * 0.83) * m["f"], None
+    if e == "P":
+        return (n * m["pe"] + m["pef"] * o["nmm"]) * m["f"], None
+    if e == "G":
+        return (170 + 2 * n * 0.83) * m["f"], None
+    return (max(64, n) + m["fix"]) * cy, None
+
+
+def finish(o, start, held, xfer, m, st):
+    if xfer is None:
+        return start + held
+    t0 = start + held + (m["hop"] - 800 if o["kind"] == "send" else m["dst"])
+    if o["kind"] == "send" and not st["sent"]:
+        st["sent"] = 1
+        t0 += m["first"]
+    if m["fifo"]:
+        t0 = max(t0, st["dma"])
+        st["dma"] = t0 + xfer
+    return t0 + xfer
+
+
+def plan(par):
+    ops, names = build_ops(par)
+    m = par["model"]
+    n = len(ops)
+    succ = [[] for _ in ops]
+    for o in ops:
+        for d in o["deps"]:
+            succ[d].append(o["ix"])
+    pr = [0.0] * n
+    rnd = [par["seed"] * 2654435761 % 4294967296 + 1]
+    jit = {}
+    for o in reversed(ops):
+        e = o["eng"][0]
+        held, xfer = cost(o, e, m)
+        d = held + m["lat"] if xfer is None else held + xfer + m["hop"]
+        if o["kind"] == "gath":
+            d *= par.get("gw", 4.0)
+        pr[o["ix"]] = d + max([pr[s] for s in succ[o["ix"]]] + [0.0])
+    key = []
+    for o in ops:
+        p = pr[o["ix"]]
+        if o["kind"] == "gath":
+            s = o["stage"]
+            if s not in jit:
+                rnd[0] = (rnd[0] * 1103515245 + 12345) % 2147483648
+                jit[s] = par["noise"] * (rnd[0] / 2147483648.0 - 0.5)
+            p += jit[s] + par["prio"].get(s[:2], 0.0)
+        elif o["eng"] in ("V", "VS", "S"):
+            p += 1e7
+        if o["kind"] in ("load", "sel", "iota", "ones"):
+            p = 1e8 - 10 * o["ix"]
+        elif o["kind"] == "send":
+            p += 1e7
+        key.append(p)
+    users = {}
+    for o in ops:
+        for b in o["virt"]:
+            users.setdefault(b, []).append(o["ix"])
+    slot, held_by = {}, {"G": [None] * NG, "ps": [None] * NB}
+    fin = [None] * n
+    left = [len(o["deps"]) for o in ops]
+    ready = [o["ix"] for o in ops if not o["deps"]]
+    free = {"V": 0.0, "S": 0.0, "P": 0.0, "G": 0.0, "Y": 0.0}
+    order = {"V": [], "S": [], "P": [], "G": [], "Y": []}
+    st = {"sent": 0, "dma": 0.0}
+
+    def offer(b):
+        best = None
+        for s, old in enumerate(held_by[b[0]]):
+            if old is None:
+                return s, 0.0, []
+            if all(fin[u] is not None for u in users[old]):
+                tt = max(fin[u] for u in users[old])
+                if best is None or tt < best[1]:
+                    best = (s, tt, users[old])
+        return best
+
+    done = 0
+    while done < n:
+        cand = []
+        for ix in ready:
+            o = ops[ix]
+            r = max([fin[d] + m["lat"] for d in o["deps"]] + [0.0])
+            ok = True
+            for b in o["virt"]:
+                if b not in slot:
+                    of = offer(b)
+                    if of is None:
+                        ok = False
+                    else:
+                        r = max(r, of[1] + m["lat"])
+            if ok:
+                for e in o["eng"]:
+                    cand.append((max(r, free[e]), e, ix))
+        t0, e0, _ = min(cand, key=lambda c: (c[0], c[2]))
+        pool = [c for c in cand if c[1] == e0 and c[0] <= t0 + par.get("eps", 1.0)]
+        sgn = 1 if e0 == "V" else -1
+        c = max(pool, key=lambda c: (round(key[c[2]]), -sgn * c[2]))
+        o = ops[c[2]]
+        for b in o["virt"]:
+            if b not in slot:
+                s, tt, us = offer(b)
+                slot[b] = s
+                held_by[b[0]][s] = b
+                for u in users[b]:
+                    ops[u]["deps"] = ops[u]["deps"] | set(us)
+        held, xfer = cost(o, e0, m)
+        o["on"] = e0
+        fin[o["ix"]] = finish(o, c[0], held, xfer, m, st)
+        free[e0] = c[0] + held
+        order[e0].append(o)
+        ready.remove(o["ix"])
+        done += 1
+        for s in succ[o["ix"]]:
+            left[s] -= 1
+            if left[s] == 0:
+                ready.append(s)
+    alias = {}
+    for e in "VS":
+        out = []
+        for o in order[e]:
+            p = out[-1] if out else None
+            if (p is not None and o["kind"] == "gath" and p["kind"] == "gath" and p["stage"] == o["stage"]
+                    and (p["hi"] == o["lo"] or p["lo"] == o["hi"]) and o["deps"] <= p["deps"]):
+                p["lo"], p["hi"] = min(p["lo"], o["lo"]), max(p["hi"], o["hi"])
+                p["n"] += o["n"]
+                alias[o["ix"]] = p["ix"]
+            else:
+                out.append(o)
+        order[e] = out
+    for e in order:
+        for o in order[e]:
+            o["deps"] = set(alias.get(d, d) for d in o["deps"])
+    return {"order": order, "slot": slot, "names": names, "ops": ops}
+
+
+PLAN = plan(PAR)
+SEMAPHORES = ["cV", "cS", "cP", "cG", "gone"] + PLAN["names"]
+
+
+def rank_program(g, core, T, topo):
+    rank = T.rank_of(core)
+    if rank is None:
+        return
+    order, slot, ops = PLAN["order"], PLAN["slot"], PLAN["ops"]
+    Q = {"V": g.vector, "S": g.scalar, "P": g.tensor, "G": g, "Y": g.sync}
+    V, S, P = g.vector, g.scalar, g.tensor
+
+    def peer(d):
+        return T.cores[(rank + d) % NR]
+
+    mark, total = {}, {}
+    for e in order:
+        for o in order[e]:
+            if o["kind"] == "send":
+                mark[o["ix"]] = (o["sem"], len(topo.engines(peer(-o["dist"]), core)))
+            elif o["sem"]:
+                mark[o["ix"]] = (o["sem"], 16)
+            else:
+                total["c" + e] = total.get("c" + e, 0) + 1
+                mark[o["ix"]] = ("c" + e, total["c" + e])
+    gone = [0]
+
+    def bank(o):
+        return T["ps%d" % slot[o["bank"]]]
+
+    def vs(e, out, in_, mul, c):
+        if e == "V":
+            if mul == 1.0:
+                return V.tensor_scalar(out, in_, c, None, A.add)
+            return V.tensor_scalar(out, in_, mul, c, A.mult, A.add)
+        return S.activation(out, in_, F.Identity, bias=c, scale=mul)
+
+    def emit(o, e):
+        k = o["kind"]
+        t, lo, hi = o.get("t"), o.get("lo"), o.get("hi")
+        Xt = T["X%d" % t] if t is not None else None
+        if k in ("load", "store"):
+            return Q[e].dma_start(T[o["dst"]][:, lo:hi], T[o["src"]][:, lo:hi])
+        if k == "copyx":
+            return Q[e].dma_start(T["X%d" % o["to"]][:, lo:hi], Xt[:, lo:hi])
+        if k == "copyg":
+            return g.affine_select(T["X%d" % o["to"]][:, lo:hi], Xt[:, lo:hi], [[0, hi - lo]], A.is_ge, 0.0, 0, 0)
+        if k == "send":
+            dst = peer(o["dist"])
+            rid, pid, _ = topo.addr(dst)
+            g.remote_dma(T[o["dst"]][:, o["d0"]:o["d0"] + o["w"]], T[o["src"]][:, o["s0"]:o["s0"] + o["w"]],
+                         T.sem[o["sem"]], T.sem["gone"], pid, rid, topo.mask(core, dst))
+            gone[0] += len(topo.engines(core, dst))
+            return None
+        if k == "ones":
+            return V.memset(T[o["buf"]][:], 1.0)
+        if k == "iota":
+            return g.iota(T[o["buf"]][:], o["pat"], 0, o["cm"])
+        if k == "sel":
+            w = o["which"]
+            if w == "IF":
+                return g.affine_select(T.IF[:], T.onef[:], [[-1, 128]], A.is_equal, 0.0, 0, 1)
+            if w == "II":
+                return g.affine_select(T.II[:], T.one[:, 0:256], [[0, 2], [-1, 128]], A.is_equal, 0.0, 0, 1)
+            if w == "D":
+                return g.affine_select(T.D[:], T.one[:], [[-128, 16], [-16, 8], [127, 16]], A.is_equal, 0.0, 0, 1)
+            if w == "EW":
+                return g.affine_select(T.EW[:], T.one[:, 0:144], [[-16, 9], [128, 16]], A.is_equal, 0.0, 16, 1)
+            if w == "T1":
+                return g.affine_select(T.TT[:], T.II[:], [[0, 2], [-1, 128]], A.not_equal, 1.0, -1, 1)
+            if w == "T2":
+                return g.affine_select(T.TT[:, 15:256:16], T.TT[:, 15:256:16], [[0, 2], [-16, 8]], A.not_equal, 0.0, -16, 1)
+            return g.affine_select(T.TT[:, 15:256:16], T.TT[:, 15:256:16], [[0, 2], [-16, 8]], A.not_equal, 1.0, 0, 1)
+        if k == "jand":
+            return V.tensor_scalar(T.jc[:], T.ja[:], 255, None, A.bitwise_and)
+        if k == "jadd":
+            return V.tensor_tensor(T.jd[:], T.jb[:], T.jc[:], A.add)
+        if k == "cv0":
+            return V.tensor_scalar(T[o["dst"]][:, 0:I], T[o["src"]][:], -2048.0, None, A.add)
+        if k == "un1":
+            return V.tensor_scalar(T.bp[:, lo:hi], T.pw[:, lo:hi], -(2.0 ** 23 - 2048.5), MAGIC, A.add, A.add)
+        if k == "un2":
+            return S.activation(T["ps%d" % slot[o["virt"][0]]][:, 0:hi - lo], T.bp[:, lo:hi], F.Identity, bias=-(MAGIC - 2047.0 * W))
+        if k == "un3":
+            return S.activation(T.X0[:, H + lo:H + hi], T.bp[:, lo:hi], F.Identity, bias=-(MAGIC / W - 2047.0), scale=1.0 / W)
+        if k == "un4":
+            return V.tensor_tensor(T.X0[:, lo:hi], T.pw[:, lo:hi], T["ps%d" % slot[o["virt"][0]]][:, 0:hi - lo], A.subtract)
+        if k == "wrap":
+            return g.affine_select(Xt[:, W:W + 1], Xt[:, 0:1], [[0, 1]], A.is_ge, 0.0, 0, 0)
+        if k == "cvs":
+            c = (L_S * RO + t) * I
+            return V.tensor_scalar(T.s16[:, t * I:t * I + I], T.L[:, c:c + I], -2048.0, None, A.add)
+        if k == "sum":
+            out = bank(o)[:, lo:hi]
+            sh = 80 if t else 0
+            P.matmul(out, T.II[:, sh:sh + 128], T.s16[:, t * I + lo:t * I + hi], True, False)
+            r = P.matmul(out, T.IF[:], Xt[:, 16 * lo + t:16 * hi:16], False, not o["second"])
+            if o["second"]:
+                r = P.matmul(out, T.II[:, 0:128], T.hn[:, t * I + lo:t * I + hi], False, True)
+            return r
+        if k == "high":
+            return vs(e, T.hn[:, t * I + lo:t * I + hi], bank(o)[:, lo:hi], -1.0, -(BIG + 0.5))
+        if k == "conv":
+            return V.tensor_scalar(T.U[:, o["o0"] + lo:o["o0"] + hi], bank(o)[:, lo:hi], o["c"], None, A.add)
+        if k == "gath":
+            Gb = T["G%d" % slot[o["virt"][0]]]
+            win = Xt[:, 0:o["width"]].indirect(T[o["obuf"]][:, o["o0"] + lo:o["o0"] + hi])
+            return vs(e, Gb[:, 16 * lo:16 * hi], win, 1.0, -2048.0)
+        if k == "pick":
+            Gb = T["G%d" % slot[o["g"]]]
+            out = bank(o)[:, lo:hi]
+            r = None
+            for j in range(16):
+                r = P.matmul(out, T.D[:, 128 * j:128 * j + 128], Gb[:, 16 * lo + j:16 * hi:16], j == 0, j == 15 and not o["extra"])
+            return r
+        if k == "tadd":
+            sh = 80 if t else 0
+            return P.matmul(bank(o)[:, lo:hi], T.TT[:, sh:sh + 128], T.tin[:, t * I + lo:t * I + hi], False, True)
+        if k == "out":
+            return vs(e, T[o["dst"]][:, o["d0"] + lo:o["d0"] + hi], bank(o)[:, lo:hi], 1.0, o["c"])
+        if k == "list":
+            Gb = T["G%d" % slot[o["g"]]]
+            r = None
+            for a in range(16):
+                r = P.matmul(bank(o)[:, 0:14], T.EW[:, 16 - a:144 - a], Gb[:, 16 * a:16 * I:256], a == 0, a == 15)
+            return r
+        c = 16 * t
+        if k == "l1":
+            return V.tensor_scalar(T.la[:, c:c + 14], bank(o)[:, 0:14], 2048.0, None, A.add)
+        if k == "l2":
+            return V.tensor_scalar(T.lb[:, c:c + 14], T.la[:, c:c + 14], 15, None, A.bitwise_and)
+        if k == "l3":
+            return V.tensor_tensor(T.lc[:, c:c + 14], T.lb[:, c:c + 14], T.jd[:, 0:14], A.add)
+        if k == "l4":
+            return V.tensor_copy(T.lx[:, c:c + 14], T.lc[:, c:c + 14])
+        if k == "xg":
+            return vs(e, T["X%d" % (t + 1)][:, t:16 * I:16], Xt[:, 0:16 * I].indirect(T.lx[:, c:c + 14]), 1.0, 0.0)
+        if k == "xs":
+            return V.tensor_copy(T["X%d" % (t + 1)][:, 0:16 * I].indirect(T.lx[:, c:c + 14]), Xt[:, t:16 * I:16])
+        c = t * I
+        if k == "m1":
+            return V.tensor_scalar(T.ia[:, c + lo:c + hi], bank(o)[:, lo:hi], 6144.0, None, A.add)
+        if k == "m2":
+            return V.tensor_scalar(T.ib[:, c + lo:c + hi], T.ia[:, c + lo:c + hi], W - 1, None, A.bitwise_and)
+        u = (U_T * RO + t) * I
+        return V.tensor_copy(T.U[:, u + lo:u + hi], T.ib[:, c + lo:c + hi])
+
+    for e in order:
+        seen = {}
+        for o in order[e]:
+            need = {}
+            for d in o["deps"]:
+                s, c = mark[d]
+                if e == "P" and s == "cP":
+                    continue
+                need[s] = max(need.get(s, 0), c)
+            for s in sorted(need):
+                if seen.get(s, 0) < need[s]:
+                    Q[e].wait_ge(T.sem[s], need[s])
+                    seen[s] = need[s]
+            r = emit(o, e)
+            if r is not None:
+                s, c = mark[o["ix"]]
+                r.then_inc(T.sem[s], 16 if o["sem"] else 1)
+    for o in order["Y"]:
+        if o["kind"] == "store":
+            g.sync.wait_ge(T.sem[o["sem"]], 16)
+    for s in sorted(total):
+        g.wait_ge(T.sem[s], total[s])
+    g.wait_ge(T.sem["gone"], gone[0])

@@ -3,11 +3,12 @@ A = AluOpType
 F = ActivationFunctionType
 
 NR, RO, I, W, H = 7, 5, 224, 4096, 2048
-NG, NB = 8, 8
+NG, NB = 12, 8
 XW = W + 8
+XE = 16 * I
 MAGIC = 1.5 * 2.0 ** 35
 BIG = 1.5 * 2.0 ** 19
-CH = [(0, 256), (256, 768), (768, 1280), (1280, 1792), (1792, 2048)]
+MID = 1.5 * 2.0 ** 14
 U_A, U_S, U_1, U_2, U_3, U_T = range(6)
 L_S, L_1, L_2, L_3 = range(4)
 
@@ -16,13 +17,13 @@ SCRATCH = {
     "si": ("sbuf", [128, I], "int32"), "ti": ("sbuf", [128, I], "int32"),
     "U": ("sbuf", [128, 6 * RO * I], "uint16"), "L": ("sbuf", [128, 4 * RO * I], "uint16"),
     "s16": ("sbuf", [128, RO * I], "float16"), "tin": ("sbuf", [128, RO * I], "float16"),
-    "tout": ("sbuf", [128, RO * I], "float16"), "hn": ("sbuf", [128, RO * I], "bfloat16"),
-    "ia": ("sbuf", [128, RO * I], "int32"), "ib": ("sbuf", [128, RO * I], "int32"),
-    "la": ("sbuf", [128, 64], "int32"), "lb": ("sbuf", [128, 64], "int32"), "lc": ("sbuf", [128, 64], "int32"),
-    "lx": ("sbuf", [128, 64], "uint16"),
+    "tout": ("sbuf", [128, RO * I], "float16"),
+    "hs": ("sbuf", [128, RO * I], "bfloat16"), "hT": ("sbuf", [128, RO * I], "bfloat16"),
+    "hl": ("sbuf", [128, 64], "float16"), "lx": ("sbuf", [128, 64], "uint16"),
+    "cs": ("sbuf", [128, I], "float16"), "cT": ("sbuf", [128, I], "float16"), "cl": ("sbuf", [128, 16], "float16"),
     "ja": ("sbuf", [128, 16], "int32"), "jb": ("sbuf", [128, 16], "int32"), "jc": ("sbuf", [128, 16], "int32"),
-    "jd": ("sbuf", [128, 16], "int32"),
-    "one": ("sbuf", [128, 2048], "bfloat16"), "onef": ("sbuf", [128, 128], "float32"),
+    "jr": ("sbuf", [128, 16], "float32"), "jd": ("sbuf", [128, 16], "float32"), "mk": ("sbuf", [128, 16], "float32"),
+    "one": ("sbuf", [128, 256], "bfloat16"), "onef": ("sbuf", [128, 128], "float32"),
     "D": ("sbuf", [128, 2048], "bfloat16"), "II": ("sbuf", [128, 256], "bfloat16"), "TT": ("sbuf", [128, 256], "bfloat16"),
     "EW": ("sbuf", [128, 144], "bfloat16"), "IF": ("sbuf", [128, 128], "float32"),
     "ysf": ("sbuf", [128, I], "float32"), "ytf": ("sbuf", [128, I], "float32"),
@@ -34,32 +35,35 @@ for _t in range(NG):
 for _t in range(NB):
     SCRATCH["ps%d" % _t] = ("psum", [128, 512], "float32")
 
-WHOLE, HALF = [(0, I)], [(0, I // 2), (I // 2, I)]
-PARTS = [WHOLE, HALF, [(0, 84), (84, 168), (168, I)], [(0, 140), (140, I)]]
 PAR = {
-    "first_copy": [(0, 768, "G"), (H, H + 768, "G"), (768, 1280, "G"), (H + 768, H + 1280, "G"), (1280, H, "G"), (H + 1280, W, "G")],
-    "tails": "G", "first_sum": [(0, 112), (128, I), (112, 128)], "s0half": 1,
-    "gx": 0, "gp": 512, "dp": 3584, "pace": 0, "prio": {},
-    "unit": 28, "ph": {}, "si_at": 2,
-    "split": {("s", 0): 1, ("p", 4): 1, ("T", 4): 1},
-    "pe_half": 0,
-    "seed": 0, "noise": 0.0,
-    "model": {"f": 1.25, "c": 1.56, "sc": 3.8, "pe": 0.417, "pef": 0, "lat": 120, "fix": 60, "hop": 2600, "iss": 500,
-              "first": 2500, "dst": 1800, "bw": 300.0, "fifo": 1},
+    "chunks": [0, 256, 768, 1280, 1792, 2048], "si_at": 1,
+    "first_sum": [(0, 112), (128, 224), (112, 128)],
+    "g0": 2560, "tails": "VVG", "gx": [0, 1792, 1792], "vx": [3584, 0, 0], "gp": 448, "dp": 896, "pace": 1,
+    "cuts": {}, "cut0": (112,), "fine": "T4", "late": 0, "step": 2, "joined": [], "narrow": 0, "load": 1.17, "ahead": 3, "soon": 3, "lean": 300.0,
+    "seq": "s0a s0b 10a 10b s1a s1b 20a 20b 11a 11b s2a s2b 30a 30b 21a 21b s3a s3b 12a 12b p0a p0b s4a s4b 31a 31b T0a T0b "
+           "22a 22b 13a 13b p1a p1b 14a 14b 32a 32b T1a T1b 23a 23b 24a 24b p2a p2b 33a 33b T2a T2b 34a 34b p3a p3b "
+           "T3a T3b p4a p4b T4a T4b",
+    "both": "s0a s0b 10a 10b s1a s1b s2a s2b s3a s3b p4a p4b T4a T4b T3a T3b",
+    "eps": {"V": 200.0, "S": 200.0, "P": 1.0, "G": 1.0, "Y": 1.0},
+    "model": {"f": 1.25, "gc": 1.6, "sc": 3.8, "fix": 25, "lat": 120, "hop": 2800, "iss": 600, "first": 2500, "dst": 1800,
+              "bw": 280.0, "row": 60, "pe": 0.417},
 }
-PAR.update({
-    'prio': {('T', 4): -6300.0, ('1', 1): 36300.0, ('T', 2): 32800.0, ('p', 3): -6300.0, ('s', 2): 46800.0, ('1', 3): -1700.0, ('s', 1): 51800.0, ('3', 4): -39900.0, ('2', 2): 200.0, ('2', 4): -9100.0, ('3', 0): 19900.0, ('3', 2): 1100.0, ('T', 3): 34600.0, ('p', 2): -2800.0, ('2', 1): 1000.0, ('p', 1): -1300.0, ('p', 0): 3900.0, ('2', 0): 18800.0, ('T', 1): 500.0, ('2', 3): -100.0, ('s', 0): 55200.0, ('1', 2): 400.0, ('3', 3): -4400.0, ('p', 4): -1200.0, ('T', 0): -500.0, ('3', 1): -500.0, ('s', 4): -400.0, ('1', 4): -3400.0, ('1', 0): 35100.0, ('s', 3): 3700.0},
-    'split': {('s', 0): 1, ('1', 0): 1, ('p', 4): 2, ('T', 4): 2, ('s', 2): 3, ('3', 3): 1, ('2', 4): 2, ('T', 3): 2, ('a', 1): 1, ('2', 1): 1, ('3', 4): 2, ('p', 1): 1, ('2', 2): 3, ('1', 1): 1, ('2', 0): 3, ('1', 2): 1},
-    'eps': 1, 'gw': 4, 'gx': 1792, 'gp': 448, 'dp': 896, 'pace': 1, 'pe_half': 1, 'ph': {('s', 3): 0},
-    "first_copy": [(0, 768, "G"), (H, H + 768, "G"), (768, 1280, "G"), (H + 768, H + 1280, "G"), (1280, H, "Y"), (H + 1280, W, "Y")],
-    "tails": "Y", "si_at": 1, "first_sum": [(0, 112), (128, 224), (112, 128)]})
+PAR.update({'chunks': [0, 512, 1024, 1408, 1792, 2048], 'si_at': 2, 'first_sum': [(0, 84), (84, 224)], 'g0': 2560, 'tails': 'YVG', 'gx': [1792, 1792, 1792], 'vx': [896, 0, 0], 'gp': 896, 'dp': 896, 'pace': 1, 'cuts': {('s', 0): (84, 154), ('s', 1): (112,), ('s', 2): (112,), ('1', 0): (112,), ('1', 1): (112,), ('2', 0): (112,), ('3', 3): (196,), ('p', 3): (70, 140), ('p', 4): (84, 154), ('T', 3): (112,), ('T', 4): (84, 168)}, 'cut0': (), 'late': 4, 'load': 1.17, 'lean': 300, 'eps': {'V': 200.0, 'S': 200.0, 'P': 300.0, 'G': 400.0, 'Y': 1.0}, 'model': {'f': 1.2, 'gc': 1.5, 'sc': 3.8, 'fix': 20, 'lat': 100, 'hop': 2300, 'iss': 800, 'first': 2500, 'dst': 1600, 'bw': 280.0, 'row': 50, 'pe': 0.417},
+'V': 's0:0-42 s0:154-196 s0:84-112 10:0-84 10:84-112 s1:0-28 s1:28-56 s1:112-168 20:0-112 11:112-140 11:0-28 11:28-56 s2:0-28 s2:28-56 s2:112-168 30:0-112 30:112-140 21:0-112 12:0-84 p0:0-112 s3:0-112 31:0-112 T0:0-84 22:0-112 13:0-112 p1:0-112 s4:0-112 32:0-140 14:0-112 T1:0-112 23:0-112 p2:0-112 24:0-112 33:0-84 33:196-224 T2:0-112 34:0-112 p3:0-28 p3:70-126 p3:140-168 T3:0-56 T3:112-140 T3:140-168 p4:84-140 p4:0-28 p4:154-182 T4:0-42 T4:84-126 T4:168-196',
+'S': 's0:56-84 s0:42-56 s0:196-224 s0:140-154 s0:112-140 10:196-224 10:168-196 10:112-168 s1:56-112 s1:168-224 20:112-224 11:196-224 11:140-196 11:56-112 s2:56-112 s2:168-224 30:140-224 21:140-224 21:112-140 12:84-224 p0:112-224 s3:112-224 31:112-224 T0:84-224 22:112-224 13:112-224 p1:112-224 s4:112-224 32:140-224 14:112-224 T1:112-224 23:112-224 p2:140-224 p2:112-140 24:112-224 33:84-196 T2:112-224 34:112-224 p3:28-70 p3:126-140 p3:168-224 T3:84-112 T3:56-84 T3:168-224 p4:140-154 p4:56-84 p4:28-56 p4:182-224 T4:56-84 T4:42-56 T4:154-168 T4:126-154 T4:196-224'})
+PAR.update({'chunks': [0, 320, 832, 1344, 1792, 2048], 'si_at': 0, 'first_sum': [(0, 84), (84, 112), (128, 224), (112, 128)], 'g0': 2048, 'tails': 'GGY', 'gx': [1792, 1792, 2688], 'vx': [0, 0, 0], 'gp': 896, 'dp': 896, 'pace': 1, 'cuts': {('s', 0): (44, 112), ('s', 1): (112,), ('1', 1): (112,), ('s', 2): (56,), ('p', 3): (50, 120), ('T', 3): (112,), ('p', 4): (84, 168), ('T', 4): (84, 168), ('T', 0): (108,), ('1', 3): (84,), ('2', 2): (122,), ('3', 3): (94,), ('3', 2): (100,), ('T', 1): (92,), ('1', 2): (92,), ('p', 2): (116,), ('s', 4): (116,), ('3', 4): (94,), ('2', 0): (116,), ('1', 0): (140,), ('T', 2): (128,)}, 'late': 0, 'load': 1.25, 'lean': 0, 'eps': {'V': 200.0, 'S': 100.0, 'P': 400.0, 'G': 400.0, 'Y': 1.0}, 'model': {'f': 1.2, 'gc': 1.5, 'sc': 3.8, 'fix': 20, 'lat': 100, 'hop': 2300, 'iss': 800, 'first': 2500, 'dst': 1600, 'bw': 280.0, 'row': 50, 'pe': 0.417}, 'V': 's0:0-44 s0:112-168 10:0-62 10:112-156 s1:0-56 s1:112-168 20:0-116 11:0-36 11:112-148 s2:0-56 s2:112-168 30:0-108 21:0-108 12:0-92 p0:0-98 s3:0-108 31:0-116 T0:0-108 22:0-136 p1:0-108 13:0-108 s4:0-130 32:0-100 14:0-108 T1:0-92 23:0-108 p2:0-116 24:0-116 33:0-94 T2:0-128 34:0-94 p3:0-50 p3:78-120 p3:162-202 T3:0-44 T3:112-174 p4:128-132 p4:0-42 p4:162-202 p4:98-128 T4:0-42 T4:84-126 T4:168-196', 'S': 's0:44-112 s0:168-224 10:62-112 10:156-224 s1:56-112 s1:168-224 20:116-224 11:36-112 11:148-224 s2:56-112 s2:168-224 30:126-224 30:108-126 21:108-224 12:92-224 p0:98-224 s3:108-224 31:116-224 T0:108-224 13:108-224 22:136-224 p1:108-224 s4:130-224 32:100-224 T1:92-224 14:134-224 14:108-134 23:108-224 p2:116-224 24:116-224 33:94-224 T2:128-224 34:94-224 p3:50-78 p3:202-224 p3:120-162 T3:44-112 T3:174-224 p4:42-98 p4:202-224 p4:132-162 T4:42-74 T4:74-84 T4:126-168 T4:196-224'})
+
+
+def pieces(cuts, lo=0, hi=I):
+    c = [lo] + list(cuts) + [hi]
+    return list(zip(c[:-1], c[1:]))
 
 
 def build_ops(par):
     ops, wr, names = [], {}, []
 
     def add(kind, eng, n, rd, wt, **kw):
-        o = {"ix": len(ops), "kind": kind, "eng": eng, "n": n, "deps": set(), "virt": [], "sem": None}
+        o = {"ix": len(ops), "kind": kind, "eng": eng, "n": n, "deps": set(), "virt": [], "sem": None, "tag": None}
         o.update(kw)
         for (b, lo, hi) in rd:
             if b[0] == "ps":
@@ -69,8 +73,6 @@ def build_ops(par):
                 if l2 < hi and lo < h2:
                     o["deps"].add(j)
         for (b, lo, hi) in wt:
-            if b[0] == "ps":
-                lo, hi = 0, 512
             for (j, l2, h2) in wr.get(b, []):
                 if l2 < hi and lo < h2:
                     o["deps"].add(j)
@@ -78,7 +80,7 @@ def build_ops(par):
         for (b, lo, hi) in rd + wt:
             if b[0] in ("ps", "G") and b not in o["virt"]:
                 o["virt"].append(b)
-        if kind in ("load", "copyx", "store", "send"):
+        if kind in DMAS:
             o["sem"] = "d%d" % len(names)
             names.append(o["sem"])
         ops.append(o)
@@ -90,289 +92,368 @@ def build_ops(par):
     def X(t, lo, hi):
         return (("X", t), lo, hi)
 
-    for j, (lo, hi) in enumerate(CH):
+    def ps(*b):
+        return (("ps",) + b, 0, 512)
+
+    ch = pieces(par["chunks"][1:-1], 0, H)
+    for j, (lo, hi) in enumerate(pieces([c for c in par["chunks"][1:-1] if c not in par["joined"]], 0, H)):
         add("load", "Y", 4 * (hi - lo), [], [rg("pw", lo, hi)], src="pm", dst="pw", lo=lo, hi=hi)
         if j == par["si_at"]:
             add("load", "Y", 4 * I, [], [rg("si", 0, I)], src="sa", dst="si", lo=0, hi=I)
     add("load", "Y", 4 * I, [], [rg("ti", 0, I)], src="ta", dst="ti", lo=0, hi=I)
+    add("ones", "V", 128, [], [rg("one", 0, 256)], buf="one")
     add("ones", "V", 128, [], [rg("onef", 0, 128)], buf="onef")
-    add("ones", "V", 1024, [], [rg("one", 0, 2048)], buf="one")
-    add("iota", "G", 16, [], [rg("ja", 0, 16)], buf="ja", pat=[[0, 16]], cm=16)
-    add("iota", "G", 16, [], [rg("jb", 0, 16)], buf="jb", pat=[[256, 16]], cm=0)
-    add("sel", "G", 128, [rg("onef", 0, 128)], [rg("IF", 0, 128)], which="IF")
+    add("iota", "G", 16, [], [rg("ja", 0, 16)], buf="ja", pat=[[-1, 16]], base=16, cm=1)
     add("sel", "G", 256, [rg("one", 0, 256)], [rg("II", 0, 256)], which="II")
-    add("sel", "G", 2048, [rg("one", 0, 2048)], [rg("D", 0, 2048)], which="D")
+    add("sel", "G", 128, [rg("onef", 0, 128)], [rg("IF", 0, 128)], which="IF")
+    add("iota", "G", 16, [], [rg("jb", 0, 16)], buf="jb", pat=[[256, 16]], base=0, cm=0)
     add("sel", "G", 144, [rg("one", 0, 144)], [rg("EW", 0, 144)], which="EW")
     add("sel", "G", 256, [rg("II", 0, 256)], [rg("TT", 0, 256)], which="T1")
     add("sel", "G", 16, [], [rg("TT", 0, 256)], which="T2")
     add("sel", "G", 16, [], [rg("TT", 0, 256)], which="T3")
+    add("const", "V", 112, [rg("one", 0, I)], [rg("cs", 0, I)], buf="cs", w=I, c=(BIG + 2048.0) / 128)
     add("jand", "V", 16, [rg("ja", 0, 16)], [rg("jc", 0, 16)])
-    add("jadd", "V", 32, [rg("jb", 0, 16), rg("jc", 0, 16)], [rg("jd", 0, 16)])
+    add("jeq", "V", 16, [rg("jc", 0, 16)], [rg("mk", 0, 16)])
+    for j in range(16):
+        add("dj", "VS", 64, [rg("II", 0, 128), rg("mk", 0, 16)], [rg("D", 128 * j, 128 * j + 128)], j=j, half=1)
+    add("const", "V", 112, [rg("one", 0, I)], [rg("cT", 0, I)], buf="cT", w=I, c=(BIG + 6144.0) / 128)
+    add("const", "V", 16, [rg("one", 0, 16)], [rg("cl", 0, 16)], buf="cl", w=16, c=(MID + 2048.0) / 128)
+    add("jrow", "V", 16, [rg("jc", 0, 16)], [rg("jr", 0, 16)])
+    add("jadd", "V", 16, [rg("jb", 0, 16), rg("jr", 0, 16)], [rg("jd", 0, 16)])
     add("cv0", "V", I, [rg("si", 0, I)], [rg("s16", 0, I)], src="si", dst="s16")
-    add("cv0", "V", I, [rg("ti", 0, I)], [rg("tin", 0, I)], src="ti", dst="tin")
-    for j, (lo, hi) in enumerate(CH):
+    add("cv0", "V", I, [rg("ti", 0, I)], [rg("tin", 0, I)], src="ti", dst="tin", tag=("p", 0))
+    for j, (lo, hi) in enumerate(ch):
         add("un1", "V", hi - lo, [rg("pw", lo, hi)], [rg("bp", lo, hi)], lo=lo, hi=hi)
-        add("un2", "S", hi - lo, [rg("bp", lo, hi)], [(("ps", "u", j), 0, 512)], lo=lo, hi=hi)
+        add("un2", "S", hi - lo, [rg("bp", lo, hi)], [ps("u", j)], lo=lo, hi=hi)
         add("un3", "S", hi - lo, [rg("bp", lo, hi)], [X(0, H + lo, H + hi)], lo=lo, hi=hi)
-    for j, (lo, hi) in enumerate(CH):
-        add("un4", "V", hi - lo, [rg("pw", lo, hi), (("ps", "u", j), 0, 512)], [X(0, lo, hi)], lo=lo, hi=hi)
+    for j, (lo, hi) in enumerate(ch):
+        add("un4", "V", hi - lo, [rg("pw", lo, hi), ps("u", j)], [X(0, lo, hi)], lo=lo, hi=hi)
+
+    calls = {}
+    for e in "VS":
+        for j, word in enumerate(par[e].split()):
+            lo, hi = word[3:].split("-")
+            calls.setdefault(word[:2], []).append((e, j, int(lo), int(hi)))
 
     def uc(k, t):
         return (k * RO + t) * I
 
-    def send(t, buf, c0, dbuf, d0, lo, hi, dist):
+    def parts_of(name, t):
+        return pieces(par["cuts"].get((name, t), par["cut0"]))
+
+    def send(tag, buf, c0, dbuf, d0, lo, hi, dist):
         add("send", "G", 2 * (hi - lo), [rg(buf, c0 + lo, c0 + hi)], [rg(dbuf, d0 + lo, d0 + hi)],
-            src=buf, s0=c0 + lo, dst=dbuf, d0=d0 + lo, w=hi - lo, dist=dist)
+            src=buf, s0=c0 + lo, dst=dbuf, d0=d0 + lo, w=hi - lo, dist=dist, tag=tag)
+
+    def copy(e, t, to, lo, hi, **kw):
+        return add({"Y": "copyx", "G": "copyg", "VS": "copyv"}[e], e, (4 if e == "Y" else 1) * (hi - lo), [X(t, lo, hi)], [X(to, lo, hi)],
+                   t=t, to=to, lo=lo, hi=hi, **kw)
 
     def stage(name, t, obuf, o0, width):
         gb = ("G", name, t)
-        parts = PARTS[par["split"].get((name, t), 0)]
-        u = par["unit"]
-        for (lo, hi) in parts:
-            for c in range(lo, hi, u):
-                add("gath", "VS", 16 * u, [X(t, 0, width), rg(obuf, o0 + c, o0 + c + u)], [(gb, c, c + u)],
-                    t=t, obuf=obuf, o0=o0, lo=c, hi=c + u, width=width, stage=(name, t, lo))
+        mine = calls["%s%d" % (name, t)]
+        for (e, j, c, d) in mine:
+            add("gath", e, 16 * (d - c), [X(t, 0, width), rg(obuf, o0 + c, o0 + d)], [(gb, c, d)],
+                t=t, obuf=obuf, o0=o0, lo=c, hi=d, width=width, turn=j, tag=(name, t))
         res = []
-        for (lo, hi) in parts:
-            bank = ("ps", name, t, lo)
-            subs = HALF if (par["ph"].get((name, t), par["pe_half"]) and len(parts) == 1) else [(lo, hi)]
-            for (l2, h2) in subs:
-                rd = [(gb, l2, h2), rg("D", 0, 2048)]
+        for (lo, hi) in parts_of(name, t):
+            bank = ps(name, t, lo)
+            seam = sorted((abs(lo + hi - 2 * c), c) for (_, _, c, _) in mine if lo + 56 <= c <= hi - 56)
+            for (l2, h2) in pieces([seam[0][1]] if seam else [], lo, hi):
                 extra = name == "p"
-                add("pick", "P", 16 * max(64, h2 - l2), rd, [(bank, 0, 512)], t=t, lo=l2, hi=h2, extra=extra,
-                    nmm=16, g=gb, bank=bank)
+                n = max(64, h2 - l2)
+                add("pick", "P", (17 if extra else 16) * n, [(gb, l2, h2), rg("D", 0, 2048), rg("cT", 0, I)], [bank], t=t, lo=l2, hi=h2,
+                    extra=extra, g=gb, bank=bank[0], tag=(name, t))
                 if extra:
-                    add("tadd", "P", max(64, h2 - l2), [rg("tin", t * I + l2, t * I + h2), rg("TT", 0, 256)], [(bank, 0, 512)],
-                        t=t, lo=l2, hi=h2, nmm=1, bank=bank)
+                    add("tadd", "P", n, [rg("tin", t * I + l2, t * I + h2), rg("TT", 0, 256)], [bank],
+                        t=t, lo=l2, hi=h2, bank=bank[0], tag=(name, t))
             res.append((lo, hi, bank))
         return res
 
-    def conv(bank, lo, hi, k, t, c):
-        add("conv", "V", hi - lo, [(bank, 0, 512)], [rg("U", uc(k, t) + lo, uc(k, t) + hi)], bank=bank, lo=lo, hi=hi, o0=uc(k, t), c=c)
+    def take(bank, lo, hi, dst, d0, c, tag):
+        add("take", "VS", hi - lo, [bank], [rg(dst, d0 + lo, d0 + hi)], bank=bank[0], lo=lo, hi=hi, dst=dst, d0=d0, c=c, tag=tag)
+
+    def reduce(bank, lo, hi, hb, t, k, tag):
+        take(bank, lo, hi, hb, t * I, -2047.5, tag)
+        add("low", "V", hi - lo, [bank, rg(hb, t * I + lo, t * I + hi)], [rg("U", uc(k, t) + lo, uc(k, t) + hi)],
+            bank=bank[0], lo=lo, hi=hi, hb=hb, h0=t * I, d0=uc(k, t), tag=tag)
 
     for t in range(RO):
-        add("wrap", "G", 1, [X(t, 0, 1)], [X(t, W, W + 1)], t=t)
+        add("wrap", "G", 1, [X(t, 0, 1)], [X(t, W, W + 1)], t=t, tag=("p", t))
         if t == 0:
-            for (lo, hi, e) in par["first_copy"]:
-                if e == "Y":
-                    add("copyx", "Y", 4 * (hi - lo), [X(0, lo, hi)], [X(1, lo, hi)], t=0, to=1, lo=lo, hi=hi)
-                else:
-                    add("copyg", "G", hi - lo, [X(0, lo, hi)], [X(1, lo, hi)], t=0, to=1, lo=lo, hi=hi)
+            left = par["g0"]
+            for (lo, hi) in ch:
+                for b in (H, 0):
+                    e = "G" if left >= hi - lo else "Y"
+                    left -= (hi - lo) if e == "G" else 0
+                    for c in range(lo, hi, par["gp"] if e == "G" else W):
+                        copy(e, 0, 1, b + c, b + min(hi, c + (par["gp"] if e == "G" else W)))
             for to in range(2, RO):
-                if par["tails"] == "Y":
-                    add("copyx", "Y", 4 * (W - 16 * I), [X(0, 16 * I, W)], [X(to, 16 * I, W)], t=0, to=to, lo=16 * I, hi=W)
+                if par["tails"][to - 2] in "YV":
+                    copy("Y" if par["tails"][to - 2] == "Y" else "VS", 0, to, XE, W)
                 else:
-                    add("copyg", "G", W - 16 * I, [X(0, 16 * I, W)], [X(to, 16 * I, W)], t=0, to=to, lo=16 * I, hi=W)
+                    copy("G", 0, to, XE, XE + 256)
+                    copy("G", 0, to, XE + 256, W)
         elif t < RO - 1:
-            gx, gp, dp = par["gx"], par["gp"], par["dp"]
-            for lo in range(0, gx, gp):
-                hi = min(gx, lo + gp)
-                add("copyg", "G", hi - lo, [X(t, lo, hi)], [X(t + 1, lo, hi)], t=t, to=t + 1, lo=lo, hi=hi)
+            gx, gp, dp, vx = par["gx"][t - 1], par["gp"], par["dp"], par["vx"][t - 1]
+            for lo in range(0, vx, 448):
+                copy("VS", t, t + 1, lo, min(vx, lo + 448))
+            gx = min(XE, vx + gx)
+            for lo in range(vx, gx, gp):
+                copy("G", t, t + 1, lo, min(gx, lo + gp))
             prev = []
-            for lo in range(gx, 16 * I, dp):
-                hi = min(16 * I, lo + dp)
-                o = add("copyx", "Y", 4 * (hi - lo), [X(t, lo, hi)], [X(t + 1, lo, hi)], t=t, to=t + 1, lo=lo, hi=hi)
+            for lo in range(gx, XE, dp):
+                o = copy("Y", t, t + 1, lo, min(XE, lo + dp))
                 if par["pace"] and len(prev) >= par["pace"]:
                     o["deps"].add(prev[-par["pace"]])
                 prev.append(o["ix"])
-        if t:
-            add("cvs", "V", I // 2, [rg("L", uc(L_S, t), uc(L_S, t) + I)], [rg("s16", t * I, t * I + I)], t=t)
-        parts = par["first_sum"] if t == 0 else PARTS[par["split"].get(("a", t), 0)]
-        for (lo, hi) in parts:
+        tag = ("s", t)
+        for (lo, hi) in (par["first_sum"] if t == 0 else parts_of("s", t - 1)):
             n = max(64, hi - lo)
-            rd = [rg("s16", t * I + lo, t * I + hi), X(t, 16 * lo, 16 * hi), rg("II", 0, 256), rg("IF", 0, 128)]
-            b1, b2 = ("ps", "a1", t, lo), ("ps", "a2", t, lo)
-            add("sum", "P", 5 * n, rd, [(b1, 0, 512)], t=t, lo=lo, hi=hi, second=0, nmm=2, bank=b1)
-            add("high", "VS", hi - lo, [(b1, 0, 512)], [rg("hn", t * I + lo, t * I + hi)], t=t, lo=lo, hi=hi, bank=b1)
-            add("sum", "P", 6 * n, rd + [rg("hn", t * I + lo, t * I + hi)], [(b2, 0, 512)], t=t, lo=lo, hi=hi, second=1, nmm=3, bank=b2)
-            conv(b2, lo, hi, U_A, t, BIG + 2048.0)
-        res = stage("s", t, "U", uc(U_A, t), W)
-        for (lo, hi, bank) in res:
-            conv(bank, lo, hi, U_S, t, 2048.0)
+            if t:
+                add("cvs", "V", (hi - lo) // 2, [rg("L", uc(L_S, t) + lo, uc(L_S, t) + hi)], [rg("s16", t * I + lo, t * I + hi)],
+                    t=t, lo=lo, hi=hi, tag=tag)
+            bank = ps("a", t, lo)
+            add("sumx", "P", 5 * n, [X(t, 16 * lo, 16 * hi), rg("IF", 0, 128), rg("cs", 0, I)], [bank], t=t, lo=lo, hi=hi, bank=bank[0], tag=tag)
+            add("sums", "P", n, [rg("s16", t * I + lo, t * I + hi), rg("II", 0, 256)], [bank], t=t, lo=lo, hi=hi, bank=bank[0], tag=tag)
+            reduce(bank, lo, hi, "hs", t, U_A, tag)
+        for (lo, hi, bank) in stage("s", t, "U", uc(U_A, t), W):
+            take(bank, lo, hi, "U", uc(U_S, t), 2048.0, tag)
             if t == RO - 1:
-                add("out", "VS", hi - lo, [(bank, 0, 512)], [rg("ysf", lo, hi)], bank=bank, lo=lo, hi=hi, dst="ysf", d0=0, c=2048.0)
+                take(bank, lo, hi, "ysf", 0, 2048.0, ("y", t))
                 add("store", "Y", 4 * (hi - lo), [rg("ysf", lo, hi)], [], src="ysf", dst="ys", lo=lo, hi=hi)
+            else:
+                send(tag, "U", uc(U_S, t), "L", uc(L_S, t + 1), lo, hi, 3)
         if t < RO - 1:
-            for (lo, hi) in (HALF if t == 0 and par["s0half"] else WHOLE):
-                send(t, "U", uc(U_S, t), "L", uc(L_S, t + 1), lo, hi, 3)
-            bl = ("ps", "l", t)
-            c = 16 * t
-            add("list", "P", 16 * 64, [(("G", "s", t), 0, I), rg("EW", 0, 144)], [(bl, 0, 512)], t=t, nmm=16, g=("G", "s", t), bank=bl)
-            add("l1", "V", 14, [(bl, 0, 512)], [rg("la", c, c + 14)], t=t, bank=bl)
-            add("l2", "V", 14, [rg("la", c, c + 14)], [rg("lb", c, c + 14)], t=t)
-            add("l3", "V", 28, [rg("lb", c, c + 14), rg("jd", 0, 16)], [rg("lc", c, c + 14)], t=t)
-            add("l4", "V", 14, [rg("lc", c, c + 14)], [rg("lx", c, c + 14)], t=t)
-            add("xg", "VS", I, [rg("lx", c, c + 14), X(t, 0, W)], [X(t + 1, 0, 16 * I)], t=t)
-            add("xs", "V", I, [rg("lx", c, c + 14), X(t, 0, W)], [X(t + 1, 0, 16 * I)], t=t)
+            bl, c, tag = ps("l", t), 16 * t, ("x", t)
+            add("list", "P", 17 * 64, [(("G", "s", t), 0, I), rg("EW", 0, 144), rg("cl", 0, 16)], [bl], t=t, g=("G", "s", t), bank=bl[0], tag=tag)
+            add("lhi", "V", 14, [bl, rg("jd", 0, 16)], [rg("hl", c, c + 14)], t=t, bank=bl[0], tag=tag)
+            add("llo", "V", 14, [bl, rg("hl", c, c + 14)], [rg("lx", c, c + 14)], t=t, bank=bl[0], tag=tag)
+            add("xg", "VS", I, [rg("lx", c, c + 14), X(t, 0, W)], [X(t + 1, 0, XE)], t=t, tag=tag)
+            add("xs", "V", I, [rg("lx", c, c + 14), X(t, 0, W)], [X(t + 1, 0, XE)], t=t, tag=tag)
         for (name, obuf, o0, k, c, lk, dist) in (("1", "U", uc(U_S, t), U_1, 2048.0, L_1, 1), ("2", "L", uc(L_1, t), U_2, 2048.0, L_2, 2),
                                                  ("3", "L", uc(L_2, t), U_3, 2049.0, L_3, -3)):
             for (lo, hi, bank) in stage(name, t, obuf, o0, W):
-                conv(bank, lo, hi, k, t, c)
-                send(t, "U", uc(k, t), "L", uc(lk, t), lo, hi, dist)
+                take(bank, lo, hi, "U", uc(k, t), c, (name, t))
+                send((name, t), "U", uc(k, t), "L", uc(lk, t), lo, hi, dist)
         for (lo, hi, bank) in stage("p", t, "L", uc(L_3, t), W + 1):
-            c = t * I
-            add("m1", "V", hi - lo, [(bank, 0, 512)], [rg("ia", c + lo, c + hi)], bank=bank, t=t, lo=lo, hi=hi)
-            add("m2", "V", hi - lo, [rg("ia", c + lo, c + hi)], [rg("ib", c + lo, c + hi)], t=t, lo=lo, hi=hi)
-            add("m3", "V", hi - lo, [rg("ib", c + lo, c + hi)], [rg("U", uc(U_T, t) + lo, uc(U_T, t) + hi)], t=t, lo=lo, hi=hi)
+            reduce(bank, lo, hi, "hT", t, U_T, ("p", t))
         for (lo, hi, bank) in stage("T", t, "U", uc(U_T, t), W):
             if t < RO - 1:
-                add("out", "VS", hi - lo, [(bank, 0, 512)], [rg("tout", t * I + lo, t * I + hi)], bank=bank, lo=lo, hi=hi, dst="tout", d0=t * I, c=0.0)
-                send(t, "tout", t * I, "tin", (t + 1) * I, lo, hi, 3)
+                take(bank, lo, hi, "tout", t * I, 0.0, ("T", t))
+                send(("T", t), "tout", t * I, "tin", (t + 1) * I, lo, hi, 3)
             else:
-                add("out", "VS", hi - lo, [(bank, 0, 512)], [rg("ytf", lo, hi)], bank=bank, lo=lo, hi=hi, dst="ytf", d0=0, c=2048.0)
+                take(bank, lo, hi, "ytf", 0, 2048.0, ("T", t))
                 add("store", "Y", 4 * (hi - lo), [rg("ytf", lo, hi)], [], src="ytf", dst="yt", lo=lo, hi=hi)
     return ops, names
 
 
 DMAS = ("load", "copyx", "store", "send")
+SETUP = ("load", "sel", "iota", "ones", "const", "jand", "jeq", "dj", "jrow", "jadd")
 
 
 def cost(o, e, m):
     k, n, cy = o["kind"], o["n"], 0.83 * m["f"]
     if k in DMAS:
-        rows = 8 * (60 + n / (m["bw"] / 16.0))
-        return (m["iss"] if k == "send" else 100), rows
+        return (m["iss"] if k == "send" else 100), 8 * (m["row"] + n / (m["bw"] / 16.0))
     if k in ("gath", "xg"):
-        return ((50 if e == "V" else 65) + n * m["c"] * 0.83) * m["f"], None
+        return (50 if e == "V" else 65) + n * m["gc"] * 0.83, None
     if k == "xs":
-        return (50 + n * m["sc"] * 0.83) * m["f"], None
+        return 50 + n * m["sc"] * 0.83, None
     if e == "P":
-        return (n * m["pe"] + m["pef"] * o["nmm"]) * m["f"], None
+        return n * m["pe"] * m["f"], None
     if e == "G":
         return (170 + 2 * n * 0.83) * m["f"], None
+    if e == "S" and o.get("half"):
+        n *= 2
     return (max(64, n) + m["fix"]) * cy, None
-
-
-def finish(o, start, held, xfer, m, st):
-    if xfer is None:
-        return start + held
-    t0 = start + held + (m["hop"] - 800 if o["kind"] == "send" else m["dst"])
-    if o["kind"] == "send" and not st["sent"]:
-        st["sent"] = 1
-        t0 += m["first"]
-    if m["fifo"]:
-        t0 = max(t0, st["dma"])
-        st["dma"] = t0 + xfer
-    return t0 + xfer
 
 
 def plan(par):
     ops, names = build_ops(par)
     m = par["model"]
-    n = len(ops)
+    n, lat = len(ops), m["lat"]
     succ = [[] for _ in ops]
     for o in ops:
         for d in o["deps"]:
             succ[d].append(o["ix"])
-    pr = [0.0] * n
-    rnd = [par["seed"] * 2654435761 % 4294967296 + 1]
-    jit = {}
+    due, key, end = [0.0] * n, [0.0] * n, {"V": 0.0, "S": 0.0}
+    for o in sorted((o for o in ops if o["kind"] == "gath"), key=lambda o: o["turn"]):
+        due[o["ix"]] = end[o["eng"]]
+        end[o["eng"]] += par["load"] * cost(o, o["eng"], m)[0]
     for o in reversed(ops):
-        e = o["eng"][0]
-        held, xfer = cost(o, e, m)
-        d = held + m["lat"] if xfer is None else held + xfer + m["hop"]
-        if o["kind"] == "gath":
-            d *= par.get("gw", 4.0)
-        pr[o["ix"]] = d + max([pr[s] for s in succ[o["ix"]]] + [0.0])
-    key = []
-    for o in ops:
-        p = pr[o["ix"]]
-        if o["kind"] == "gath":
-            s = o["stage"]
-            if s not in jit:
-                rnd[0] = (rnd[0] * 1103515245 + 12345) % 2147483648
-                jit[s] = par["noise"] * (rnd[0] / 2147483648.0 - 0.5)
-            p += jit[s] + par["prio"].get(s[:2], 0.0)
-        elif o["eng"] in ("V", "VS", "S"):
+        ix = o["ix"]
+        held, xfer = cost(o, o["eng"][0], m)
+        if o["kind"] != "gath":
+            due[ix] = min([due[u] for u in succ[ix]] + [end["V"] + 1000.0]) - held - lat - (0.0 if xfer is None else xfer + m["hop"] - 800)
+        p = 1e7 - due[ix]
+        if o["kind"] in SETUP:
+            p = 1e8 - 10 * ix
+        elif o["kind"] in ("un1", "un2", "un3", "un4"):
+            p = 2e8 - ix - (par["late"] if o["kind"] == "un3" else 0)
+        elif o["kind"] in ("send", "tadd"):
             p += 1e7
-        if o["kind"] in ("load", "sel", "iota", "ones"):
-            p = 1e8 - 10 * o["ix"]
-        elif o["kind"] == "send":
-            p += 1e7
-        key.append(p)
+        elif o["kind"] == "gath":
+            p = 0.0
+        elif o["kind"] == "copyv" or (o["kind"] == "cv0" and o["tag"]):
+            p -= 2e7
+        key[ix] = p
+    turn = {"V": 0, "S": 0}
     users = {}
     for o in ops:
         for b in o["virt"]:
             users.setdefault(b, []).append(o["ix"])
     slot, held_by = {}, {"G": [None] * NG, "ps": [None] * NB}
+    open_users = {b: len(u) for b, u in users.items()}
+    done_at = {b: 0.0 for b in users}
     fin = [None] * n
     left = [len(o["deps"]) for o in ops]
-    ready = [o["ix"] for o in ops if not o["deps"]]
-    free = {"V": 0.0, "S": 0.0, "P": 0.0, "G": 0.0, "Y": 0.0}
-    order = {"V": [], "S": [], "P": [], "G": [], "Y": []}
-    st = {"sent": 0, "dma": 0.0}
+    ready = {o["ix"]: 0.0 for o in ops if not o["deps"]}
+    free = {e: 0.0 for e in "VSPGY"}
+    order = {e: [] for e in "VSPGY"}
+    sent, dma = 0, 0.0
 
-    def offer(b):
+    def offer(kind):
         best = None
-        for s, old in enumerate(held_by[b[0]]):
+        for s, old in enumerate(held_by[kind]):
             if old is None:
-                return s, 0.0, []
-            if all(fin[u] is not None for u in users[old]):
-                tt = max(fin[u] for u in users[old])
-                if best is None or tt < best[1]:
-                    best = (s, tt, users[old])
+                return s, 0.0, None
+            if not open_users[old] and (best is None or done_at[old] + lat < best[1]):
+                best = (s, done_at[old] + lat, old)
         return best
 
-    done = 0
-    while done < n:
-        cand = []
-        for ix in ready:
+    for nth in range(n):
+        offers = {"G": offer("G"), "ps": offer("ps")}
+        cand, first = {e: [] for e in free}, None
+        for ix, r in ready.items():
             o = ops[ix]
-            r = max([fin[d] + m["lat"] for d in o["deps"]] + [0.0])
-            ok = True
+            eng = o["eng"]
+            if o["kind"] == "gath" and o["turn"] != turn[eng]:
+                continue
             for b in o["virt"]:
                 if b not in slot:
-                    of = offer(b)
+                    of = offers[b[0]]
                     if of is None:
-                        ok = False
-                    else:
-                        r = max(r, of[1] + m["lat"])
-            if ok:
-                for e in o["eng"]:
-                    cand.append((max(r, free[e]), e, ix))
-        t0, e0, _ = min(cand, key=lambda c: (c[0], c[2]))
-        pool = [c for c in cand if c[1] == e0 and c[0] <= t0 + par.get("eps", 1.0)]
-        sgn = 1 if e0 == "V" else -1
-        c = max(pool, key=lambda c: (round(key[c[2]]), -sgn * c[2]))
-        o = ops[c[2]]
+                        r = None
+                        break
+                    r = max(r, of[1])
+            if r is None:
+                continue
+            if o["kind"] == "take" and max(r, free["S"]) <= max(r, free["V"]) + par["lean"]:
+                eng = "S"
+            for e in eng:
+                s = max(r, free[e])
+                cand[e].append((s, ix))
+                if first is None or s < first[0]:
+                    first = (s, e)
+        t0, e = first
+        _, ix, s = max((key[ix], -ix, s) for (s, ix) in cand[e] if s <= t0 + par["eps"][e])
+        o = ops[-ix]
+        if o["kind"] == "gath":
+            turn[e] += 1
         for b in o["virt"]:
             if b not in slot:
-                s, tt, us = offer(b)
-                slot[b] = s
-                held_by[b[0]][s] = b
-                for u in users[b]:
-                    ops[u]["deps"] = ops[u]["deps"] | set(us)
-        held, xfer = cost(o, e0, m)
-        o["on"] = e0
-        fin[o["ix"]] = finish(o, c[0], held, xfer, m, st)
-        free[e0] = c[0] + held
-        order[e0].append(o)
-        ready.remove(o["ix"])
-        done += 1
-        for s in succ[o["ix"]]:
-            left[s] -= 1
-            if left[s] == 0:
-                ready.append(s)
-    alias = {}
-    for e in "VS":
-        out = []
-        for o in order[e]:
-            p = out[-1] if out else None
-            if (p is not None and o["kind"] == "gath" and p["kind"] == "gath" and p["stage"] == o["stage"]
-                    and (p["hi"] == o["lo"] or p["lo"] == o["hi"]) and o["deps"] <= p["deps"]):
-                p["lo"], p["hi"] = min(p["lo"], o["lo"]), max(p["hi"], o["hi"])
-                p["n"] += o["n"]
-                alias[o["ix"]] = p["ix"]
-            else:
-                out.append(o)
-        order[e] = out
-    for e in order:
-        for o in order[e]:
-            o["deps"] = set(alias.get(d, d) for d in o["deps"])
+                sl, _, old = offers[b[0]]
+                slot[b] = sl
+                held_by[b[0]][sl] = b
+                if old is not None:
+                    for u in users[b]:
+                        ops[u]["deps"] = ops[u]["deps"] | set(users[old])
+        held, xfer = cost(o, e, m)
+        if xfer is None:
+            f = s + held
+        else:
+            f = s + held + (m["hop"] - 800 if o["kind"] == "send" else m["dst"])
+            if o["kind"] == "send":
+                o["every"] = par["step"] if sent < par["narrow"] else 1
+                xfer *= o["every"]
+                if not sent:
+                    f += m["first"]
+                    held += m["first"] / 2
+                sent += 1
+            f = dma = max(f, dma) + xfer
+        ix = o["ix"]
+        fin[ix] = f
+        o["nth"], o["at"] = nth, s
+        free[e] = s + held
+        order[e].append(o)
+        del ready[ix]
+        for b in o["virt"]:
+            open_users[b] -= 1
+            done_at[b] = max(done_at[b], f)
+        for u in succ[ix]:
+            left[u] -= 1
+            if left[u] == 0:
+                ready[u] = max(fin[d] for d in ops[u]["deps"] if fin[d] is not None) + lat
     return {"order": order, "slot": slot, "names": names, "ops": ops}
 
 
-PLAN = plan(PAR)
+def arrange(par):
+    words = {e: par["Q"][e].split() for e in "VSPGY"}
+    ops, names = build_ops(dict(par, V=" ".join(sorted(w for e in "VS" for w in words[e] if ":" in w)), S=""))
+    by, count, users = {}, {}, {}
+    for o in ops:
+        k, tag = o["kind"], "%s%d" % o["tag"] if o["tag"] else ""
+        if k == "take" and o["dst"] in ("hs", "hT"):
+            k = "high"
+        if k[:4] == "copy":
+            k, tag = "copy", str(o["to"])
+        j = count[k, tag] = count.get((k, tag), -1) + 1
+        by["%s:%d-%d" % (tag, o["lo"], o["hi"]) if k == "gath" else k + "." + tag + "abcdefghijklmnop"[j]] = o
+        for b in o["virt"]:
+            users.setdefault(b, []).append(o["ix"])
+    order = {e: [by[w] for w in words[e]] for e in words}
+    assert sorted(o["ix"] for e in order for o in order[e]) == list(range(len(ops)))
+    m = par["model"]
+    fin, pos, free = {}, {e: 0 for e in order}, {e: 0.0 for e in order}
+    slot, held = {}, {"G": [None] * NG, "ps": [None] * NB}
+    left, done = {b: len(u) for b, u in users.items()}, {}
+    sent, dma = 0, 0.0
+    for nth in range(len(ops)):
+        best = None
+        for e in order:
+            o = order[e][pos[e]] if pos[e] < len(order[e]) else None
+            if o is None or any(d not in fin for d in o["deps"]):
+                continue
+            r, offer = max([free[e]] + [fin[d] for d in o["deps"]]), None
+            new = [b for b in o["virt"] if b not in slot]
+            if new:
+                idle = [(0.0 if old is None else done[old], old is not None, s, old) for s, old in enumerate(held[new[0][0]])
+                        if old is None or not left[old]]
+                if not idle:
+                    continue
+                offer = min(idle, key=lambda x: (x[1], x[0], x[2]))
+                r = max(r, offer[0])
+            if best is None or r < best[0]:
+                best = (r, e, o, new, offer)
+        r, e, o, new, offer = best
+        if new:
+            slot[new[0]], held[new[0][0]][offer[2]], done[new[0]] = offer[2], new[0], offer[0]
+            for u in users[new[0]]:
+                ops[u]["deps"] = ops[u]["deps"] | set(users.get(offer[3], []))
+        hold, xfer = cost(o, e, m)
+        f = r + hold
+        if xfer is not None:
+            f += m["hop"] - 800 if o["kind"] == "send" else m["dst"]
+            if o["kind"] == "send":
+                o["every"] = 1
+                if not sent:
+                    f += m["first"]
+                    hold += m["first"] / 2
+                sent = 1
+            f = dma = max(f, dma) + xfer
+        fin[o["ix"]] = f + m["lat"]
+        o["nth"] = nth
+        free[e] = r + hold
+        pos[e] += 1
+        for b in o["virt"]:
+            left[b] -= 1
+            done[b] = max(done[b], f + m["lat"])
+    return {"order": order, "slot": slot, "names": names, "ops": ops}
+
+
+FIN = {'chunks': [0, 448, 896, 1408, 1792, 2048], 'joined': [448], 'si_at': 0, 'first_sum': [(0, 56), (56, 112), (128, 224), (112, 128)], 'g0': 2048, 'tails': 'GGY', 'gx': [1792, 1792, 2240], 'vx': [448, 0, 0], 'gp': 896, 'dp': 896, 'pace': 1, 'narrow': 0, 'cuts': {('s', 0): (54, 112), ('s', 1): (112,), ('1', 1): (112,), ('p', 3): (52, 118), ('T', 3): (112,), ('p', 4): (84, 166), ('T', 4): (84, 166), ('1', 3): (104,), ('T', 1): (90,), ('1', 2): (102,), ('p', 2): (120,), ('s', 4): (132,), ('2', 0): (118,), ('T', 2): (142,)}, 'Q': {'V': 'jand.a ones.a const.c jeq.a jrow.a ones.b dj.m dj.n dj.f const.a dj.b const.b dj.g dj.p un1.a dj.k un1.b cv0.a un4.a un1.c un4.b dj.l un1.d un4.c un1.e un4.d jadd.a un4.e low.s0a cv0.p0a low.s0b s0:0-42 low.s0d low.s0c s0:112-168 take.s0b 10:0-12 10:12-60 lhi.x0a take.s0c llo.x0a 10:112-158 xg.x0a xs.x0a cvs.s1b cvs.s1a high.s1b cvs.s1c low.s1b high.s1a high.s1c low.s1a low.s1c s1:0-54 s1:112-176 take.s1a 20:0-118 lhi.x1a 11:0-26 llo.x1a take.20b xg.x1a take.20a xs.x1a cvs.s2a cvs.s2b 11:112-146 low.s2a low.s2b s2:0-52 s2:106-166 30:0-108 lhi.x2a 21:0-104 llo.x2a take.30a 12:0-102 xg.x2a cvs.s3a xs.x2a p0:0-90 high.s3a p0:90-94 low.s3a take.12b s3:0-110 high.p0a s3:110-114 low.p0a 31:0-108 lhi.x3a T0:0-98 llo.x3a 22:0-132 xs.x3a cvs.s4a take.T0a p1:0-114 low.s4a 13:0-104 s4:0-132 take.13a low.p1a 32:0-90 take.13b 14:0-114 T1:0-90 23:0-102 take.14a p2:0-120 take.23a take.y4a 24:0-110 high.p2a high.p2b low.p2a low.p2b 33:0-92 take.24a T2:0-142 34:0-88 take.T2a p3:0-52 take.T2b p3:82-118 p3:158-210 low.p3a low.p3b T3:0-44 high.p3c T3:112-118 low.p3c T3:118-174 p4:0-44 take.T3b p4:166-196 p4:98-142 low.p4a T4:0-42 low.p4b low.p4c T4:84-126 take.T4a T4:166-194 take.T4b', 'S': 'dj.o dj.d dj.h dj.j dj.c dj.i dj.e dj.a un3.a un2.a un2.b un3.b un2.c un3.c un2.d un3.d un2.e high.s0a un3.e high.s0b s0:42-56 high.s0c high.s0d s0:56-112 take.s0a s0:168-224 10:60-112 10:158-224 take.10a copy.2c s1:54-112 s1:176-224 20:118-224 take.s1b 11:26-112 11:146-224 high.s2a high.s2b take.11a s2:52-106 take.11b s2:166-224 30:108-224 take.s2a 21:104-224 12:102-224 take.21a take.12a p0:94-224 s3:114-224 31:108-224 take.s3a T0:98-224 take.31a xg.x3a 22:132-224 13:104-224 take.22a high.s4a p1:114-224 s4:132-224 high.p1a 32:90-224 take.s4a T1:90-224 take.s4b take.32a 14:114-224 take.T1b 23:102-224 take.T1a p2:120-224 24:110-224 33:92-224 T2:142-192 take.33a T2:192-224 34:88-224 p3:210-224 p3:52-82 take.y4b take.34a p3:118-158 high.p3a high.p3b T3:44-112 T3:174-224 take.T3a p4:44-98 p4:196-224 p4:142-166 high.p4a T4:42-72 high.p4b high.p4c T4:72-84 T4:126-166 T4:194-224 take.T4c', 'P': 'sumx.s0a sums.s0a sumx.s0b sums.s0b sumx.s0c sumx.s0d sums.s0c sums.s0d pick.s0a pick.s0b pick.s0c list.x0a pick.s0d pick.10a pick.10b sumx.s1b sumx.s1a sums.s1b sumx.s1c sums.s1a sums.s1c pick.s1a list.x1a pick.s1b pick.20b pick.20a pick.11a sumx.s2a sumx.s2b sums.s2a sums.s2b pick.11b pick.s2a list.x2a pick.s2b pick.30a pick.30b pick.21a pick.21b pick.12a sumx.s3a sums.s3a pick.12b pick.p0a tadd.p0a pick.p0b tadd.p0b pick.s3a pick.s3b list.x3a pick.31a pick.31b pick.T0a pick.T0b pick.22a sumx.s4a pick.22b sums.s4a pick.13b pick.p1a tadd.p1a pick.p1b tadd.p1b pick.13a pick.s4a pick.s4b pick.32a pick.32b pick.14a pick.T1b pick.14b pick.T1a pick.23a pick.23b pick.p2a pick.p2b tadd.p2b tadd.p2a pick.24a pick.24b pick.33a pick.33b pick.T2a pick.T2b pick.34a pick.34b pick.p3a pick.p3b tadd.p3a tadd.p3b pick.p3c tadd.p3c pick.T3a pick.T3b pick.p4a pick.p4c tadd.p4a pick.p4b tadd.p4b tadd.p4c pick.T4a pick.T4b pick.T4c', 'G': 'iota.a sel.a sel.b sel.c sel.d iota.b sel.e copy.1a wrap.p0a sel.f copy.1b copy.1c copy.1d copy.2b copy.1i send.s0a send.s0b send.s0c copy.3a send.10a copy.2d copy.2e copy.2a send.s1a send.s1b send.20b send.20a copy.3c send.11a send.11b copy.3d send.s2a wrap.p1a send.30a copy.3b send.21a copy.4d copy.4c send.12a send.12b send.s3a copy.4b send.31a wrap.p2a send.T0a send.22a send.13b send.13a send.32a send.T1b send.14a send.T1a send.23a send.24a send.33a wrap.p3a wrap.p4a send.T2a send.T2b send.34a send.T3a send.T3b', 'Y': 'load.a load.b load.c load.d load.e load.f copy.1f copy.1j copy.1h copy.1e copy.1g copy.2f copy.2g copy.3e copy.3f copy.4e copy.4f copy.4a store.a store.b store.c store.d store.e'}}
+PLAN = arrange(dict(PAR, **FIN))
 SEMAPHORES = ["cV", "cS", "cP", "cG", "gone"] + PLAN["names"]
 
 
@@ -380,7 +461,7 @@ def rank_program(g, core, T, topo):
     rank = T.rank_of(core)
     if rank is None:
         return
-    order, slot, ops = PLAN["order"], PLAN["slot"], PLAN["ops"]
+    order, slot = PLAN["order"], PLAN["slot"]
     Q = {"V": g.vector, "S": g.scalar, "P": g.tensor, "G": g, "Y": g.sync}
     V, S, P = g.vector, g.scalar, g.tensor
 
@@ -391,7 +472,7 @@ def rank_program(g, core, T, topo):
     for e in order:
         for o in order[e]:
             if o["kind"] == "send":
-                mark[o["ix"]] = (o["sem"], len(topo.engines(peer(-o["dist"]), core)))
+                mark[o["ix"]] = (o["sem"], len(topo.engines(peer(-o["dist"]), core)[::o["every"]]))
             elif o["sem"]:
                 mark[o["ix"]] = (o["sem"], 16)
             else:
@@ -399,45 +480,44 @@ def rank_program(g, core, T, topo):
                 mark[o["ix"]] = ("c" + e, total["c" + e])
     gone = [0]
 
-    def bank(o):
-        return T["ps%d" % slot[o["bank"]]]
-
-    def vs(e, out, in_, mul, c):
+    def plus(e, out, in_, c):
         if e == "V":
-            if mul == 1.0:
-                return V.tensor_scalar(out, in_, c, None, A.add)
-            return V.tensor_scalar(out, in_, mul, c, A.mult, A.add)
-        return S.activation(out, in_, F.Identity, bias=c, scale=mul)
+            return V.tensor_scalar(out, in_, c, None, A.add)
+        return S.activation(out, in_, F.Identity, bias=c)
 
     def emit(o, e):
         k = o["kind"]
         t, lo, hi = o.get("t"), o.get("lo"), o.get("hi")
         Xt = T["X%d" % t] if t is not None else None
+        bank = T["ps%d" % slot[o["bank"]]] if "bank" in o else None
         if k in ("load", "store"):
             return Q[e].dma_start(T[o["dst"]][:, lo:hi], T[o["src"]][:, lo:hi])
         if k == "copyx":
             return Q[e].dma_start(T["X%d" % o["to"]][:, lo:hi], Xt[:, lo:hi])
         if k == "copyg":
             return g.affine_select(T["X%d" % o["to"]][:, lo:hi], Xt[:, lo:hi], [[0, hi - lo]], A.is_ge, 0.0, 0, 0)
+        if k == "copyv":
+            return plus(e, T["X%d" % o["to"]][:, lo:hi], Xt[:, lo:hi], 0.0)
         if k == "send":
             dst = peer(o["dist"])
             rid, pid, _ = topo.addr(dst)
+            use = topo.engines(core, dst)[::o["every"]]
             g.remote_dma(T[o["dst"]][:, o["d0"]:o["d0"] + o["w"]], T[o["src"]][:, o["s0"]:o["s0"] + o["w"]],
-                         T.sem[o["sem"]], T.sem["gone"], pid, rid, topo.mask(core, dst))
-            gone[0] += len(topo.engines(core, dst))
+                         T.sem[o["sem"]], T.sem["gone"], pid, rid, sum(1 << x for x in use))
+            gone[0] += len(use)
             return None
         if k == "ones":
             return V.memset(T[o["buf"]][:], 1.0)
+        if k == "const":
+            return V.tensor_scalar(T[o["buf"]][:], T.one[:, 0:o["w"]], o["c"], None, A.mult)
         if k == "iota":
-            return g.iota(T[o["buf"]][:], o["pat"], 0, o["cm"])
+            return g.iota(T[o["buf"]][:], o["pat"], o["base"], o["cm"])
         if k == "sel":
             w = o["which"]
             if w == "IF":
                 return g.affine_select(T.IF[:], T.onef[:], [[-1, 128]], A.is_equal, 0.0, 0, 1)
             if w == "II":
-                return g.affine_select(T.II[:], T.one[:, 0:256], [[0, 2], [-1, 128]], A.is_equal, 0.0, 0, 1)
-            if w == "D":
-                return g.affine_select(T.D[:], T.one[:], [[-128, 16], [-16, 8], [127, 16]], A.is_equal, 0.0, 0, 1)
+                return g.affine_select(T.II[:], T.one[:], [[0, 2], [-1, 128]], A.is_equal, 0.0, 0, 1)
             if w == "EW":
                 return g.affine_select(T.EW[:], T.one[:, 0:144], [[-16, 9], [128, 16]], A.is_equal, 0.0, 16, 1)
             if w == "T1":
@@ -446,9 +526,18 @@ def rank_program(g, core, T, topo):
                 return g.affine_select(T.TT[:, 15:256:16], T.TT[:, 15:256:16], [[0, 2], [-16, 8]], A.not_equal, 0.0, -16, 1)
             return g.affine_select(T.TT[:, 15:256:16], T.TT[:, 15:256:16], [[0, 2], [-16, 8]], A.not_equal, 1.0, 0, 1)
         if k == "jand":
-            return V.tensor_scalar(T.jc[:], T.ja[:], 255, None, A.bitwise_and)
+            return V.tensor_scalar(T.jc[:], T.ja[:], 15, None, A.bitwise_and)
+        if k == "jeq":
+            return V.tensor_scalar(T.mk[:], T.jc[:], 0.0, None, A.is_equal)
+        if k == "dj":
+            j = o["j"]
+            if e == "V":
+                return V.tensor_scalar(T.D[:, 128 * j:128 * j + 128], T.II[:, 0:128], T.mk[:, j:j + 1], None, A.mult)
+            return S.activation(T.D[:, 128 * j:128 * j + 128], T.II[:, 0:128], F.Identity, scale=T.mk[:, j:j + 1])
+        if k == "jrow":
+            return V.tensor_scalar(T.jr[:], T.jc[:], 16.0, 7.5, A.mult, A.add)
         if k == "jadd":
-            return V.tensor_tensor(T.jd[:], T.jb[:], T.jc[:], A.add)
+            return V.tensor_scalar(T.jd[:], T.jb[:], T.jr[:, 0:1], None, A.add)
         if k == "cv0":
             return V.tensor_scalar(T[o["dst"]][:, 0:I], T[o["src"]][:], -2048.0, None, A.add)
         if k == "un1":
@@ -463,61 +552,44 @@ def rank_program(g, core, T, topo):
             return g.affine_select(Xt[:, W:W + 1], Xt[:, 0:1], [[0, 1]], A.is_ge, 0.0, 0, 0)
         if k == "cvs":
             c = (L_S * RO + t) * I
-            return V.tensor_scalar(T.s16[:, t * I:t * I + I], T.L[:, c:c + I], -2048.0, None, A.add)
-        if k == "sum":
-            out = bank(o)[:, lo:hi]
-            sh = 80 if t else 0
-            P.matmul(out, T.II[:, sh:sh + 128], T.s16[:, t * I + lo:t * I + hi], True, False)
-            r = P.matmul(out, T.IF[:], Xt[:, 16 * lo + t:16 * hi:16], False, not o["second"])
-            if o["second"]:
-                r = P.matmul(out, T.II[:, 0:128], T.hn[:, t * I + lo:t * I + hi], False, True)
-            return r
-        if k == "high":
-            return vs(e, T.hn[:, t * I + lo:t * I + hi], bank(o)[:, lo:hi], -1.0, -(BIG + 0.5))
-        if k == "conv":
-            return V.tensor_scalar(T.U[:, o["o0"] + lo:o["o0"] + hi], bank(o)[:, lo:hi], o["c"], None, A.add)
+            return V.tensor_scalar(T.s16[:, t * I + lo:t * I + hi], T.L[:, c + lo:c + hi], -2048.0, None, A.add)
+        sh = 80 if t else 0
+        if k == "sumx":
+            P.matmul(bank[:, lo:hi], T.one[:, 0:128], T.cs[:, lo:hi], True, False)
+            return P.matmul(bank[:, lo:hi], T.IF[:], Xt[:, 16 * lo + t:16 * hi:16], False, False)
+        if k == "sums":
+            return P.matmul(bank[:, lo:hi], T.II[:, sh:sh + 128], T.s16[:, t * I + lo:t * I + hi], False, True)
+        if k == "take":
+            return plus(e, T[o["dst"]][:, o["d0"] + lo:o["d0"] + hi], bank[:, lo:hi], o["c"])
+        if k == "low":
+            return V.tensor_tensor(T.U[:, o["d0"] + lo:o["d0"] + hi], bank[:, lo:hi], T[o["hb"]][:, o["h0"] + lo:o["h0"] + hi], A.subtract)
         if k == "gath":
-            Gb = T["G%d" % slot[o["virt"][0]]]
             win = Xt[:, 0:o["width"]].indirect(T[o["obuf"]][:, o["o0"] + lo:o["o0"] + hi])
-            return vs(e, Gb[:, 16 * lo:16 * hi], win, 1.0, -2048.0)
+            return plus(e, T["G%d" % slot[o["virt"][0]]][:, 16 * lo:16 * hi], win, -2048.0)
         if k == "pick":
             Gb = T["G%d" % slot[o["g"]]]
-            out = bank(o)[:, lo:hi]
-            r = None
+            if o["extra"]:
+                P.matmul(bank[:, lo:hi], T.one[:, 0:128], T.cT[:, lo:hi], True, False)
             for j in range(16):
-                r = P.matmul(out, T.D[:, 128 * j:128 * j + 128], Gb[:, 16 * lo + j:16 * hi:16], j == 0, j == 15 and not o["extra"])
+                r = P.matmul(bank[:, lo:hi], T.D[:, 128 * j:128 * j + 128], Gb[:, 16 * lo + j:16 * hi:16],
+                             j == 0 and not o["extra"], j == 15 and not o["extra"])
             return r
         if k == "tadd":
-            sh = 80 if t else 0
-            return P.matmul(bank(o)[:, lo:hi], T.TT[:, sh:sh + 128], T.tin[:, t * I + lo:t * I + hi], False, True)
-        if k == "out":
-            return vs(e, T[o["dst"]][:, o["d0"] + lo:o["d0"] + hi], bank(o)[:, lo:hi], 1.0, o["c"])
+            return P.matmul(bank[:, lo:hi], T.TT[:, sh:sh + 128], T.tin[:, t * I + lo:t * I + hi], False, True)
+        c = 16 * t
         if k == "list":
             Gb = T["G%d" % slot[o["g"]]]
-            r = None
+            P.matmul(bank[:, 0:14], T.one[:, 0:128], T.cl[:, 0:14], True, False)
             for a in range(16):
-                r = P.matmul(bank(o)[:, 0:14], T.EW[:, 16 - a:144 - a], Gb[:, 16 * a:16 * I:256], a == 0, a == 15)
+                r = P.matmul(bank[:, 0:14], T.EW[:, 16 - a:144 - a], Gb[:, 16 * a:XE:256], False, a == 15)
             return r
-        c = 16 * t
-        if k == "l1":
-            return V.tensor_scalar(T.la[:, c:c + 14], bank(o)[:, 0:14], 2048.0, None, A.add)
-        if k == "l2":
-            return V.tensor_scalar(T.lb[:, c:c + 14], T.la[:, c:c + 14], 15, None, A.bitwise_and)
-        if k == "l3":
-            return V.tensor_tensor(T.lc[:, c:c + 14], T.lb[:, c:c + 14], T.jd[:, 0:14], A.add)
-        if k == "l4":
-            return V.tensor_copy(T.lx[:, c:c + 14], T.lc[:, c:c + 14])
+        if k == "lhi":
+            return V.tensor_tensor(T.hl[:, c:c + 14], bank[:, 0:14], T.jd[:, 0:14], A.subtract)
+        if k == "llo":
+            return V.tensor_tensor(T.lx[:, c:c + 14], bank[:, 0:14], T.hl[:, c:c + 14], A.subtract)
         if k == "xg":
-            return vs(e, T["X%d" % (t + 1)][:, t:16 * I:16], Xt[:, 0:16 * I].indirect(T.lx[:, c:c + 14]), 1.0, 0.0)
-        if k == "xs":
-            return V.tensor_copy(T["X%d" % (t + 1)][:, 0:16 * I].indirect(T.lx[:, c:c + 14]), Xt[:, t:16 * I:16])
-        c = t * I
-        if k == "m1":
-            return V.tensor_scalar(T.ia[:, c + lo:c + hi], bank(o)[:, lo:hi], 6144.0, None, A.add)
-        if k == "m2":
-            return V.tensor_scalar(T.ib[:, c + lo:c + hi], T.ia[:, c + lo:c + hi], W - 1, None, A.bitwise_and)
-        u = (U_T * RO + t) * I
-        return V.tensor_copy(T.U[:, u + lo:u + hi], T.ib[:, c + lo:c + hi])
+            return plus(e, T["X%d" % (t + 1)][:, t:XE:16], Xt[:, 0:XE].indirect(T.lx[:, c:c + 14]), 0.0)
+        return V.tensor_copy(T["X%d" % (t + 1)][:, 0:XE].indirect(T.lx[:, c:c + 14]), Xt[:, t:XE:16])
 
     for e in order:
         seen = {}

@@ -1,3 +1,4 @@
+from concourse.bass import DstId, RemoteDMATransfer
 from concourse.mybir import AluOpType, ActivationFunctionType
 A = AluOpType
 F = ActivationFunctionType
@@ -9,49 +10,37 @@ XE = 16 * I
 MAGIC = 1.5 * 2.0 ** 35
 BIG = 1.5 * 2.0 ** 19
 MID = 1.5 * 2.0 ** 14
+TB, TW = 96, 136
 U_A, U_S, U_1, U_2, U_3, U_T = range(6)
 L_S, L_1, L_2, L_3 = range(4)
 
 SCRATCH = {
-    "pw": ("sbuf", [128, H], "int32"), "bp": ("sbuf", [128, H], "float32"),
+    "pw": ("sbuf", [128, H], "int32"),
     "si": ("sbuf", [128, I], "int32"), "ti": ("sbuf", [128, I], "int32"),
     "U": ("sbuf", [128, 6 * RO * I], "uint16"), "L": ("sbuf", [128, 4 * RO * I], "uint16"),
-    "s16": ("sbuf", [128, RO * I], "float16"), "tin": ("sbuf", [128, RO * I], "float16"),
-    "tout": ("sbuf", [128, RO * I], "float16"),
-    "hs": ("sbuf", [128, RO * I], "bfloat16"), "hT": ("sbuf", [128, RO * I], "bfloat16"),
+    "s16": ("sbuf", [128, RO * I], "float16"), "col": ("sbuf", [128, RO * I], "float16"), "t16": ("sbuf", [128, I], "float16"),
+    "tout": ("sbuf", [128, 8 * TW], "float16"), "tin": ("sbuf", [128, 8 * TW], "float16"), "tnx": ("sbuf", [128, 8 * TW], "float16"),
+    "hT": ("sbuf", [128, RO * I], "bfloat16"),
     "hl": ("sbuf", [128, 64], "float16"), "lx": ("sbuf", [128, 64], "uint16"),
-    "cs": ("sbuf", [128, I], "float16"), "cT": ("sbuf", [128, I], "float16"), "cl": ("sbuf", [128, 16], "float16"),
+    "cN": ("sbuf", [128, I], "float16"), "cM": ("sbuf", [128, 2 * I], "bfloat16"), "NH": ("sbuf", [128, 256], "bfloat16"),
+    "cT": ("sbuf", [128, I], "float16"), "cl": ("sbuf", [128, 16], "float16"),
     "ja": ("sbuf", [128, 16], "int32"), "jb": ("sbuf", [128, 16], "int32"), "jc": ("sbuf", [128, 16], "int32"),
     "jr": ("sbuf", [128, 16], "float32"), "jd": ("sbuf", [128, 16], "float32"), "mk": ("sbuf", [128, 16], "float32"),
-    "one": ("sbuf", [128, 256], "bfloat16"), "onef": ("sbuf", [128, 128], "float32"),
+    "one": ("sbuf", [128, 256], "bfloat16"),
     "D": ("sbuf", [128, 2048], "bfloat16"), "II": ("sbuf", [128, 256], "bfloat16"), "TT": ("sbuf", [128, 256], "bfloat16"),
-    "EW": ("sbuf", [128, 144], "bfloat16"), "IF": ("sbuf", [128, 128], "float32"),
+    "EW": ("sbuf", [128, 144], "bfloat16"),
+    "own": ("sbuf", [128, 256], "float16"), "run": ("sbuf", [128, 256], "float16"),
+    "gm": ("sbuf", [128, 256], "float16"), "gs": ("sbuf", [128, 256], "float16"),
     "ysf": ("sbuf", [128, I], "float32"), "ytf": ("sbuf", [128, I], "float32"),
 }
 for _t in range(RO):
-    SCRATCH["X%d" % _t] = ("sbuf", [128, XW], "float32")
+    SCRATCH["X%d" % _t] = ("sbuf", [128, XW], "int32")
 for _t in range(NG):
     SCRATCH["G%d" % _t] = ("sbuf", [128, 16 * I], "float16")
 for _t in range(NB):
     SCRATCH["ps%d" % _t] = ("psum", [128, 512], "float32")
 
-PAR = {
-    "chunks": [0, 256, 768, 1280, 1792, 2048], "si_at": 1,
-    "first_sum": [(0, 112), (128, 224), (112, 128)],
-    "g0": 2560, "tails": "VVG", "gx": [0, 1792, 1792], "vx": [3584, 0, 0], "gp": 448, "dp": 896, "pace": 1,
-    "cuts": {}, "cut0": (112,), "fine": "T4", "late": 0, "step": 2, "joined": [], "narrow": 0, "load": 1.17, "ahead": 3, "soon": 3, "lean": 300.0,
-    "seq": "s0a s0b 10a 10b s1a s1b 20a 20b 11a 11b s2a s2b 30a 30b 21a 21b s3a s3b 12a 12b p0a p0b s4a s4b 31a 31b T0a T0b "
-           "22a 22b 13a 13b p1a p1b 14a 14b 32a 32b T1a T1b 23a 23b 24a 24b p2a p2b 33a 33b T2a T2b 34a 34b p3a p3b "
-           "T3a T3b p4a p4b T4a T4b",
-    "both": "s0a s0b 10a 10b s1a s1b s2a s2b s3a s3b p4a p4b T4a T4b T3a T3b",
-    "eps": {"V": 200.0, "S": 200.0, "P": 1.0, "G": 1.0, "Y": 1.0},
-    "model": {"f": 1.25, "gc": 1.6, "sc": 3.8, "fix": 25, "lat": 120, "hop": 2800, "iss": 600, "first": 2500, "dst": 1800,
-              "bw": 280.0, "row": 60, "pe": 0.417},
-}
-PAR.update({'chunks': [0, 512, 1024, 1408, 1792, 2048], 'si_at': 2, 'first_sum': [(0, 84), (84, 224)], 'g0': 2560, 'tails': 'YVG', 'gx': [1792, 1792, 1792], 'vx': [896, 0, 0], 'gp': 896, 'dp': 896, 'pace': 1, 'cuts': {('s', 0): (84, 154), ('s', 1): (112,), ('s', 2): (112,), ('1', 0): (112,), ('1', 1): (112,), ('2', 0): (112,), ('3', 3): (196,), ('p', 3): (70, 140), ('p', 4): (84, 154), ('T', 3): (112,), ('T', 4): (84, 168)}, 'cut0': (), 'late': 4, 'load': 1.17, 'lean': 300, 'eps': {'V': 200.0, 'S': 200.0, 'P': 300.0, 'G': 400.0, 'Y': 1.0}, 'model': {'f': 1.2, 'gc': 1.5, 'sc': 3.8, 'fix': 20, 'lat': 100, 'hop': 2300, 'iss': 800, 'first': 2500, 'dst': 1600, 'bw': 280.0, 'row': 50, 'pe': 0.417},
-'V': 's0:0-42 s0:154-196 s0:84-112 10:0-84 10:84-112 s1:0-28 s1:28-56 s1:112-168 20:0-112 11:112-140 11:0-28 11:28-56 s2:0-28 s2:28-56 s2:112-168 30:0-112 30:112-140 21:0-112 12:0-84 p0:0-112 s3:0-112 31:0-112 T0:0-84 22:0-112 13:0-112 p1:0-112 s4:0-112 32:0-140 14:0-112 T1:0-112 23:0-112 p2:0-112 24:0-112 33:0-84 33:196-224 T2:0-112 34:0-112 p3:0-28 p3:70-126 p3:140-168 T3:0-56 T3:112-140 T3:140-168 p4:84-140 p4:0-28 p4:154-182 T4:0-42 T4:84-126 T4:168-196',
-'S': 's0:56-84 s0:42-56 s0:196-224 s0:140-154 s0:112-140 10:196-224 10:168-196 10:112-168 s1:56-112 s1:168-224 20:112-224 11:196-224 11:140-196 11:56-112 s2:56-112 s2:168-224 30:140-224 21:140-224 21:112-140 12:84-224 p0:112-224 s3:112-224 31:112-224 T0:84-224 22:112-224 13:112-224 p1:112-224 s4:112-224 32:140-224 14:112-224 T1:112-224 23:112-224 p2:140-224 p2:112-140 24:112-224 33:84-196 T2:112-224 34:112-224 p3:28-70 p3:126-140 p3:168-224 T3:84-112 T3:56-84 T3:168-224 p4:140-154 p4:56-84 p4:28-56 p4:182-224 T4:56-84 T4:42-56 T4:154-168 T4:126-154 T4:196-224'})
-PAR.update({'chunks': [0, 320, 832, 1344, 1792, 2048], 'si_at': 0, 'first_sum': [(0, 84), (84, 112), (128, 224), (112, 128)], 'g0': 2048, 'tails': 'GGY', 'gx': [1792, 1792, 2688], 'vx': [0, 0, 0], 'gp': 896, 'dp': 896, 'pace': 1, 'cuts': {('s', 0): (44, 112), ('s', 1): (112,), ('1', 1): (112,), ('s', 2): (56,), ('p', 3): (50, 120), ('T', 3): (112,), ('p', 4): (84, 168), ('T', 4): (84, 168), ('T', 0): (108,), ('1', 3): (84,), ('2', 2): (122,), ('3', 3): (94,), ('3', 2): (100,), ('T', 1): (92,), ('1', 2): (92,), ('p', 2): (116,), ('s', 4): (116,), ('3', 4): (94,), ('2', 0): (116,), ('1', 0): (140,), ('T', 2): (128,)}, 'late': 0, 'load': 1.25, 'lean': 0, 'eps': {'V': 200.0, 'S': 100.0, 'P': 400.0, 'G': 400.0, 'Y': 1.0}, 'model': {'f': 1.2, 'gc': 1.5, 'sc': 3.8, 'fix': 20, 'lat': 100, 'hop': 2300, 'iss': 800, 'first': 2500, 'dst': 1600, 'bw': 280.0, 'row': 50, 'pe': 0.417}, 'V': 's0:0-44 s0:112-168 10:0-62 10:112-156 s1:0-56 s1:112-168 20:0-116 11:0-36 11:112-148 s2:0-56 s2:112-168 30:0-108 21:0-108 12:0-92 p0:0-98 s3:0-108 31:0-116 T0:0-108 22:0-136 p1:0-108 13:0-108 s4:0-130 32:0-100 14:0-108 T1:0-92 23:0-108 p2:0-116 24:0-116 33:0-94 T2:0-128 34:0-94 p3:0-50 p3:78-120 p3:162-202 T3:0-44 T3:112-174 p4:128-132 p4:0-42 p4:162-202 p4:98-128 T4:0-42 T4:84-126 T4:168-196', 'S': 's0:44-112 s0:168-224 10:62-112 10:156-224 s1:56-112 s1:168-224 20:116-224 11:36-112 11:148-224 s2:56-112 s2:168-224 30:126-224 30:108-126 21:108-224 12:92-224 p0:98-224 s3:108-224 31:116-224 T0:108-224 13:108-224 22:136-224 p1:108-224 s4:130-224 32:100-224 T1:92-224 14:134-224 14:108-134 23:108-224 p2:116-224 24:116-224 33:94-224 T2:128-224 34:94-224 p3:50-78 p3:202-224 p3:120-162 T3:44-112 T3:174-224 p4:42-98 p4:202-224 p4:132-162 T4:42-74 T4:74-84 T4:126-168 T4:196-224'})
+DMAS = ("load", "copyx", "store", "send")
 
 
 def pieces(cuts, lo=0, hi=I):
@@ -63,8 +52,10 @@ def build_ops(par):
     ops, wr, names = [], {}, []
 
     def add(kind, eng, n, rd, wt, **kw):
-        o = {"ix": len(ops), "kind": kind, "eng": eng, "n": n, "deps": set(), "virt": [], "sem": None, "tag": None}
+        o = {"ix": len(ops), "kind": kind, "eng": eng, "n": n, "deps": set(), "virt": [], "sem": None, "tag": None, "mm": 0}
         o.update(kw)
+        if kind != "col":
+            rd = rd + [(("xg", b[1]), 0, 1) for (b, lo, hi) in rd if b[0] == "X" and lo < XE]
         for (b, lo, hi) in rd:
             if b[0] == "ps":
                 wt = wt + [(b, 0, 512)]
@@ -95,88 +86,104 @@ def build_ops(par):
     def ps(*b):
         return (("ps",) + b, 0, 512)
 
-    ch = pieces(par["chunks"][1:-1], 0, H)
-    for j, (lo, hi) in enumerate(pieces([c for c in par["chunks"][1:-1] if c not in par["joined"]], 0, H)):
+    ch, sc, last = pieces(par["chunks"][1:-1], 0, H), par["si_cut"], par["last"]
+    for j, (lo, hi) in enumerate(ch):
         add("load", "Y", 4 * (hi - lo), [], [rg("pw", lo, hi)], src="pm", dst="pw", lo=lo, hi=hi)
-        if j == par["si_at"]:
-            add("load", "Y", 4 * I, [], [rg("si", 0, I)], src="sa", dst="si", lo=0, hi=I)
-    add("load", "Y", 4 * I, [], [rg("ti", 0, I)], src="ta", dst="ti", lo=0, hi=I)
-    add("ones", "V", 128, [], [rg("one", 0, 256)], buf="one")
-    add("ones", "V", 128, [], [rg("onef", 0, 128)], buf="onef")
+    for (lo, hi) in pieces([sc]):
+        add("load", "Y", 4 * (hi - lo), [], [rg("si", lo, hi)], src="sa", dst="si", lo=lo, hi=hi, tag=("s", 0))
+    add("load", "Y", 4 * I, [], [rg("ti", 0, I)], src="ta", dst="ti", lo=0, hi=I, tag=("T", 0))
+    add("ones", "V", 128, [], [rg("one", 0, 256)])
     add("iota", "G", 16, [], [rg("ja", 0, 16)], buf="ja", pat=[[-1, 16]], base=16, cm=1)
     add("sel", "G", 256, [rg("one", 0, 256)], [rg("II", 0, 256)], which="II")
-    add("sel", "G", 128, [rg("onef", 0, 128)], [rg("IF", 0, 128)], which="IF")
     add("iota", "G", 16, [], [rg("jb", 0, 16)], buf="jb", pat=[[256, 16]], base=0, cm=0)
     add("sel", "G", 144, [rg("one", 0, 144)], [rg("EW", 0, 144)], which="EW")
     add("sel", "G", 256, [rg("II", 0, 256)], [rg("TT", 0, 256)], which="T1")
     add("sel", "G", 16, [], [rg("TT", 0, 256)], which="T2")
     add("sel", "G", 16, [], [rg("TT", 0, 256)], which="T3")
-    add("const", "V", 112, [rg("one", 0, I)], [rg("cs", 0, I)], buf="cs", w=I, c=(BIG + 2048.0) / 128)
+    add("pads", "V", 68, [rg("one", 0, 256)], [rg("tout", 0, 8 * TW)])
     add("jand", "V", 16, [rg("ja", 0, 16)], [rg("jc", 0, 16)])
     add("jeq", "V", 16, [rg("jc", 0, 16)], [rg("mk", 0, 16)])
     for j in range(16):
         add("dj", "VS", 64, [rg("II", 0, 128), rg("mk", 0, 16)], [rg("D", 128 * j, 128 * j + 128)], j=j, half=1)
-    add("const", "V", 112, [rg("one", 0, I)], [rg("cT", 0, I)], buf="cT", w=I, c=(BIG + 6144.0) / 128)
-    add("const", "V", 16, [rg("one", 0, 16)], [rg("cl", 0, 16)], buf="cl", w=16, c=(MID + 2048.0) / 128)
+    add("const", "V", 112, [], [rg("cT", 0, I)], buf="cT", lo=0, hi=I, c=(BIG + 6144.0) / 128)
+    add("const", "V", 16, [], [rg("cl", 0, 16)], buf="cl", lo=0, hi=16, c=(MID + 2048.0) / 128)
+    add("const", "V", 112, [], [rg("cN", 0, I)], buf="cN", lo=0, hi=I, c=-2048.0 / 128)
+    add("big", "V", 112, [], [rg("cM", 0, I)], lo=0, c=MAGIC / 128)
+    add("big", "V", 112, [], [rg("cM", I, 2 * I)], lo=I, c=-MAGIC / 128)
+    add("half", "V", 128, [rg("II", 0, 256)], [rg("NH", 0, 256)])
     add("jrow", "V", 16, [rg("jc", 0, 16)], [rg("jr", 0, 16)])
     add("jadd", "V", 16, [rg("jb", 0, 16), rg("jr", 0, 16)], [rg("jd", 0, 16)])
-    add("cv0", "V", I, [rg("si", 0, I)], [rg("s16", 0, I)], src="si", dst="s16")
-    add("cv0", "V", I, [rg("ti", 0, I)], [rg("tin", 0, I)], src="ti", dst="tin", tag=("p", 0))
-    for j, (lo, hi) in enumerate(ch):
-        add("un1", "V", hi - lo, [rg("pw", lo, hi)], [rg("bp", lo, hi)], lo=lo, hi=hi)
-        add("un2", "S", hi - lo, [rg("bp", lo, hi)], [ps("u", j)], lo=lo, hi=hi)
-        add("un3", "S", hi - lo, [rg("bp", lo, hi)], [X(0, H + lo, H + hi)], lo=lo, hi=hi)
-    for j, (lo, hi) in enumerate(ch):
-        add("un4", "V", hi - lo, [rg("pw", lo, hi), ps("u", j)], [X(0, lo, hi)], lo=lo, hi=hi)
+    for o in ops:
+        if o["kind"] == "const":
+            o["deps"].add(len(ch) + 3)
+    if last < I:
+        add("sel", "G", 256, [rg("one", 0, 256)], [rg("run", 0, 256)], which="run")
+        add("own", "V", 16, [rg("mk", 0, 16)], [rg("own", 0, 16)], w=0)
+        for w in (16, 32, 64, 128):
+            add("own", "V", w // 2, [rg("own", 0, w)], [rg("own", w, 2 * w)], w=w)
+    for (lo, hi) in pieces([sc]):
+        add("cv0", "VS", hi - lo, [rg("si", lo, hi)], [rg("s16", lo, hi)], src="si", dst="s16", lo=lo, hi=hi)
+    add("cv0", "VS", I, [rg("ti", 0, I)], [rg("t16", 0, I)], src="ti", dst="t16", lo=0, hi=I, tag=("p", 0))
+    for (lo, hi) in ch:
+        add("ua", "V", hi - lo, [rg("pw", lo, hi)], [X(0, lo, hi)], lo=lo, hi=hi)
+        add("ub", "S", hi - lo, [rg("pw", lo, hi)], [X(0, H + lo, H + hi)], lo=lo, hi=hi)
+        mid = (lo + hi) // 2
+        add("uc", "V", mid - lo, [], [X(0, lo, mid)], lo=lo, hi=mid)
+        add("uc", "S", hi - mid, [], [X(0, mid, hi)], lo=mid, hi=hi)
 
     calls = {}
-    for e in "VS":
-        for j, word in enumerate(par[e].split()):
-            lo, hi = word[3:].split("-")
-            calls.setdefault(word[:2], []).append((e, j, int(lo), int(hi)))
+    for word in par["V"].split():
+        lo, hi = word[3:].split("-")
+        calls.setdefault(word[:2], []).append((int(lo), int(hi)))
 
     def uc(k, t):
         return (k * RO + t) * I
 
-    def parts_of(name, t):
-        return pieces(par["cuts"].get((name, t), par["cut0"]))
+    def parts_of(name, t, end=I):
+        return pieces(par["cuts"].get("%s%d" % (name, t), ()), 0, end)
 
     def send(tag, buf, c0, dbuf, d0, lo, hi, dist):
         add("send", "G", 2 * (hi - lo), [rg(buf, c0 + lo, c0 + hi)], [rg(dbuf, d0 + lo, d0 + hi)],
             src=buf, s0=c0 + lo, dst=dbuf, d0=d0 + lo, w=hi - lo, dist=dist, tag=tag)
 
-    def copy(e, t, to, lo, hi, **kw):
-        return add({"Y": "copyx", "G": "copyg", "VS": "copyv"}[e], e, (4 if e == "Y" else 1) * (hi - lo), [X(t, lo, hi)], [X(to, lo, hi)],
-                   t=t, to=to, lo=lo, hi=hi, **kw)
+    def copy(e, t, to, lo, hi, tag=None):
+        return add("copyx" if e == "Y" else "copyg", e, (4 if e == "Y" else 1) * (hi - lo), [X(t, lo, hi)], [X(to, lo, hi)],
+                   t=t, to=to, lo=lo, hi=hi, tag=tag)
 
-    def stage(name, t, obuf, o0, width):
+    def gathers(name, t, obuf, o0, width):
         gb = ("G", name, t)
-        mine = calls["%s%d" % (name, t)]
-        for (e, j, c, d) in mine:
-            add("gath", e, 16 * (d - c), [X(t, 0, width), rg(obuf, o0 + c, o0 + d)], [(gb, c, d)],
-                t=t, obuf=obuf, o0=o0, lo=c, hi=d, width=width, turn=j, tag=(name, t))
+        for (c, d) in calls["%s%d" % (name, t)]:
+            add("gath", "VS", 16 * (d - c), [X(t, 0, width), rg(obuf, o0 + c, o0 + d)], [(gb, c, d)],
+                t=t, obuf=obuf, o0=o0, lo=c, hi=d, width=width, tag=(name, t))
+        return gb
+
+    def stage(name, t, obuf, o0, width, end=I):
+        gb = gathers(name, t, obuf, o0, width)
         res = []
-        for (lo, hi) in parts_of(name, t):
+        for (lo, hi) in parts_of(name, t, end):
             bank = ps(name, t, lo)
-            seam = sorted((abs(lo + hi - 2 * c), c) for (_, _, c, _) in mine if lo + 56 <= c <= hi - 56)
-            for (l2, h2) in pieces([seam[0][1]] if seam else [], lo, hi):
+            seam = sorted((abs(lo + hi - 2 * c), c) for (c, _) in calls["%s%d" % (name, t)] if lo + 64 <= c <= hi - 64)
+            for (l2, h2) in pieces([seam[0][1]] if seam and "%s%d" % (name, t) not in par["noseam"] else [], lo, hi):
                 extra = name == "p"
                 n = max(64, h2 - l2)
                 add("pick", "P", (17 if extra else 16) * n, [(gb, l2, h2), rg("D", 0, 2048), rg("cT", 0, I)], [bank], t=t, lo=l2, hi=h2,
-                    extra=extra, g=gb, bank=bank[0], tag=(name, t))
-                if extra:
-                    add("tadd", "P", n, [rg("tin", t * I + l2, t * I + h2), rg("TT", 0, 256)], [bank],
-                        t=t, lo=l2, hi=h2, bank=bank[0], tag=(name, t))
+                    extra=extra, g=gb, bank=bank[0], tag=(name, t), mm=17 if extra else 16)
+                if extra and str(t - 1) not in par["turned"]:
+                    src, c = ("tin", (2 * t - 2) * TW) if t else ("t16", 0)
+                    add("tadd", "P", n, [rg(src, c + l2, c + h2), rg("TT", 0, 256)], [bank], t=t, lo=l2, hi=h2, src=src, c=c, sub=None,
+                        bank=bank[0], tag=(name, t), mm=1)
+                elif extra:
+                    bs = TW if len(parts_of("T", t - 1)) > 1 else 128
+                    sub = [(l2, h2, 0)] if h2 <= 128 else [(l2, h2, 1)] if l2 >= TB else [(l2, 112, 0), (112, h2, 1)]
+                    sub = [(a, b, j, (2 * t - 2) * TW + j * bs) for (a, b, j) in sub]
+                    add("tadd", "P", sum(2 * max(64, b - a) for (a, b, _, _) in sub),
+                        [rg("tnx", c, c + 128) for (_, _, _, c) in sub] + [rg("II", 0, 256)], [bank],
+                        t=t, lo=l2, hi=h2, sub=sub, bank=bank[0], tag=(name, t), mm=2 * len(sub))
             res.append((lo, hi, bank))
         return res
 
-    def take(bank, lo, hi, dst, d0, c, tag):
-        add("take", "VS", hi - lo, [bank], [rg(dst, d0 + lo, d0 + hi)], bank=bank[0], lo=lo, hi=hi, dst=dst, d0=d0, c=c, tag=tag)
-
-    def reduce(bank, lo, hi, hb, t, k, tag):
-        take(bank, lo, hi, hb, t * I, -2047.5, tag)
-        add("low", "V", hi - lo, [bank, rg(hb, t * I + lo, t * I + hi)], [rg("U", uc(k, t) + lo, uc(k, t) + hi)],
-            bank=bank[0], lo=lo, hi=hi, hb=hb, h0=t * I, d0=uc(k, t), tag=tag)
+    def take(bank, lo, hi, dst, d0, c, tag, kind="take"):
+        add(kind, "VS", hi - lo, [bank], [rg(dst, d0 + lo, d0 + hi)], bank=bank[0], lo=lo, hi=hi, dst=dst, d0=d0, c=c, tag=tag)
 
     for t in range(RO):
         add("wrap", "G", 1, [X(t, 0, 1)], [X(t, W, W + 1)], t=t, tag=("p", t))
@@ -186,274 +193,140 @@ def build_ops(par):
                 for b in (H, 0):
                     e = "G" if left >= hi - lo else "Y"
                     left -= (hi - lo) if e == "G" else 0
-                    for c in range(lo, hi, par["gp"] if e == "G" else W):
-                        copy(e, 0, 1, b + c, b + min(hi, c + (par["gp"] if e == "G" else W)))
-            for to in range(2, RO):
-                if par["tails"][to - 2] in "YV":
-                    copy("Y" if par["tails"][to - 2] == "Y" else "VS", 0, to, XE, W)
-                else:
-                    copy("G", 0, to, XE, XE + 256)
-                    copy("G", 0, to, XE + 256, W)
+                    step = par["gp"] if e == "G" else W
+                    for c in range(lo, hi, step):
+                        if b + c < XE:
+                            copy(e, 0, 1, b + c, min(b + hi, b + c + step, XE))
+            for to in range(1, RO):
+                copy(par["tails"][to - 1], 0, to, XE, W, tag=("e", to))
         elif t < RO - 1:
-            gx, gp, dp, vx = par["gx"][t - 1], par["gp"], par["dp"], par["vx"][t - 1]
-            for lo in range(0, vx, 448):
-                copy("VS", t, t + 1, lo, min(vx, lo + 448))
-            gx = min(XE, vx + gx)
-            for lo in range(vx, gx, gp):
+            gx, gp, dp = par["gx"][t - 1], par["gp"], par["dp"]
+            for lo in range(0, gx, gp):
                 copy("G", t, t + 1, lo, min(gx, lo + gp))
             prev = []
             for lo in range(gx, XE, dp):
-                o = copy("Y", t, t + 1, lo, min(XE, lo + dp))
+                o = copy("Y", t, t + 1, lo, min(lo + dp, XE))
                 if par["pace"] and len(prev) >= par["pace"]:
                     o["deps"].add(prev[-par["pace"]])
                 prev.append(o["ix"])
         tag = ("s", t)
         for (lo, hi) in (par["first_sum"] if t == 0 else parts_of("s", t - 1)):
-            n = max(64, hi - lo)
+            n, c = max(64, hi - lo), t * I
             if t:
-                add("cvs", "V", (hi - lo) // 2, [rg("L", uc(L_S, t) + lo, uc(L_S, t) + hi)], [rg("s16", t * I + lo, t * I + hi)],
+                add("cvs", "V", (hi - lo) // 2, [rg("L", uc(L_S, t) + lo, uc(L_S, t) + hi)], [rg("s16", c + lo, c + hi)],
                     t=t, lo=lo, hi=hi, tag=tag)
+            add("col", "VS" if t == 0 and lo in par["col0"] else "G", hi - lo, [X(t, 16 * lo, 1 + 16 * (hi - 1) + t)],
+                [rg("col", c + lo, c + hi)], t=t, lo=lo, hi=hi, tag=tag)
             bank = ps("a", t, lo)
-            add("sumx", "P", 5 * n, [X(t, 16 * lo, 16 * hi), rg("IF", 0, 128), rg("cs", 0, I)], [bank], t=t, lo=lo, hi=hi, bank=bank[0], tag=tag)
-            add("sums", "P", n, [rg("s16", t * I + lo, t * I + hi), rg("II", 0, 256)], [bank], t=t, lo=lo, hi=hi, bank=bank[0], tag=tag)
-            reduce(bank, lo, hi, "hs", t, U_A, tag)
+            add("pre", "P", 2 * n, [rg("col", c + lo, c + hi), rg("NH", 0, 256), rg("cN", 0, I)], [bank],
+                t=t, lo=lo, hi=hi, bank=bank[0], tag=tag, mm=2)
+            add("sum", "P", 5 * n, [rg("s16", c + lo, c + hi), rg("II", 0, 256), rg("cM", 0, 2 * I)], [bank],
+                t=t, lo=lo, hi=hi, bank=bank[0], tag=tag, mm=5)
+            take(bank, lo, hi, "U", uc(U_A, t), W - 1.0, tag, "rest")
         for (lo, hi, bank) in stage("s", t, "U", uc(U_A, t), W):
             take(bank, lo, hi, "U", uc(U_S, t), 2048.0, tag)
             if t == RO - 1:
-                take(bank, lo, hi, "ysf", 0, 2048.0, ("y", t))
-                add("store", "Y", 4 * (hi - lo), [rg("ysf", lo, hi)], [], src="ysf", dst="ys", lo=lo, hi=hi)
+                add("cast", "G", hi - lo, [rg("U", uc(U_S, t) + lo, uc(U_S, t) + hi)], [rg("ysf", lo, hi)], lo=lo, hi=hi,
+                    c=uc(U_S, t), tag=("y", t))
+                add("store", "Y", 4 * (hi - lo), [rg("ysf", lo, hi)], [], src="ysf", dst="ys", lo=lo, hi=hi, tag=("y", t))
             else:
                 send(tag, "U", uc(U_S, t), "L", uc(L_S, t + 1), lo, hi, 3)
         if t < RO - 1:
             bl, c, tag = ps("l", t), 16 * t, ("x", t)
-            add("list", "P", 17 * 64, [(("G", "s", t), 0, I), rg("EW", 0, 144), rg("cl", 0, 16)], [bl], t=t, g=("G", "s", t), bank=bl[0], tag=tag)
+            add("list", "P", 17 * 64, [(("G", "s", t), 0, I), rg("EW", 0, 144), rg("cl", 0, 16)], [bl], t=t, g=("G", "s", t), bank=bl[0],
+                tag=tag, mm=17)
             add("lhi", "V", 14, [bl, rg("jd", 0, 16)], [rg("hl", c, c + 14)], t=t, bank=bl[0], tag=tag)
             add("llo", "V", 14, [bl, rg("hl", c, c + 14)], [rg("lx", c, c + 14)], t=t, bank=bl[0], tag=tag)
-            add("xg", "VS", I, [rg("lx", c, c + 14), X(t, 0, W)], [X(t + 1, 0, XE)], t=t, tag=tag)
-            add("xs", "V", I, [rg("lx", c, c + 14), X(t, 0, W)], [X(t + 1, 0, XE)], t=t, tag=tag)
+            add("xs", "V", I, [rg("lx", c, c + 14), X(t, 0, XE)], [X(t + 1, 0, XE)], t=t, tag=tag)
+            add("xg", "VS", I, [rg("lx", c, c + 14), X(t, 0, XE), X(t + 1, 0, XE)], [(("xg", t + 1), 0, 1)], t=t, tag=tag)
         for (name, obuf, o0, k, c, lk, dist) in (("1", "U", uc(U_S, t), U_1, 2048.0, L_1, 1), ("2", "L", uc(L_1, t), U_2, 2048.0, L_2, 2),
                                                  ("3", "L", uc(L_2, t), U_3, 2049.0, L_3, -3)):
             for (lo, hi, bank) in stage(name, t, obuf, o0, W):
                 take(bank, lo, hi, "U", uc(k, t), c, (name, t))
                 send((name, t), "U", uc(k, t), "L", uc(lk, t), lo, hi, dist)
         for (lo, hi, bank) in stage("p", t, "L", uc(L_3, t), W + 1):
-            reduce(bank, lo, hi, "hT", t, U_T, ("p", t))
-        for (lo, hi, bank) in stage("T", t, "U", uc(U_T, t), W):
-            if t < RO - 1:
-                take(bank, lo, hi, "tout", t * I, 0.0, ("T", t))
-                send(("T", t), "tout", t * I, "tin", (t + 1) * I, lo, hi, 3)
-            else:
-                take(bank, lo, hi, "ytf", 0, 2048.0, ("T", t))
-                add("store", "Y", 4 * (hi - lo), [rg("ytf", lo, hi)], [], src="ytf", dst="yt", lo=lo, hi=hi)
+            take(bank, lo, hi, "hT", t * I, -2047.5, ("p", t))
+            add("low", "V", hi - lo, [bank, rg("hT", t * I + lo, t * I + hi)], [rg("U", uc(U_T, t) + lo, uc(U_T, t) + hi)],
+                bank=bank[0], t=t, lo=lo, hi=hi, tag=("p", t))
+        tag = ("T", t)
+        if str(t) in par["turned"]:
+            gb = gathers("T", t, "U", uc(U_T, t), W)
+            for blocks in ([(0,), (1,)] if len(parts_of("T", t)) > 1 else [(0, 1)]):
+                bank, c = ps("T", t, blocks[0]), (2 * t + blocks[0]) * TW
+                for j in blocks:
+                    add("turn", "P", 16 * 64, [(gb, TB * j, TB * j + 128), rg("II", 0, 256)], [bank], j=j, c=128 * (j - blocks[0]),
+                        g=gb, bank=bank[0], tag=tag, mm=16)
+                n = 128 * len(blocks)
+                take(bank, 0, n, "tout", c, 0.0, tag)
+                add("send", "G", 4 * n, [rg("tout", c, c + n + 1)], [rg("tin", c, c + n), rg("tnx", c, c + n)], src=None, c=c, w=n,
+                    dist=3, tag=tag)
+                add("mend", "G", n // 16, [rg("tin", c, c + n)], [rg("tnx", c, c + n)], c=c, w=n, tag=tag)
+        elif t < RO - 1:
+            for (lo, hi, bank) in stage("T", t, "U", uc(U_T, t), W):
+                take(bank, lo, hi, "tout", 2 * t * TW, 0.0, tag)
+                send(tag, "tout", 2 * t * TW, "tin", 2 * t * TW, lo, hi, 3)
+        else:
+            for (lo, hi, bank) in stage("T", t, "U", uc(U_T, t), W, last):
+                take(bank, lo, hi, "ytf", 0, 2048.0, tag)
+                if hi < last or last == I:
+                    add("store", "Y", 4 * (hi - lo), [rg("ytf", lo, hi)], [], src="ytf", dst="yt", lo=lo, hi=hi, tag=tag)
+            if last < I:
+                n = 16 * (I - last)
+                add("gown", "V", n, [X(t, 0, W), rg("U", uc(U_T, t) + last, uc(U_T, t) + I), rg("own", 0, 256)], [rg("gm", 0, n)], t=t, tag=tag)
+                add("scan", "V", n // 2, [rg("gm", 0, n), rg("run", 0, 256)], [rg("gs", 0, n)], tag=tag)
+                add("ends", "V", I - last, [rg("gs", 0, n)], [rg("ytf", last, I)], tag=tag)
+                add("store", "Y", 4 * (I - lo), [rg("ytf", lo, I)], [], src="ytf", dst="yt", lo=lo, hi=I, tag=tag)
+    count = {}
+    for o in ops:
+        k, tag = o["kind"], "%s%d" % o["tag"] if o["tag"] else ""
+        if k[:4] == "copy":
+            k, tag = "copy", tag or str(o["to"])
+        j = count[k, tag] = count.get((k, tag), -1) + 1
+        o["name"] = k + "." + tag + "abcdefghijklmnopqrstuvwxyz"[j]
+        o["lane"] = par["lanes"].get(o["name"][5:], 3) if k == "send" else 0
     return ops, names
 
 
-DMAS = ("load", "copyx", "store", "send")
-SETUP = ("load", "sel", "iota", "ones", "const", "jand", "jeq", "dj", "jrow", "jadd")
-
-
-def cost(o, e, m):
-    k, n, cy = o["kind"], o["n"], 0.83 * m["f"]
-    if k in DMAS:
-        return (m["iss"] if k == "send" else 100), 8 * (m["row"] + n / (m["bw"] / 16.0))
-    if k in ("gath", "xg"):
-        return (50 if e == "V" else 65) + n * m["gc"] * 0.83, None
-    if k == "xs":
-        return 50 + n * m["sc"] * 0.83, None
-    if e == "P":
-        return n * m["pe"] * m["f"], None
-    if e == "G":
-        return (170 + 2 * n * 0.83) * m["f"], None
-    if e == "S" and o.get("half"):
-        n *= 2
-    return (max(64, n) + m["fix"]) * cy, None
-
-
-def plan(par):
-    ops, names = build_ops(par)
-    m = par["model"]
-    n, lat = len(ops), m["lat"]
-    succ = [[] for _ in ops]
+def arrange(par, text):
+    words = text.split()
+    ops, names = build_ops(dict(par, V=" ".join(w.rstrip("*") for w in words if ":" in w)))
+    rank = {w.rstrip("*"): j for j, w in enumerate(words)}
+    users, todo = {}, []
     for o in ops:
-        for d in o["deps"]:
-            succ[d].append(o["ix"])
-    due, key, end = [0.0] * n, [0.0] * n, {"V": 0.0, "S": 0.0}
-    for o in sorted((o for o in ops if o["kind"] == "gath"), key=lambda o: o["turn"]):
-        due[o["ix"]] = end[o["eng"]]
-        end[o["eng"]] += par["load"] * cost(o, o["eng"], m)[0]
-    for o in reversed(ops):
-        ix = o["ix"]
-        held, xfer = cost(o, o["eng"][0], m)
-        if o["kind"] != "gath":
-            due[ix] = min([due[u] for u in succ[ix]] + [end["V"] + 1000.0]) - held - lat - (0.0 if xfer is None else xfer + m["hop"] - 800)
-        p = 1e7 - due[ix]
-        if o["kind"] in SETUP:
-            p = 1e8 - 10 * ix
-        elif o["kind"] in ("un1", "un2", "un3", "un4"):
-            p = 2e8 - ix - (par["late"] if o["kind"] == "un3" else 0)
-        elif o["kind"] in ("send", "tadd"):
-            p += 1e7
-        elif o["kind"] == "gath":
-            p = 0.0
-        elif o["kind"] == "copyv" or (o["kind"] == "cv0" and o["tag"]):
-            p -= 2e7
-        key[ix] = p
-    turn = {"V": 0, "S": 0}
-    users = {}
-    for o in ops:
+        j = rank["%s%d:%d-%d" % (o["tag"] + (o["lo"], o["hi"])) if o["kind"] == "gath" else o["name"]]
+        o["on"] = ("S" if words[j].endswith("*") else "V") if o["eng"] == "VS" else o["eng"]
+        todo.append((j, o))
         for b in o["virt"]:
             users.setdefault(b, []).append(o["ix"])
-    slot, held_by = {}, {"G": [None] * NG, "ps": [None] * NB}
-    open_users = {b: len(u) for b, u in users.items()}
-    done_at = {b: 0.0 for b in users}
-    fin = [None] * n
-    left = [len(o["deps"]) for o in ops]
-    ready = {o["ix"]: 0.0 for o in ops if not o["deps"]}
-    free = {e: 0.0 for e in "VSPGY"}
-    order = {e: [] for e in "VSPGY"}
-    sent, dma = 0, 0.0
-
-    def offer(kind):
-        best = None
-        for s, old in enumerate(held_by[kind]):
-            if old is None:
-                return s, 0.0, None
-            if not open_users[old] and (best is None or done_at[old] + lat < best[1]):
-                best = (s, done_at[old] + lat, old)
-        return best
-
-    for nth in range(n):
-        offers = {"G": offer("G"), "ps": offer("ps")}
-        cand, first = {e: [] for e in free}, None
-        for ix, r in ready.items():
-            o = ops[ix]
-            eng = o["eng"]
-            if o["kind"] == "gath" and o["turn"] != turn[eng]:
-                continue
-            for b in o["virt"]:
-                if b not in slot:
-                    of = offers[b[0]]
-                    if of is None:
-                        r = None
-                        break
-                    r = max(r, of[1])
-            if r is None:
-                continue
-            if o["kind"] == "take" and max(r, free["S"]) <= max(r, free["V"]) + par["lean"]:
-                eng = "S"
-            for e in eng:
-                s = max(r, free[e])
-                cand[e].append((s, ix))
-                if first is None or s < first[0]:
-                    first = (s, e)
-        t0, e = first
-        _, ix, s = max((key[ix], -ix, s) for (s, ix) in cand[e] if s <= t0 + par["eps"][e])
-        o = ops[-ix]
-        if o["kind"] == "gath":
-            turn[e] += 1
+    todo = [o for (_, o) in sorted(todo, key=lambda x: x[0])]
+    free = {"G": [(s, None) for s in range(NG)], "ps": [(s, None) for s in range(NB)]}
+    slot, left, done, order = {}, {b: len(u) for b, u in users.items()}, set(), {e: [] for e in "VSPGY"}
+    while todo:
+        o = next(o for o in todo if o["deps"] <= done and all(b in slot or free[b[0]] for b in o["virt"]))
+        todo.remove(o)
         for b in o["virt"]:
             if b not in slot:
-                sl, _, old = offers[b[0]]
-                slot[b] = sl
-                held_by[b[0]][sl] = b
-                if old is not None:
-                    for u in users[b]:
-                        ops[u]["deps"] = ops[u]["deps"] | set(users[old])
-        held, xfer = cost(o, e, m)
-        if xfer is None:
-            f = s + held
-        else:
-            f = s + held + (m["hop"] - 800 if o["kind"] == "send" else m["dst"])
-            if o["kind"] == "send":
-                o["every"] = par["step"] if sent < par["narrow"] else 1
-                xfer *= o["every"]
-                if not sent:
-                    f += m["first"]
-                    held += m["first"] / 2
-                sent += 1
-            f = dma = max(f, dma) + xfer
-        ix = o["ix"]
-        fin[ix] = f
-        o["nth"], o["at"] = nth, s
-        free[e] = s + held
-        order[e].append(o)
-        del ready[ix]
-        for b in o["virt"]:
-            open_users[b] -= 1
-            done_at[b] = max(done_at[b], f)
-        for u in succ[ix]:
-            left[u] -= 1
-            if left[u] == 0:
-                ready[u] = max(fin[d] for d in ops[u]["deps"] if fin[d] is not None) + lat
-    return {"order": order, "slot": slot, "names": names, "ops": ops}
-
-
-def arrange(par):
-    words = {e: par["Q"][e].split() for e in "VSPGY"}
-    ops, names = build_ops(dict(par, V=" ".join(sorted(w for e in "VS" for w in words[e] if ":" in w)), S=""))
-    by, count, users = {}, {}, {}
-    for o in ops:
-        k, tag = o["kind"], "%s%d" % o["tag"] if o["tag"] else ""
-        if k == "take" and o["dst"] in ("hs", "hT"):
-            k = "high"
-        if k[:4] == "copy":
-            k, tag = "copy", str(o["to"])
-        j = count[k, tag] = count.get((k, tag), -1) + 1
-        by["%s:%d-%d" % (tag, o["lo"], o["hi"]) if k == "gath" else k + "." + tag + "abcdefghijklmnop"[j]] = o
-        for b in o["virt"]:
-            users.setdefault(b, []).append(o["ix"])
-    order = {e: [by[w] for w in words[e]] for e in words}
-    assert sorted(o["ix"] for e in order for o in order[e]) == list(range(len(ops)))
-    m = par["model"]
-    fin, pos, free = {}, {e: 0 for e in order}, {e: 0.0 for e in order}
-    slot, held = {}, {"G": [None] * NG, "ps": [None] * NB}
-    left, done = {b: len(u) for b, u in users.items()}, {}
-    sent, dma = 0, 0.0
-    for nth in range(len(ops)):
-        best = None
-        for e in order:
-            o = order[e][pos[e]] if pos[e] < len(order[e]) else None
-            if o is None or any(d not in fin for d in o["deps"]):
-                continue
-            r, offer = max([free[e]] + [fin[d] for d in o["deps"]]), None
-            new = [b for b in o["virt"] if b not in slot]
-            if new:
-                idle = [(0.0 if old is None else done[old], old is not None, s, old) for s, old in enumerate(held[new[0][0]])
-                        if old is None or not left[old]]
-                if not idle:
-                    continue
-                offer = min(idle, key=lambda x: (x[1], x[0], x[2]))
-                r = max(r, offer[0])
-            if best is None or r < best[0]:
-                best = (r, e, o, new, offer)
-        r, e, o, new, offer = best
-        if new:
-            slot[new[0]], held[new[0][0]][offer[2]], done[new[0]] = offer[2], new[0], offer[0]
-            for u in users[new[0]]:
-                ops[u]["deps"] = ops[u]["deps"] | set(users.get(offer[3], []))
-        hold, xfer = cost(o, e, m)
-        f = r + hold
-        if xfer is not None:
-            f += m["hop"] - 800 if o["kind"] == "send" else m["dst"]
-            if o["kind"] == "send":
-                o["every"] = 1
-                if not sent:
-                    f += m["first"]
-                    hold += m["first"] / 2
-                sent = 1
-            f = dma = max(f, dma) + xfer
-        fin[o["ix"]] = f + m["lat"]
-        o["nth"] = nth
-        free[e] = r + hold
-        pos[e] += 1
-        for b in o["virt"]:
+                slot[b], old = free[b[0]].pop(0)
+                for u in users[b]:
+                    ops[u]["deps"] = ops[u]["deps"] | set(users.get(old, []))
             left[b] -= 1
-            done[b] = max(done[b], f + m["lat"])
+            if not left[b]:
+                free[b[0]].append((slot[b], b))
+        o["nth"] = len(done)
+        done.add(o["ix"])
+        order[o["on"]].append(o)
     return {"order": order, "slot": slot, "names": names, "ops": ops}
 
 
-FIN = {'chunks': [0, 448, 896, 1408, 1792, 2048], 'joined': [448], 'si_at': 0, 'first_sum': [(0, 56), (56, 112), (128, 224), (112, 128)], 'g0': 2048, 'tails': 'GGY', 'gx': [1792, 1792, 2240], 'vx': [448, 0, 0], 'gp': 896, 'dp': 896, 'pace': 1, 'narrow': 0, 'cuts': {('s', 0): (54, 112), ('s', 1): (112,), ('1', 1): (112,), ('p', 3): (52, 118), ('T', 3): (112,), ('p', 4): (84, 166), ('T', 4): (84, 166), ('1', 3): (104,), ('T', 1): (90,), ('1', 2): (102,), ('p', 2): (120,), ('s', 4): (132,), ('2', 0): (118,), ('T', 2): (142,)}, 'Q': {'V': 'jand.a ones.a const.c jeq.a jrow.a ones.b dj.m dj.n dj.f const.a dj.b const.b dj.g dj.p un1.a dj.k un1.b cv0.a un4.a un1.c un4.b dj.l un1.d un4.c un1.e un4.d jadd.a un4.e low.s0a cv0.p0a low.s0b s0:0-42 low.s0d low.s0c s0:112-168 take.s0b 10:0-12 10:12-60 lhi.x0a take.s0c llo.x0a 10:112-158 xg.x0a xs.x0a cvs.s1b cvs.s1a high.s1b cvs.s1c low.s1b high.s1a high.s1c low.s1a low.s1c s1:0-54 s1:112-176 take.s1a 20:0-118 lhi.x1a 11:0-26 llo.x1a take.20b xg.x1a take.20a xs.x1a cvs.s2a cvs.s2b 11:112-146 low.s2a low.s2b s2:0-52 s2:106-166 30:0-108 lhi.x2a 21:0-104 llo.x2a take.30a 12:0-102 xg.x2a cvs.s3a xs.x2a p0:0-90 high.s3a p0:90-94 low.s3a take.12b s3:0-110 high.p0a s3:110-114 low.p0a 31:0-108 lhi.x3a T0:0-98 llo.x3a 22:0-132 xs.x3a cvs.s4a take.T0a p1:0-114 low.s4a 13:0-104 s4:0-132 take.13a low.p1a 32:0-90 take.13b 14:0-114 T1:0-90 23:0-102 take.14a p2:0-120 take.23a take.y4a 24:0-110 high.p2a high.p2b low.p2a low.p2b 33:0-92 take.24a T2:0-142 34:0-88 take.T2a p3:0-52 take.T2b p3:82-118 p3:158-210 low.p3a low.p3b T3:0-44 high.p3c T3:112-118 low.p3c T3:118-174 p4:0-44 take.T3b p4:166-196 p4:98-142 low.p4a T4:0-42 low.p4b low.p4c T4:84-126 take.T4a T4:166-194 take.T4b', 'S': 'dj.o dj.d dj.h dj.j dj.c dj.i dj.e dj.a un3.a un2.a un2.b un3.b un2.c un3.c un2.d un3.d un2.e high.s0a un3.e high.s0b s0:42-56 high.s0c high.s0d s0:56-112 take.s0a s0:168-224 10:60-112 10:158-224 take.10a copy.2c s1:54-112 s1:176-224 20:118-224 take.s1b 11:26-112 11:146-224 high.s2a high.s2b take.11a s2:52-106 take.11b s2:166-224 30:108-224 take.s2a 21:104-224 12:102-224 take.21a take.12a p0:94-224 s3:114-224 31:108-224 take.s3a T0:98-224 take.31a xg.x3a 22:132-224 13:104-224 take.22a high.s4a p1:114-224 s4:132-224 high.p1a 32:90-224 take.s4a T1:90-224 take.s4b take.32a 14:114-224 take.T1b 23:102-224 take.T1a p2:120-224 24:110-224 33:92-224 T2:142-192 take.33a T2:192-224 34:88-224 p3:210-224 p3:52-82 take.y4b take.34a p3:118-158 high.p3a high.p3b T3:44-112 T3:174-224 take.T3a p4:44-98 p4:196-224 p4:142-166 high.p4a T4:42-72 high.p4b high.p4c T4:72-84 T4:126-166 T4:194-224 take.T4c', 'P': 'sumx.s0a sums.s0a sumx.s0b sums.s0b sumx.s0c sumx.s0d sums.s0c sums.s0d pick.s0a pick.s0b pick.s0c list.x0a pick.s0d pick.10a pick.10b sumx.s1b sumx.s1a sums.s1b sumx.s1c sums.s1a sums.s1c pick.s1a list.x1a pick.s1b pick.20b pick.20a pick.11a sumx.s2a sumx.s2b sums.s2a sums.s2b pick.11b pick.s2a list.x2a pick.s2b pick.30a pick.30b pick.21a pick.21b pick.12a sumx.s3a sums.s3a pick.12b pick.p0a tadd.p0a pick.p0b tadd.p0b pick.s3a pick.s3b list.x3a pick.31a pick.31b pick.T0a pick.T0b pick.22a sumx.s4a pick.22b sums.s4a pick.13b pick.p1a tadd.p1a pick.p1b tadd.p1b pick.13a pick.s4a pick.s4b pick.32a pick.32b pick.14a pick.T1b pick.14b pick.T1a pick.23a pick.23b pick.p2a pick.p2b tadd.p2b tadd.p2a pick.24a pick.24b pick.33a pick.33b pick.T2a pick.T2b pick.34a pick.34b pick.p3a pick.p3b tadd.p3a tadd.p3b pick.p3c tadd.p3c pick.T3a pick.T3b pick.p4a pick.p4c tadd.p4a pick.p4b tadd.p4b tadd.p4c pick.T4a pick.T4b pick.T4c', 'G': 'iota.a sel.a sel.b sel.c sel.d iota.b sel.e copy.1a wrap.p0a sel.f copy.1b copy.1c copy.1d copy.2b copy.1i send.s0a send.s0b send.s0c copy.3a send.10a copy.2d copy.2e copy.2a send.s1a send.s1b send.20b send.20a copy.3c send.11a send.11b copy.3d send.s2a wrap.p1a send.30a copy.3b send.21a copy.4d copy.4c send.12a send.12b send.s3a copy.4b send.31a wrap.p2a send.T0a send.22a send.13b send.13a send.32a send.T1b send.14a send.T1a send.23a send.24a send.33a wrap.p3a wrap.p4a send.T2a send.T2b send.34a send.T3a send.T3b', 'Y': 'load.a load.b load.c load.d load.e load.f copy.1f copy.1j copy.1h copy.1e copy.1g copy.2f copy.2g copy.3e copy.3f copy.4e copy.4f copy.4a store.a store.b store.c store.d store.e'}}
-PLAN = arrange(dict(PAR, **FIN))
+PAR = {'chunks': [0, 640, 1472, 2048], 'first_sum': [(144, 224), (80, 144), (0, 80)], 'g0': 2560, 'tails': 'YYGY', 'gx': [1344, 1344, 1344], 'gp': 896, 'dp': 1344, 'pace': 0, 'cuts': {'s0': (26, 116), 's1': (116,), 's3': (102,), '11': (168,), '34': (114,), 'T3': (112,), 'p4': (112,), 'T4': (110, 176), '23': (108,), 'p3': (100,), 'p2': (108,)}, 'noseam': ['13', '14', '23', '24', '32', '34', 'T2', 'p1', 'p3', 's0', 's1', 's4'], 'turned': '01', 'si_cut': 84, 'col0': (0,), 'last': 212, 'narrow': 0}
+ORDER = 'iota.a ones.a jand.a sel.a jeq.a dj.m* load.a dj.i* big.a dj.h pads.a const.a half.a sel.b iota.b load.b const.b dj.j* const.c dj.b* dj.n* dj.p dj.l* dj.c big.b dj.k jrow.a jadd.a dj.a own.a own.b own.c own.d own.e ua.a uc.a ua.b dj.f* dj.d* dj.o* uc.c ub.a* dj.g* dj.e* uc.b* ub.b* load.c load.s0a load.s0b copy.1a copy.1b uc.d* ua.c col.s0c pre.s0c uc.e ub.c* cv0.a* uc.f* cv0.b* sum.s0c rest.s0c col.s0a col.s0b s0:0-26 pre.s0a pre.s0b sum.s0a sum.s0b rest.s0b s0:26-80* load.T0a copy.1d copy.1e copy.1f copy.e1a copy.1c pick.s0a rest.s0a take.s0a* s0:166-224* s0:80-118 send.s0a pick.s0b s0:118-166 take.s0b* list.x0a pick.s0c 10:0-72* 10:72-116 lhi.x0a llo.x0a xs.x0a take.s0c* 10:116-176* 10:176-224 pick.10a send.s0b send.s0c col.s1b col.s1a col.s1c pre.s1b pre.s1a pick.10b cv0.p0a* take.10a* xg.x0a cvs.s1a cvs.s1b cvs.s1c sum.s1b rest.s1b copy.2d sum.s1a rest.s1a* s1:62-116 s1:0-62* send.10a pre.s1c sum.s1c rest.s1c s1:178-224 pick.s1a s1:116-178* take.s1a* 20:116-224* list.x1a pick.s1b 20:0-116 copy.2c copy.e2a pick.20a pick.20b lhi.x1a take.s1b llo.x1a copy.2a copy.2b send.s1a sel.c xs.x1a send.s1b col.s2b col.s2a 11:90-168 cvs.s2a pre.s2a pre.s2b sum.s2a take.20a cvs.s2b xg.x1a rest.s2a sum.s2b rest.s2b s2:46-164 11:168-224* 11:0-90* pick.11c pick.11a pick.11b s2:164-224* take.11b* s2:0-46* take.11a* copy.e4a send.20a send.11b send.11a copy.3b copy.e3a 30:102-224 30:0-102* pick.s2a list.x2a pick.30a pick.30b take.s2a 21:0-102 lhi.x2a take.30a 12:0-92 llo.x2a copy.3c copy.3d 21:102-224* 12:92-224* pick.21a pick.21b pick.12a pick.12b take.21a* wrap.p0a copy.3a send.s2a send.30a cvs.s3a xs.x2a sel.d sel.e sel.f col.s3a send.21a p0:78-224* pre.s3a sum.s3a p0:0-78 xg.x2a rest.s3a copy.4d copy.4c s3:102-224* pick.p0a tadd.p0a pick.p0b take.12a s3:0-102 31:0-102 pick.s3a tadd.p0b list.x3a take.p0a take.s3a lhi.x3a low.p0a pick.s3b 31:102-224* llo.x3a T0:0-78 take.s3b pick.31a pick.31b T0:78-224* send.12a wrap.p3a copy.4a copy.4b send.s3a send.s3b wrap.p2a take.31a* wrap.p1a send.31a 22:144-224* turn.T0a 22:0-144 turn.T0b pick.22a cvs.s4a xs.x3a cvs.s4b col.s4b take.T0a* col.s4a send.T0a 13:118-224 xg.x3a p1:0-112 pre.s4b pre.s4a pick.22b sum.s4b sum.s4a 13:0-118* take.22a* rest.s4b* send.22a pick.13a rest.s4a p1:112-224* take.13a* mend.T0a send.13a pick.p1a tadd.p1a s4:0-134* s4:134-224 pick.s4a 23:108-224* pick.23b 32:0-130 23:0-108 take.p1a* take.s4a* 32:130-224* take.23b* low.p1a 14:0-118 pick.23a 14:118-224* take.23a send.23b cast.y4a store.y4a pick.32a T1:0-116 pick.14a take.32a T1:116-224* turn.T1a turn.T1b take.14a* 33:116-224* take.T1a* send.23a 33:0-116 pick.33a pick.33b send.32a send.14a send.T1a mend.T1a p2:0-108 p2:108-224* pick.p2a take.33a* 24:132-224* 24:0-132 send.33a pick.p2b tadd.p2a tadd.p2b take.p2a take.p2b low.p2a low.p2b T2:0-106 pick.24a take.24a p3:0-100 T2:106-224* pick.T2a take.T2a send.24a send.T2a p3:100-224* pick.p3a 34:76-116* 34:0-76 34:176-224 pick.p3b pick.34a tadd.p3a tadd.p3b take.p3a take.p3b low.p3a low.p3b T3:0-64 34:116-176* take.34a* pick.34b T3:64-122* take.34b* T3:122-170* send.34a send.34b wrap.p4a T3:170-224 pick.T3a take.T3a p4:0-50 pick.T3b p4:50-112* p4:112-174* send.T3a take.T3b p4:174-224 pick.p4a tadd.p4a send.T3b take.p4a low.p4a T4:0-52 T4:52-112* pick.p4b tadd.p4b pick.T4a take.p4b low.p4b T4:112-148 T4:148-176* pick.T4b T4:176-190 T4:190-212* take.T4a* take.T4b* store.T4a store.T4b gown.T4a pick.T4c scan.T4a ends.T4a take.T4c* store.T4c'
+PAR = {'chunks': [0, 576, 1312, 2048], 'first_sum': [(148, 224), (80, 148), (0, 80)], 'g0': 2048, 'tails': 'YYGY', 'gx': [1792, 1792, 1344], 'gp': 896, 'dp': 1344, 'pace': 0, 'cuts': {'s0': (26, 116), 's1': (108,), 's3': (102,), '11': (168,), '34': (112,), 'T3': (112,), 'p4': (112,), 'T4': (110, 172), '23': (108,), 'p3': (98,), 'p2': (108,)}, 'noseam': ['13', '14', '23', '24', '32', '34', 'T0', 'T2', 'T4', 'p1', 'p2', 'p3', 'p4', 's2', 's3', 's4'], 'turned': '01', 'si_cut': 80, 'col0': (0,), 'last': 210, 'lanes': {'s0a': 1, 's0b': 1, 's0c': 1}}
+ORDER = 'iota.a big.b ones.a jand.a sel.a jeq.a load.a const.c dj.e dj.l dj.m own.a dj.d dj.a* dj.o* dj.g* dj.b sel.b iota.b load.b load.c load.s0a load.s0b dj.c* dj.p big.a half.a dj.j* own.b const.a pads.a dj.i own.c ua.a jrow.a uc.a own.d ua.b own.e uc.c dj.n* dj.h* dj.f* ub.a* copy.1a dj.k* uc.b* copy.1b ub.b* uc.d* jadd.a col.s0c ua.c uc.e ub.c* cv0.a* uc.f* cv0.b* pre.s0c sum.s0c col.s0a col.s0b rest.s0c const.b s0:0-26 pre.s0a sum.s0a pre.s0b sum.s0b s0:26-80* copy.1d copy.1e copy.1f load.T0a copy.e1a copy.1c pick.s0a rest.s0b rest.s0a take.s0a* s0:168-224* s0:80-118 send.s0a pick.s0b s0:118-168 take.s0b* 10:0-74* list.x0a pick.s0c 10:74-116 lhi.x0a llo.x0a xs.x0a take.s0c* 10:174-224 pick.10a send.s0b send.s0c col.s1b col.s1a pre.s1b pre.s1a 10:116-174* xg.x0a pick.10b cvs.s1b cvs.s1a cv0.p0a take.10a* sum.s1b cvs.s1c rest.s1b copy.2d sum.s1a s1:56-108 rest.s1a* s1:0-56* col.s1c wrap.p1a send.10a pre.s1c sum.s1c rest.s1c s1:180-224 pick.s1a s1:108-180* take.s1a* 20:114-224* pick.s1b list.x1a 20:0-114 copy.2c copy.e2a pick.20a pick.20b lhi.x1a take.s1b llo.x1a copy.2a copy.2b xs.x1a send.s1a send.s1b col.s2b wrap.p0a col.s2a 11:92-168 cvs.s2a 11:168-224* pick.11c pre.s2a pre.s2b sum.s2a take.20a cvs.s2b xg.x1a rest.s2a sum.s2b rest.s2b take.11b s2:34-164 11:0-92* pick.11a pick.11b s2:0-34* s2:164-224* take.11a* send.20a send.11b send.11a 30:98-224 30:0-98* pick.s2a pick.30a pick.30b list.x2a take.s2a 21:0-96 take.30a lhi.x2a 12:0-94 llo.x2a copy.3c copy.3d 21:96-224* 12:94-224* pick.21a pick.21b pick.12a pick.12b take.21a* copy.3b copy.3a send.s2a cvs.s3a xs.x2a sel.c send.30a copy.e4a p0:0-72 xg.x2a send.21a col.s3a copy.e3a sel.d wrap.p2a sel.e p0:72-224* pre.s3a sum.s3a copy.4d pick.p0a tadd.p0a pick.p0b rest.s3a take.12a s3:102-224* s3:0-102 31:0-102 pick.s3a tadd.p0b list.x3a take.p0a lhi.x3a 31:102-224* take.s3a low.p0a llo.x3a pick.s3b pick.31a pick.31b T0:78-224* take.s3b* take.31a* send.12a copy.4c copy.4a send.s3a copy.4b send.s3b send.31a 22:144-224* T0:0-78 turn.T0a 22:0-144 turn.T0b pick.22a xs.x3a 13:118-224 cvs.s4b cvs.s4a col.s4a col.s4b pre.s4b pre.s4a pick.22b sum.s4b sum.s4a 13:0-118* take.T0a* take.22a* rest.s4b* p1:112-224* send.22a pick.13a take.13a* xg.x3a p1:0-112 rest.s4a send.T0a wrap.p3a send.13a wrap.p4a sel.f mend.T0a pick.p1a s4:0-136* s4:136-224 tadd.p1a pick.s4a 23:108-224* pick.23b 32:0-136 23:0-108 take.p1a take.s4a* 32:136-224* take.23b* 14:0-116 low.p1a pick.23a 14:116-224* take.23a send.23b pick.32a T1:0-112 pick.14a take.32a T1:112-224* turn.T1a turn.T1b take.14a* 33:116-224* take.T1a* send.23a 33:0-116 pick.33a pick.33b send.32a send.14a p2:0-108 p2:108-224* pick.p2a take.33a* 24:130-224* 24:0-130 send.T1a mend.T1a send.33a pick.p2b tadd.p2a tadd.p2b take.p2a take.p2b low.p2a low.p2b T2:0-108 pick.24a take.24a p3:0-98 T2:108-224* pick.T2a take.T2a send.24a send.T2a p3:98-224* pick.p3a 34:74-112* 34:0-74 34:174-224 pick.p3b pick.34a tadd.p3a tadd.p3b take.p3a take.p3b low.p3a low.p3b T3:0-64 34:112-174* take.34a* pick.34b T3:64-112* take.34b* T3:112-170* send.34a send.34b T3:170-224 pick.T3a take.T3a p4:0-54 pick.T3b p4:54-112* p4:112-178* take.T3b send.T3a cast.y4a send.T3b p4:178-224 pick.p4a tadd.p4a store.y4a take.p4a low.p4a T4:0-52 T4:52-112* pick.p4b tadd.p4b pick.T4a take.p4b low.p4b T4:112-144 T4:144-172* pick.T4b T4:172-194 T4:194-210* take.T4a* store.T4a take.T4b* store.T4b gown.T4a scan.T4a pick.T4c take.T4c* ends.T4a store.T4c'
+PAR = {'chunks': [0, 576, 1376, 2048], 'first_sum': [(156, 224), (80, 156), (0, 80)], 'g0': 2560, 'tails': 'YYYG', 'gx': [1792, 1792, 896], 'gp': 896, 'dp': 1792, 'pace': 2, 'cuts': {'s0': (26, 120), 's1': (106,), 's3': (102,), '11': (172,), '34': (112,), 'T3': (112,), 'p4': (112,), 'T4': (108, 170), '23': (108,), 'p3': (100,), 'p2': (108,), '10': (116,)}, 'noseam': ['10', '13', '14', '23', '24', '32', 'T0', 'T2', 'T3', 'T4', 'p1', 'p2', 's4'], 'turned': '01', 'si_cut': 88, 'col0': (0,), 'last': 208, 'lanes': {'s0a': 1}}
+ORDER = 'load.a iota.a ones.a pads.a jand.a sel.a jeq.a dj.l* own.a iota.b sel.b load.b load.c load.s0a load.s0b own.b half.a own.c dj.k* const.a dj.o dj.e big.b own.d big.a dj.n const.c jrow.a dj.b dj.a* dj.f* dj.h* dj.j* dj.i* dj.m const.b ua.a ub.a* uc.b* dj.g uc.a dj.d* dj.p ub.b* jadd.a copy.1a copy.1b ua.b dj.c uc.c uc.d* ua.c cv0.a col.s0c* ub.c* uc.f* pre.s0c sum.s0c uc.e own.e rest.s0c cv0.b* s0:0-26 col.s0a col.s0b pre.s0a sum.s0a pre.s0b sum.s0b s0:26-80* copy.1d copy.1e copy.1f load.T0a copy.e1a copy.1c pick.s0a rest.s0b rest.s0a s0:80-120 take.s0a* s0:170-224* send.s0a pick.s0b s0:120-170 take.s0b* 10:0-74* list.x0a pick.s0c 10:74-116 lhi.x0a llo.x0a xs.x0a take.s0c* 10:116-180* 10:180-224 pick.10a send.s0b send.s0c col.s1a col.s1b take.10a* send.10a pre.s1b pre.s1a cvs.s1a cvs.s1b sum.s1a sum.s1b pick.10b rest.s1a rest.s1b cvs.s1c xg.x0a* col.s1c pre.s1c copy.2c s1:0-64* s1:64-120 sum.s1c rest.s1c take.10b copy.2a send.10b s1:168-224* pick.s1a s1:120-168 take.s1a 11:0-94* pick.s1b list.x1a 20:0-114 copy.e2a pick.11a pick.20a lhi.x1a take.s1b llo.x1a cv0.p0a 20:114-224* send.s1a copy.2b xs.x1a send.s1b col.s2a sel.c wrap.p0a sel.d col.s2b pre.s2a cvs.s2a sum.s2a pick.20b 11:94-172 rest.s2a xg.x1a cvs.s2b 11:172-224* s2:42-96 take.20a* pre.s2b pick.11b sum.s2b pick.11c take.11a s2:0-42* rest.s2b* s2:96-164 take.11b* s2:164-224* send.20a send.11a send.11b sel.e copy.3b copy.3a 30:98-224 30:0-98* pick.s2a pick.s2b list.x2a pick.30a pick.30b 21:88-224* lhi.x2a take.s2a 21:0-88 take.30a 12:0-96 pick.21a pick.21b copy.3c 12:96-224* pick.12a pick.12b send.s2a send.30a take.21a llo.x2a cvs.s3a xs.x2a p0:0-72 xg.x2a copy.e3a wrap.p1a send.21a col.s3a p0:72-224* pre.s3a sum.s3a pick.p0a tadd.p0a pick.p0b rest.s3a take.12a s3:102-224* s3:0-102 31:0-102 pick.s3a tadd.p0b list.x3a 31:102-224* take.p0a lhi.x3a take.s3a low.p0a llo.x3a T0:0-74 pick.s3b pick.31a pick.31b T0:74-224* take.s3b* take.31a* copy.4c send.12a copy.4b wrap.p3a copy.4a send.s3a send.s3b send.31a 22:144-224* turn.T0a 22:0-144 turn.T0b pick.22a xs.x3a 13:118-224 cvs.s4b cvs.s4a xg.x3a take.T0a* col.s4b send.T0a col.s4a copy.e4a pre.s4b pick.22b pre.s4a sum.s4b sum.s4a 13:0-118* rest.s4b* take.22a* p1:0-112* pick.13a take.13a* p1:112-224 rest.s4a send.22a mend.T0a send.13a pick.p1a s4:0-134* s4:134-224 tadd.p1a pick.s4a 23:108-224* pick.23b 32:0-136 23:0-108 take.p1a take.s4a* 32:136-224* take.23b* 14:0-116 low.p1a pick.23a 14:116-224* take.23a send.23b pick.32a T1:0-110 pick.14a take.32a T1:110-224* turn.T1a turn.T1b take.14a* 33:116-224* take.T1a* send.23a send.32a wrap.p2a 33:0-116 pick.33a pick.33b p2:0-108 p2:108-224* pick.p2a take.33a* send.14a wrap.p4a send.T1a cast.y4a sel.f send.33a mend.T1a 24:128-224* 24:0-128 pick.p2b tadd.p2a tadd.p2b take.p2a take.p2b low.p2a low.p2b T2:0-108 pick.24a take.24a p3:0-100 T2:108-224* pick.T2a take.T2a send.24a send.T2a p3:100-224* pick.p3a 34:72-112* 34:0-72 34:174-224 pick.p3b pick.34a tadd.p3a tadd.p3b take.p3a take.p3b low.p3a low.p3b T3:0-62 34:112-174* take.34a* pick.34b T3:62-112* take.34b* T3:112-170* send.34a send.34b T3:170-224 pick.T3a take.T3a p4:0-54 pick.T3b p4:54-112* p4:112-178* take.T3b send.T3a send.T3b p4:178-224 pick.p4a tadd.p4a store.y4a take.p4a low.p4a T4:0-54 T4:54-112* pick.p4b tadd.p4b pick.T4a take.p4b low.p4b T4:142-170 T4:112-142* pick.T4b T4:170-194 T4:194-208* take.T4a* store.T4a take.T4b* store.T4b pick.T4c take.T4c* gown.T4a scan.T4a ends.T4a store.T4c'
+PAR = {'chunks': [0, 576, 1312, 2048], 'first_sum': [(148, 224), (80, 148), (0, 80)], 'g0': 1536, 'tails': 'YYGG', 'gx': [1792, 896, 1792], 'gp': 896, 'dp': 896, 'pace': 1, 'cuts': {'s0': (28, 120), 's1': (106,), 's3': (100,), '11': (172,), '34': (112,), 'T3': (112,), 'p4': (112,), 'T4': (108, 172), '23': (110,), 'p3': (100,), 'p2': (108,), '10': (116,)}, 'noseam': ['13', '14', '23', '24', '32', 'T0', 'T2', 'T3', 'p1', 'p2', 's0', 's3', 's4'], 'turned': '01', 'si_cut': 80, 'col0': (0,), 'last': 208, 'lanes': {'s0a': 1, 's0b': 1, 's0c': 1, '10a': 1}}
+ORDER = 'load.a ones.a iota.a big.b const.c jand.a pads.a const.b const.a jrow.a jeq.a own.a big.a sel.a dj.o* dj.a* dj.m* dj.d* dj.p* dj.f* dj.b* dj.i own.b dj.k half.a dj.e own.c dj.n dj.c own.d dj.j own.e ua.a dj.h load.b load.s0a load.c load.s0b ub.a* uc.b* ub.b* uc.a ua.b sel.b iota.b copy.1a dj.l uc.c uc.d* cv0.a* col.s0c* pre.s0c sum.s0c jadd.a ua.c rest.s0c uc.e dj.g ub.c* uc.f* cv0.b* s0:0-28 col.s0a col.s0b copy.1b pre.s0a sum.s0a pre.s0b sum.s0b s0:28-80* copy.1d copy.1e copy.e2a copy.1f copy.1c copy.e1a pick.s0a rest.s0b rest.s0a s0:80-120 take.s0a* s0:168-224* send.s0a pick.s0b s0:120-168 take.s0b* 10:0-64* list.x0a pick.s0c 10:64-116 lhi.x0a llo.x0a xs.x0a take.s0c* 10:116-186* pick.10a send.s0b send.s0c col.s1a col.s1b col.s1c pre.s1a cvs.s1a 10:186-224 sum.s1a pre.s1b cvs.s1b rest.s1a sum.s1b rest.s1b cvs.s1c take.10a* xg.x0a* send.10a s1:0-62* s1:62-114 pre.s1c pick.10b sum.s1c rest.s1c take.10b copy.2a send.10b s1:172-224 pick.s1a s1:114-172* take.s1a 11:0-100* list.x1a pick.s1b 20:0-116 copy.2c load.T0a copy.2d pick.11a pick.20a lhi.x1a take.s1b 20:116-224* send.s1a copy.2b send.s1b llo.x1a cvs.s2a xs.x1a col.s2a sel.c wrap.p1a col.s2b sel.d pre.s2a sum.s2a 11:100-172 rest.s2a xg.x1a cvs.s2b 11:172-224* s2:40-96 pick.20b take.20a* pre.s2b pick.11b sum.s2b pick.11c take.11a s2:0-40* rest.s2b* s2:96-164 take.11b* s2:164-224* send.20a send.11a wrap.p0a send.11b copy.3a 30:98-224 30:0-98* pick.s2a pick.s2b list.x2a pick.30a pick.30b 21:88-224* take.s2a 21:0-88 pick.21a pick.21b lhi.x2a take.30a 12:0-96 copy.3b copy.3c copy.3d send.s2a send.30a take.21a send.21a cvs.s3a llo.x2a cv0.p0a xs.x2a p0:0-72 xg.x2a 12:96-224* pick.12a pick.12b sel.e col.s3a copy.e3a p0:72-224* pre.s3a sum.s3a rest.s3a pick.p0a tadd.p0a take.12a s3:100-224* s3:0-100 pick.p0b tadd.p0b pick.s3a list.x3a 31:0-104 31:104-224* take.p0a lhi.x3a low.p0a llo.x3a take.s3a T0:0-70 pick.s3b pick.31a pick.31b T0:70-224* take.s3b* take.31a* copy.4c copy.4a send.12a wrap.p3a wrap.p2a copy.4b copy.e4a copy.4d send.s3a send.s3b send.31a 22:144-224* turn.T0a 22:0-144 turn.T0b pick.22a cvs.s4a xs.x3a 13:118-224 cvs.s4b col.s4b col.s4a pre.s4b pre.s4a pick.22b xg.x3a p1:112-224 sum.s4a rest.s4a sum.s4b take.T0a* 13:0-118* take.22a* rest.s4b* p1:0-112* pick.13a take.13a* send.T0a send.22a send.13a mend.T0a sel.f pick.p1a s4:0-134* s4:134-224 tadd.p1a pick.s4a 23:110-224* pick.23b 32:0-134 take.p1a 23:0-110 take.s4a* 32:134-224* take.23b* low.p1a 14:0-110 pick.23a 14:110-224* take.23a send.23b send.23a pick.32a T1:0-118 pick.14a take.32a T1:118-224* turn.T1a turn.T1b take.14a* 33:116-224* take.T1a* send.32a send.14a send.T1a 33:0-116 pick.33a pick.33b p2:0-108 p2:108-224* pick.p2a take.33a* mend.T1a send.33a 24:128-224* 24:0-128 pick.p2b tadd.p2b tadd.p2a take.p2a take.p2b low.p2a low.p2b T2:0-108 pick.24a take.24a p3:0-100 T2:108-224* pick.T2a take.T2a send.24a wrap.p4a send.T2a p3:100-224* pick.p3a 34:74-112* 34:0-74 34:174-224 pick.p3b pick.34a tadd.p3a tadd.p3b take.p3a take.p3b low.p3a low.p3b T3:0-62 34:112-174* take.34a* pick.34b T3:62-112* take.34b* T3:112-170* cast.y4a send.34a send.34b T3:170-224 pick.T3a take.T3a p4:0-54 pick.T3b p4:54-112* p4:112-178* take.T3b send.T3a send.T3b p4:178-224 pick.p4a tadd.p4a store.y4a take.p4a low.p4a T4:0-54 T4:54-110* pick.p4b tadd.p4b pick.T4a take.p4b low.p4b T4:140-172 T4:110-140* pick.T4b T4:172-190 T4:190-208* take.T4a* take.T4b* pick.T4c gown.T4a scan.T4a store.T4a store.T4b ends.T4a take.T4c* store.T4c'
+PLAN = arrange(PAR, ORDER)
 SEMAPHORES = ["cV", "cS", "cP", "cG", "gone"] + PLAN["names"]
 
 
@@ -461,18 +334,22 @@ def rank_program(g, core, T, topo):
     rank = T.rank_of(core)
     if rank is None:
         return
-    order, slot = PLAN["order"], PLAN["slot"]
+    order, slot, last = PLAN["order"], PLAN["slot"], PAR["last"]
     Q = {"V": g.vector, "S": g.scalar, "P": g.tensor, "G": g, "Y": g.sync}
     V, S, P = g.vector, g.scalar, g.tensor
 
     def peer(d):
         return T.cores[(rank + d) % NR]
 
+    def engines(o, src, dst):
+        use = topo.engines(src, dst)
+        return use if o["lane"] == 3 else use[o["lane"] - 1::2]
+
     mark, total = {}, {}
     for e in order:
         for o in order[e]:
             if o["kind"] == "send":
-                mark[o["ix"]] = (o["sem"], len(topo.engines(peer(-o["dist"]), core)[::o["every"]]))
+                mark[o["ix"]] = (o["sem"], len(engines(o, peer(-o["dist"]), core)))
             elif o["sem"]:
                 mark[o["ix"]] = (o["sem"], 16)
             else:
@@ -485,41 +362,57 @@ def rank_program(g, core, T, topo):
             return V.tensor_scalar(out, in_, c, None, A.add)
         return S.activation(out, in_, F.Identity, bias=c)
 
+    def move(out, in_, n):
+        return g.affine_select(out, in_, [[0, n]], A.is_ge, 0.0, 0, 0)
+
     def emit(o, e):
         k = o["kind"]
         t, lo, hi = o.get("t"), o.get("lo"), o.get("hi")
         Xt = T["X%d" % t] if t is not None else None
         bank = T["ps%d" % slot[o["bank"]]] if "bank" in o else None
+        Gb = T["G%d" % slot[o["g"]]] if "g" in o else None
         if k in ("load", "store"):
             return Q[e].dma_start(T[o["dst"]][:, lo:hi], T[o["src"]][:, lo:hi])
         if k == "copyx":
             return Q[e].dma_start(T["X%d" % o["to"]][:, lo:hi], Xt[:, lo:hi])
         if k == "copyg":
-            return g.affine_select(T["X%d" % o["to"]][:, lo:hi], Xt[:, lo:hi], [[0, hi - lo]], A.is_ge, 0.0, 0, 0)
-        if k == "copyv":
-            return plus(e, T["X%d" % o["to"]][:, lo:hi], Xt[:, lo:hi], 0.0)
+            return move(T["X%d" % o["to"]][:, lo:hi], Xt[:, lo:hi], hi - lo)
         if k == "send":
             dst = peer(o["dist"])
             rid, pid, _ = topo.addr(dst)
-            use = topo.engines(core, dst)[::o["every"]]
-            g.remote_dma(T[o["dst"]][:, o["d0"]:o["d0"] + o["w"]], T[o["src"]][:, o["s0"]:o["s0"] + o["w"]],
-                         T.sem[o["sem"]], T.sem["gone"], pid, rid, sum(1 << x for x in use))
+            w, use = o["w"], engines(o, core, dst)
+            if o["src"]:
+                g.remote_dma(T[o["dst"]][:, o["d0"]:o["d0"] + w], T[o["src"]][:, o["s0"]:o["s0"] + w], T.sem[o["sem"]], T.sem["gone"],
+                             pid, rid, sum(1 << x for x in use))
+            else:
+                c = o["c"]
+                g.remote_dma_fused([RemoteDMATransfer(dst_ids=[DstId(rid=rid, pnc=pid)], dma_engine_mask=sum(1 << x for x in use[nxt::2]),
+                                                      remote_sem=T.sem[o["sem"]], src=T.tout[:, c + nxt:c + nxt + w],
+                                                      dst=(T.tnx if nxt else T.tin)[:, c:c + w]) for nxt in (0, 1)],
+                                   local_sem=T.sem["gone"])
             gone[0] += len(use)
             return None
+        if k == "mend":
+            c, w = o["c"], o["w"]
+            return move(T.tnx[:, c + 15:c + w:16], T.tin[:, c:c + w:16], w // 16)
+        if k == "cast":
+            return move(T.ysf[:, lo:hi], T.U[:, o["c"] + lo:o["c"] + hi], hi - lo)
+        if k == "pads":
+            return V.tensor_copy(T.tout[:, 0:8 * TW:8], T.one[:, 0:TW])
         if k == "ones":
-            return V.memset(T[o["buf"]][:], 1.0)
+            return V.memset(T.one[:], 1.0)
         if k == "const":
-            return V.tensor_scalar(T[o["buf"]][:], T.one[:, 0:o["w"]], o["c"], None, A.mult)
+            return V.tensor_scalar(T[o["buf"]][:], T.one[:, lo:hi], o["c"], None, A.mult)
         if k == "iota":
             return g.iota(T[o["buf"]][:], o["pat"], o["base"], o["cm"])
         if k == "sel":
             w = o["which"]
-            if w == "IF":
-                return g.affine_select(T.IF[:], T.onef[:], [[-1, 128]], A.is_equal, 0.0, 0, 1)
             if w == "II":
                 return g.affine_select(T.II[:], T.one[:], [[0, 2], [-1, 128]], A.is_equal, 0.0, 0, 1)
             if w == "EW":
                 return g.affine_select(T.EW[:], T.one[:, 0:144], [[-16, 9], [128, 16]], A.is_equal, 0.0, 16, 1)
+            if w == "run":
+                return g.affine_select(T.run[:], T.one[:], [[0, 16], [1, 16]], A.not_equal, 0.0, 0, 0)
             if w == "T1":
                 return g.affine_select(T.TT[:], T.II[:], [[0, 2], [-1, 128]], A.not_equal, 1.0, -1, 1)
             if w == "T2":
@@ -529,6 +422,9 @@ def rank_program(g, core, T, topo):
             return V.tensor_scalar(T.jc[:], T.ja[:], 15, None, A.bitwise_and)
         if k == "jeq":
             return V.tensor_scalar(T.mk[:], T.jc[:], 0.0, None, A.is_equal)
+        if k == "own":
+            w = o["w"]
+            return V.tensor_copy(T.own[:, w:2 * w], T.own[:, 0:w]) if w else V.tensor_copy(T.own[:, 0:16], T.mk[:])
         if k == "dj":
             j = o["j"]
             if e == "V":
@@ -539,46 +435,76 @@ def rank_program(g, core, T, topo):
         if k == "jadd":
             return V.tensor_scalar(T.jd[:], T.jb[:], T.jr[:, 0:1], None, A.add)
         if k == "cv0":
-            return V.tensor_scalar(T[o["dst"]][:, 0:I], T[o["src"]][:], -2048.0, None, A.add)
-        if k == "un1":
-            return V.tensor_scalar(T.bp[:, lo:hi], T.pw[:, lo:hi], -(2.0 ** 23 - 2048.5), MAGIC, A.add, A.add)
-        if k == "un2":
-            return S.activation(T["ps%d" % slot[o["virt"][0]]][:, 0:hi - lo], T.bp[:, lo:hi], F.Identity, bias=-(MAGIC - 2047.0 * W))
-        if k == "un3":
-            return S.activation(T.X0[:, H + lo:H + hi], T.bp[:, lo:hi], F.Identity, bias=-(MAGIC / W - 2047.0), scale=1.0 / W)
-        if k == "un4":
-            return V.tensor_tensor(T.X0[:, lo:hi], T.pw[:, lo:hi], T["ps%d" % slot[o["virt"][0]]][:, 0:hi - lo], A.subtract)
+            return plus(e, T[o["dst"]][:, lo:hi], T[o["src"]][:, lo:hi], -2048.0)
+        if k == "ua":
+            return V.tensor_scalar(T.X0[:, lo:hi], T.pw[:, lo:hi], W - 1, None, A.bitwise_and)
+        if k == "ub":
+            return S.activation(T.X0[:, H + lo:H + hi], T.pw[:, lo:hi], F.Identity, bias=-(2.0 ** 23 - 2048.5) / W, scale=1.0 / W)
+        if k == "uc":
+            return plus(e, T.X0[:, lo:hi], T.X0[:, lo:hi], -2047.0)
         if k == "wrap":
-            return g.affine_select(Xt[:, W:W + 1], Xt[:, 0:1], [[0, 1]], A.is_ge, 0.0, 0, 0)
+            return move(Xt[:, W:W + 1], Xt[:, 0:1], 1)
         if k == "cvs":
             c = (L_S * RO + t) * I
             return V.tensor_scalar(T.s16[:, t * I + lo:t * I + hi], T.L[:, c + lo:c + hi], -2048.0, None, A.add)
-        sh = 80 if t else 0
-        if k == "sumx":
-            P.matmul(bank[:, lo:hi], T.one[:, 0:128], T.cs[:, lo:hi], True, False)
-            return P.matmul(bank[:, lo:hi], T.IF[:], Xt[:, 16 * lo + t:16 * hi:16], False, False)
-        if k == "sums":
+        if k == "col":
+            if e != "G":
+                return plus(e, T.col[:, t * I + lo:t * I + hi], Xt[:, 16 * lo + t:16 * hi:16], 0.0)
+            return move(T.col[:, t * I + lo:t * I + hi], Xt[:, 16 * lo + t:16 * hi:16], hi - lo)
+        if k == "big":
+            return V.memset(T.cM[:, lo:lo + I], o["c"])
+        if k == "half":
+            return V.tensor_scalar(T.NH[:], T.II[:], -0.5, None, A.mult)
+        if k == "pre":
+            P.matmul(bank[:, lo:hi], T.one[:, 0:128], T.cN[:, lo:hi], True, False)
+            return P.matmul(bank[:, lo:hi], T.NH[:, 0:128], T.col[:, t * I + lo:t * I + hi], False, False)
+        if k == "sum":
+            sh = 80 if t else 0
+            P.matmul(bank[:, lo:hi], T.NH[:, sh:sh + 128], T.s16[:, t * I + lo:t * I + hi], False, False)
+            P.matmul(bank[:, lo:hi], T.one[:, 0:128], T.cM[:, lo:hi], False, False)
+            P.matmul(bank[:, lo:hi], T.one[:, 0:128], T.cM[:, I + lo:I + hi], False, False)
+            P.matmul(bank[:, lo:hi], T.II[:, 0:128], T.col[:, t * I + lo:t * I + hi], False, False)
             return P.matmul(bank[:, lo:hi], T.II[:, sh:sh + 128], T.s16[:, t * I + lo:t * I + hi], False, True)
-        if k == "take":
+        if k in ("take", "rest"):
             return plus(e, T[o["dst"]][:, o["d0"] + lo:o["d0"] + hi], bank[:, lo:hi], o["c"])
         if k == "low":
-            return V.tensor_tensor(T.U[:, o["d0"] + lo:o["d0"] + hi], bank[:, lo:hi], T[o["hb"]][:, o["h0"] + lo:o["h0"] + hi], A.subtract)
+            c = (U_T * RO + t) * I
+            return V.tensor_tensor(T.U[:, c + lo:c + hi], bank[:, lo:hi], T.hT[:, t * I + lo:t * I + hi], A.subtract)
         if k == "gath":
             win = Xt[:, 0:o["width"]].indirect(T[o["obuf"]][:, o["o0"] + lo:o["o0"] + hi])
-            return plus(e, T["G%d" % slot[o["virt"][0]]][:, 16 * lo:16 * hi], win, -2048.0)
+            return plus(e, T["G%d" % slot[o["virt"][0]]][:, 16 * lo:16 * hi], win, -1.0)
+        if k == "gown":
+            c = (U_T * RO + t) * I
+            return V.tensor_tensor(T.gm[:, 0:o["n"]], Xt[:, 0:W].indirect(T.U[:, c + last:c + I]), T.own[:, 0:o["n"]], A.mult)
+        if k == "scan":
+            n = 2 * o["n"]
+            return V.tensor_tensor_scan(T.gs[:, 0:n], T.run[:, 0:n], T.gm[:, 0:n], 0.0, A.mult, A.add)
+        if k == "ends":
+            return V.tensor_scalar(T.ytf[:, last:I], T.gs[:, 15:16 * o["n"]:16], 2047.0, None, A.add)
         if k == "pick":
-            Gb = T["G%d" % slot[o["g"]]]
             if o["extra"]:
                 P.matmul(bank[:, lo:hi], T.one[:, 0:128], T.cT[:, lo:hi], True, False)
             for j in range(16):
                 r = P.matmul(bank[:, lo:hi], T.D[:, 128 * j:128 * j + 128], Gb[:, 16 * lo + j:16 * hi:16],
                              j == 0 and not o["extra"], j == 15 and not o["extra"])
             return r
+        if k == "turn":
+            j = o["j"]
+            for a in range(16):
+                r = P.matmul(bank[:, o["c"] + a:o["c"] + 128:16], Gb[:, 16 * TB * j + a:16 * (TB * j + 128):16],
+                             T.II[:, 80 + a:208:16], True, True)
+            return r
         if k == "tadd":
-            return P.matmul(bank[:, lo:hi], T.TT[:, sh:sh + 128], T.tin[:, t * I + lo:t * I + hi], False, True)
+            if not o["sub"]:
+                sh = 80 if t else 0
+                return P.matmul(bank[:, lo:hi], T.TT[:, sh:sh + 128], T[o["src"]][:, o["c"] + lo:o["c"] + hi], False, True)
+            for (a, b, j, c) in o["sub"]:
+                for nxt in (0, 1):
+                    r = P.matmul(bank[:, a:b], (T.tnx if nxt else T.tin)[:, c:c + 128], T.II[:, a - TB * j:b - TB * j],
+                                 False, nxt == 1 and b == hi)
+            return r
         c = 16 * t
         if k == "list":
-            Gb = T["G%d" % slot[o["g"]]]
             P.matmul(bank[:, 0:14], T.one[:, 0:128], T.cl[:, 0:14], True, False)
             for a in range(16):
                 r = P.matmul(bank[:, 0:14], T.EW[:, 16 - a:144 - a], Gb[:, 16 * a:XE:256], False, a == 15)

from concourse.bass import DstId, RemoteDMATransfer
from concourse.mybir import AluOpType, ActivationFunctionType
A = AluOpType
F = ActivationFunctionType

NR, RO, I, W, H = 7, 5, 224, 4096, 2048
NG, NB = 12, 8
XW = W + 8
XE = 16 * I
MAGIC = 1.5 * 2.0 ** 35
BIG = 1.5 * 2.0 ** 19
MID = 1.5 * 2.0 ** 14
TB, TW = 96, 136
U_A, U_S, U_1, U_2, U_3, U_T = range(6)
L_S, L_1, L_2, L_3 = range(4)

SCRATCH = {
    "pw": ("sbuf", [128, H], "int32"),
    "si": ("sbuf", [128, I], "int32"), "ti": ("sbuf", [128, I], "int32"),
    "U": ("sbuf", [128, 6 * RO * I], "uint16"), "L": ("sbuf", [128, 4 * RO * I], "uint16"),
    "s16": ("sbuf", [128, RO * I], "float16"), "col": ("sbuf", [128, RO * I], "float16"), "t16": ("sbuf", [128, I], "float16"),
    "tout": ("sbuf", [128, 8 * TW], "float16"), "tin": ("sbuf", [128, 8 * TW], "float16"), "tnx": ("sbuf", [128, 8 * TW], "float16"),
    "hT": ("sbuf", [128, RO * I], "bfloat16"),
    "hl": ("sbuf", [128, 64], "float16"), "lx": ("sbuf", [128, 64], "uint16"),
    "cN": ("sbuf", [128, I], "float16"), "cM": ("sbuf", [128, 2 * I], "bfloat16"), "NH": ("sbuf", [128, 256], "bfloat16"),
    "cT": ("sbuf", [128, I], "float16"), "cl": ("sbuf", [128, 16], "float16"),
    "ja": ("sbuf", [128, 16], "int32"), "jb": ("sbuf", [128, 16], "int32"), "jc": ("sbuf", [128, 16], "int32"),
    "jr": ("sbuf", [128, 16], "float32"), "jd": ("sbuf", [128, 16], "float32"), "mk": ("sbuf", [128, 16], "float32"),
    "one": ("sbuf", [128, 256], "bfloat16"),
    "D": ("sbuf", [128, 2048], "bfloat16"), "II": ("sbuf", [128, 256], "bfloat16"), "TT": ("sbuf", [128, 256], "bfloat16"),
    "EW": ("sbuf", [128, 144], "bfloat16"),
    "own": ("sbuf", [128, 256], "float16"), "run": ("sbuf", [128, 256], "float16"),
    "gm": ("sbuf", [128, 256], "float16"), "gs": ("sbuf", [128, 256], "float16"),
    "ysf": ("sbuf", [128, I], "float32"), "ytf": ("sbuf", [128, I], "float32"),
}
for _t in range(RO):
    SCRATCH["X%d" % _t] = ("sbuf", [128, XW], "int32")
for _t in range(NG):
    SCRATCH["G%d" % _t] = ("sbuf", [128, 16 * I], "float16")
for _t in range(NB):
    SCRATCH["ps%d" % _t] = ("psum", [128, 512], "float32")

DMAS = ("load", "copyx", "store", "send")


def pieces(cuts, lo=0, hi=I):
    c = [lo] + list(cuts) + [hi]
    return list(zip(c[:-1], c[1:]))


def build_ops(par):
    ops, wr, names = [], {}, []

    def add(kind, eng, n, rd, wt, **kw):
        o = {"ix": len(ops), "kind": kind, "eng": eng, "n": n, "deps": set(), "virt": [], "sem": None, "tag": None, "mm": 0}
        o.update(kw)
        if kind != "col":
            rd = rd + [(("xg", b[1]), 0, 1) for (b, lo, hi) in rd if b[0] == "X" and lo < XE]
        for (b, lo, hi) in rd:
            if b[0] == "ps":
                wt = wt + [(b, 0, 512)]
                continue
            for (j, l2, h2) in wr.get(b, []):
                if l2 < hi and lo < h2:
                    o["deps"].add(j)
        for (b, lo, hi) in wt:
            for (j, l2, h2) in wr.get(b, []):
                if l2 < hi and lo < h2:
                    o["deps"].add(j)
            wr.setdefault(b, []).append((o["ix"], lo, hi))
        for (b, lo, hi) in rd + wt:
            if b[0] in ("ps", "G") and b not in o["virt"]:
                o["virt"].append(b)
        if kind in DMAS:
            o["sem"] = "d%d" % len(names)
            names.append(o["sem"])
        ops.append(o)
        return o

    def rg(b, lo, hi):
        return ((b,), lo, hi)

    def X(t, lo, hi):
        return (("X", t), lo, hi)

    def ps(*b):
        return (("ps",) + b, 0, 512)

    ch, sc, last = pieces(par["chunks"][1:-1], 0, H), par["si_cut"], par["last"]
    for j, (lo, hi) in enumerate(ch):
        add("load", "Y", 4 * (hi - lo), [], [rg("pw", lo, hi)], src="pm", dst="pw", lo=lo, hi=hi)
    for (lo, hi) in pieces([sc]):
        add("load", "Y", 4 * (hi - lo), [], [rg("si", lo, hi)], src="sa", dst="si", lo=lo, hi=hi, tag=("s", 0))
    add("load", "Y", 4 * I, [], [rg("ti", 0, I)], src="ta", dst="ti", lo=0, hi=I, tag=("T", 0))
    add("ones", "V", 128, [], [rg("one", 0, 256)])
    add("iota", "G", 16, [], [rg("ja", 0, 16)], buf="ja", pat=[[-1, 16]], base=16, cm=1)
    add("sel", "G", 256, [rg("one", 0, 256)], [rg("II", 0, 256)], which="II")
    add("iota", "G", 16, [], [rg("jb", 0, 16)], buf="jb", pat=[[256, 16]], base=0, cm=0)
    add("sel", "G", 144, [rg("one", 0, 144)], [rg("EW", 0, 144)], which="EW")
    add("sel", "G", 256, [rg("II", 0, 256)], [rg("TT", 0, 256)], which="T1")
    add("sel", "G", 16, [], [rg("TT", 0, 256)], which="T2")
    add("sel", "G", 16, [], [rg("TT", 0, 256)], which="T3")
    add("pads", "V", 68, [rg("one", 0, 256)], [rg("tout", 0, 8 * TW)])
    add("jand", "V", 16, [rg("ja", 0, 16)], [rg("jc", 0, 16)])
    add("jeq", "V", 16, [rg("jc", 0, 16)], [rg("mk", 0, 16)])
    for j in range(16):
        add("dj", "VS", 64, [rg("II", 0, 128), rg("mk", 0, 16)], [rg("D", 128 * j, 128 * j + 128)], j=j, half=1)
    add("const", "V", 112, [], [rg("cT", 0, I)], buf="cT", lo=0, hi=I, c=(BIG + 6144.0) / 128)
    add("const", "V", 16, [], [rg("cl", 0, 16)], buf="cl", lo=0, hi=16, c=(MID + 2048.0) / 128)
    add("const", "V", 112, [], [rg("cN", 0, I)], buf="cN", lo=0, hi=I, c=-2048.0 / 128)
    add("big", "V", 112, [], [rg("cM", 0, I)], lo=0, c=MAGIC / 128)
    add("big", "V", 112, [], [rg("cM", I, 2 * I)], lo=I, c=-MAGIC / 128)
    add("half", "V", 128, [rg("II", 0, 256)], [rg("NH", 0, 256)])
    add("jrow", "V", 16, [rg("jc", 0, 16)], [rg("jr", 0, 16)])
    add("jadd", "V", 16, [rg("jb", 0, 16), rg("jr", 0, 16)], [rg("jd", 0, 16)])
    for o in ops:
        if o["kind"] == "const":
            o["deps"].add(len(ch) + 3)
    if last < I:
        add("sel", "G", 256, [rg("one", 0, 256)], [rg("run", 0, 256)], which="run")
        add("own", "V", 16, [rg("mk", 0, 16)], [rg("own", 0, 16)], w=0)
        for w in (16, 32, 64, 128):
            add("own", "V", w // 2, [rg("own", 0, w)], [rg("own", w, 2 * w)], w=w)
    for (lo, hi) in pieces([sc]):
        add("cv0", "VS", hi - lo, [rg("si", lo, hi)], [rg("s16", lo, hi)], src="si", dst="s16", lo=lo, hi=hi)
    add("cv0", "VS", I, [rg("ti", 0, I)], [rg("t16", 0, I)], src="ti", dst="t16", lo=0, hi=I, tag=("p", 0))
    for (lo, hi) in ch:
        add("ua", "V", hi - lo, [rg("pw", lo, hi)], [X(0, lo, hi)], lo=lo, hi=hi)
        add("ub", "S", hi - lo, [rg("pw", lo, hi)], [X(0, H + lo, H + hi)], lo=lo, hi=hi)
        mid = (lo + hi) // 2
        add("uc", "V", mid - lo, [], [X(0, lo, mid)], lo=lo, hi=mid)
        add("uc", "S", hi - mid, [], [X(0, mid, hi)], lo=mid, hi=hi)

    calls = {}
    for word in par["V"].split():
        lo, hi = word[3:].split("-")
        calls.setdefault(word[:2], []).append((int(lo), int(hi)))

    def uc(k, t):
        return (k * RO + t) * I

    def parts_of(name, t, end=I):
        return pieces(par["cuts"].get("%s%d" % (name, t), ()), 0, end)

    def send(tag, buf, c0, dbuf, d0, lo, hi, dist):
        add("send", "G", 2 * (hi - lo), [rg(buf, c0 + lo, c0 + hi)], [rg(dbuf, d0 + lo, d0 + hi)],
            src=buf, s0=c0 + lo, dst=dbuf, d0=d0 + lo, w=hi - lo, dist=dist, tag=tag)

    def copy(e, t, to, lo, hi, tag=None):
        return add("copyx" if e == "Y" else "copyg", e, (4 if e == "Y" else 1) * (hi - lo), [X(t, lo, hi)], [X(to, lo, hi)],
                   t=t, to=to, lo=lo, hi=hi, tag=tag)

    def gathers(name, t, obuf, o0, width):
        gb = ("G", name, t)
        for (c, d) in calls["%s%d" % (name, t)]:
            add("gath", "VS", 16 * (d - c), [X(t, 0, width), rg(obuf, o0 + c, o0 + d)], [(gb, c, d)],
                t=t, obuf=obuf, o0=o0, lo=c, hi=d, width=width, tag=(name, t))
        return gb

    def stage(name, t, obuf, o0, width, end=I):
        gb = gathers(name, t, obuf, o0, width)
        res = []
        for (lo, hi) in parts_of(name, t, end):
            bank = ps(name, t, lo)
            seam = sorted((abs(lo + hi - 2 * c), c) for (c, _) in calls["%s%d" % (name, t)] if lo + 64 <= c <= hi - 64)
            for (l2, h2) in pieces([seam[0][1]] if seam and "%s%d" % (name, t) not in par["noseam"] else [], lo, hi):
                extra = name == "p"
                n = max(64, h2 - l2)
                add("pick", "P", (17 if extra else 16) * n, [(gb, l2, h2), rg("D", 0, 2048), rg("cT", 0, I)], [bank], t=t, lo=l2, hi=h2,
                    extra=extra, g=gb, bank=bank[0], tag=(name, t), mm=17 if extra else 16)
                if extra and str(t - 1) not in par["turned"]:
                    src, c = ("tin", (2 * t - 2) * TW) if t else ("t16", 0)
                    add("tadd", "P", n, [rg(src, c + l2, c + h2), rg("TT", 0, 256)], [bank], t=t, lo=l2, hi=h2, src=src, c=c, sub=None,
                        bank=bank[0], tag=(name, t), mm=1)
                elif extra:
                    bs = TW if len(parts_of("T", t - 1)) > 1 else 128
                    sub = [(l2, h2, 0)] if h2 <= 128 else [(l2, h2, 1)] if l2 >= TB else [(l2, 112, 0), (112, h2, 1)]
                    sub = [(a, b, j, (2 * t - 2) * TW + j * bs) for (a, b, j) in sub]
                    add("tadd", "P", sum(2 * max(64, b - a) for (a, b, _, _) in sub),
                        [rg("tnx", c, c + 128) for (_, _, _, c) in sub] + [rg("II", 0, 256)], [bank],
                        t=t, lo=l2, hi=h2, sub=sub, bank=bank[0], tag=(name, t), mm=2 * len(sub))
            res.append((lo, hi, bank))
        return res

    def take(bank, lo, hi, dst, d0, c, tag, kind="take"):
        add(kind, "VS", hi - lo, [bank], [rg(dst, d0 + lo, d0 + hi)], bank=bank[0], lo=lo, hi=hi, dst=dst, d0=d0, c=c, tag=tag)

    for t in range(RO):
        add("wrap", "G", 1, [X(t, 0, 1)], [X(t, W, W + 1)], t=t, tag=("p", t))
        if t == 0:
            left = par["g0"]
            for (lo, hi) in ch:
                for b in (H, 0):
                    e = "G" if left >= hi - lo else "Y"
                    left -= (hi - lo) if e == "G" else 0
                    step = par["gp"] if e == "G" else W
                    for c in range(lo, hi, step):
                        if b + c < XE:
                            copy(e, 0, 1, b + c, min(b + hi, b + c + step, XE))
            for to in range(1, RO):
                copy(par["tails"][to - 1], 0, to, XE, W, tag=("e", to))
        elif t < RO - 1:
            gx, gp, dp = par["gx"][t - 1], par["gp"], par["dp"]
            for lo in range(0, gx, gp):
                copy("G", t, t + 1, lo, min(gx, lo + gp))
            prev = []
            for lo in range(gx, XE, dp):
                o = copy("Y", t, t + 1, lo, min(lo + dp, XE))
                if par["pace"] and len(prev) >= par["pace"]:
                    o["deps"].add(prev[-par["pace"]])
                prev.append(o["ix"])
        tag = ("s", t)
        for (lo, hi) in (par["first_sum"] if t == 0 else parts_of("s", t - 1)):
            n, c = max(64, hi - lo), t * I
            if t:
                add("cvs", "V", (hi - lo) // 2, [rg("L", uc(L_S, t) + lo, uc(L_S, t) + hi)], [rg("s16", c + lo, c + hi)],
                    t=t, lo=lo, hi=hi, tag=tag)
            add("col", "VS" if t == 0 and lo in par["col0"] else "G", hi - lo, [X(t, 16 * lo, 1 + 16 * (hi - 1) + t)],
                [rg("col", c + lo, c + hi)], t=t, lo=lo, hi=hi, tag=tag)
            bank = ps("a", t, lo)
            add("pre", "P", 2 * n, [rg("col", c + lo, c + hi), rg("NH", 0, 256), rg("cN", 0, I)], [bank],
                t=t, lo=lo, hi=hi, bank=bank[0], tag=tag, mm=2)
            add("sum", "P", 5 * n, [rg("s16", c + lo, c + hi), rg("II", 0, 256), rg("cM", 0, 2 * I)], [bank],
                t=t, lo=lo, hi=hi, bank=bank[0], tag=tag, mm=5)
            take(bank, lo, hi, "U", uc(U_A, t), W - 1.0, tag, "rest")
        for (lo, hi, bank) in stage("s", t, "U", uc(U_A, t), W):
            take(bank, lo, hi, "U", uc(U_S, t), 2048.0, tag)
            if t == RO - 1:
                add("cast", "G", hi - lo, [rg("U", uc(U_S, t) + lo, uc(U_S, t) + hi)], [rg("ysf", lo, hi)], lo=lo, hi=hi,
                    c=uc(U_S, t), tag=("y", t))
                add("store", "Y", 4 * (hi - lo), [rg("ysf", lo, hi)], [], src="ysf", dst="ys", lo=lo, hi=hi, tag=("y", t))
            else:
                send(tag, "U", uc(U_S, t), "L", uc(L_S, t + 1), lo, hi, 3)
        if t < RO - 1:
            bl, c, tag = ps("l", t), 16 * t, ("x", t)
            add("list", "P", 17 * 64, [(("G", "s", t), 0, I), rg("EW", 0, 144), rg("cl", 0, 16)], [bl], t=t, g=("G", "s", t), bank=bl[0],
                tag=tag, mm=17)
            add("lhi", "V", 14, [bl, rg("jd", 0, 16)], [rg("hl", c, c + 14)], t=t, bank=bl[0], tag=tag)
            add("llo", "V", 14, [bl, rg("hl", c, c + 14)], [rg("lx", c, c + 14)], t=t, bank=bl[0], tag=tag)
            add("xs", "V", I, [rg("lx", c, c + 14), X(t, 0, XE)], [X(t + 1, 0, XE)], t=t, tag=tag)
            add("xg", "VS", I, [rg("lx", c, c + 14), X(t, 0, XE), X(t + 1, 0, XE)], [(("xg", t + 1), 0, 1)], t=t, tag=tag)
        for (name, obuf, o0, k, c, lk, dist) in (("1", "U", uc(U_S, t), U_1, 2048.0, L_1, 1), ("2", "L", uc(L_1, t), U_2, 2048.0, L_2, 2),
                                                 ("3", "L", uc(L_2, t), U_3, 2049.0, L_3, -3)):
            for (lo, hi, bank) in stage(name, t, obuf, o0, W):
                take(bank, lo, hi, "U", uc(k, t), c, (name, t))
                send((name, t), "U", uc(k, t), "L", uc(lk, t), lo, hi, dist)
        for (lo, hi, bank) in stage("p", t, "L", uc(L_3, t), W + 1):
            take(bank, lo, hi, "hT", t * I, -2047.5, ("p", t))
            add("low", "V", hi - lo, [bank, rg("hT", t * I + lo, t * I + hi)], [rg("U", uc(U_T, t) + lo, uc(U_T, t) + hi)],
                bank=bank[0], t=t, lo=lo, hi=hi, tag=("p", t))
        tag = ("T", t)
        if str(t) in par["turned"]:
            gb = gathers("T", t, "U", uc(U_T, t), W)
            for blocks in ([(0,), (1,)] if len(parts_of("T", t)) > 1 else [(0, 1)]):
                bank, c = ps("T", t, blocks[0]), (2 * t + blocks[0]) * TW
                for j in blocks:
                    add("turn", "P", 16 * 64, [(gb, TB * j, TB * j + 128), rg("II", 0, 256)], [bank], j=j, c=128 * (j - blocks[0]),
                        g=gb, bank=bank[0], tag=tag, mm=16)
                n = 128 * len(blocks)
                take(bank, 0, n, "tout", c, 0.0, tag)
                add("send", "G", 4 * n, [rg("tout", c, c + n + 1)], [rg("tin", c, c + n), rg("tnx", c, c + n)], src=None, c=c, w=n,
                    dist=3, tag=tag)
                add("mend", "G", n // 16, [rg("tin", c, c + n)], [rg("tnx", c, c + n)], c=c, w=n, tag=tag)
        elif t < RO - 1:
            for (lo, hi, bank) in stage("T", t, "U", uc(U_T, t), W):
                take(bank, lo, hi, "tout", 2 * t * TW, 0.0, tag)
                send(tag, "tout", 2 * t * TW, "tin", 2 * t * TW, lo, hi, 3)
        else:
            for (lo, hi, bank) in stage("T", t, "U", uc(U_T, t), W, last):
                take(bank, lo, hi, "ytf", 0, 2048.0, tag)
                if hi < last or last == I:
                    add("store", "Y", 4 * (hi - lo), [rg("ytf", lo, hi)], [], src="ytf", dst="yt", lo=lo, hi=hi, tag=tag)
            if last < I:
                n = 16 * (I - last)
                add("gown", "V", n, [X(t, 0, W), rg("U", uc(U_T, t) + last, uc(U_T, t) + I), rg("own", 0, 256)], [rg("gm", 0, n)], t=t, tag=tag)
                add("scan", "V", n // 2, [rg("gm", 0, n), rg("run", 0, 256)], [rg("gs", 0, n)], tag=tag)
                add("ends", "V", I - last, [rg("gs", 0, n)], [rg("ytf", last, I)], tag=tag)
                add("store", "Y", 4 * (I - lo), [rg("ytf", lo, I)], [], src="ytf", dst="yt", lo=lo, hi=I, tag=tag)
    count = {}
    for o in ops:
        k, tag = o["kind"], "%s%d" % o["tag"] if o["tag"] else ""
        if k[:4] == "copy":
            k, tag = "copy", tag or str(o["to"])
        j = count[k, tag] = count.get((k, tag), -1) + 1
        o["name"] = k + "." + tag + "abcdefghijklmnopqrstuvwxyz"[j]
        o["lane"] = par["lanes"].get(o["name"][5:], 3) if k == "send" else 0
    return ops, names


def arrange(par, text):
    words = text.split()
    ops, names = build_ops(dict(par, V=" ".join(w.rstrip("*") for w in words if ":" in w)))
    rank = {w.rstrip("*"): j for j, w in enumerate(words)}
    users, todo = {}, []
    for o in ops:
        j = rank["%s%d:%d-%d" % (o["tag"] + (o["lo"], o["hi"])) if o["kind"] == "gath" else o["name"]]
        o["on"] = ("S" if words[j].endswith("*") else "V") if o["eng"] == "VS" else o["eng"]
        todo.append((j, o))
        for b in o["virt"]:
            users.setdefault(b, []).append(o["ix"])
    todo = [o for (_, o) in sorted(todo, key=lambda x: x[0])]
    free = {"G": [(s, None) for s in range(NG)], "ps": [(s, None) for s in range(NB)]}
    slot, left, done, order = {}, {b: len(u) for b, u in users.items()}, set(), {e: [] for e in "VSPGY"}
    while todo:
        o = next(o for o in todo if o["deps"] <= done and all(b in slot or free[b[0]] for b in o["virt"]))
        todo.remove(o)
        for b in o["virt"]:
            if b not in slot:
                slot[b], old = free[b[0]].pop(0)
                for u in users[b]:
                    ops[u]["deps"] = ops[u]["deps"] | set(users.get(old, []))
            left[b] -= 1
            if not left[b]:
                free[b[0]].append((slot[b], b))
        o["nth"] = len(done)
        done.add(o["ix"])
        order[o["on"]].append(o)
    return {"order": order, "slot": slot, "names": names, "ops": ops}


PAR = {'chunks': [0, 640, 1472, 2048], 'first_sum': [(144, 224), (80, 144), (0, 80)], 'g0': 2560, 'tails': 'YYGY', 'gx': [1344, 1344, 1344], 'gp': 896, 'dp': 1344, 'pace': 0, 'cuts': {'s0': (26, 116), 's1': (116,), 's3': (102,), '11': (168,), '34': (114,), 'T3': (112,), 'p4': (112,), 'T4': (110, 176), '23': (108,), 'p3': (100,), 'p2': (108,)}, 'noseam': ['13', '14', '23', '24', '32', '34', 'T2', 'p1', 'p3', 's0', 's1', 's4'], 'turned': '01', 'si_cut': 84, 'col0': (0,), 'last': 212, 'narrow': 0}
ORDER = 'iota.a ones.a jand.a sel.a jeq.a dj.m* load.a dj.i* big.a dj.h pads.a const.a half.a sel.b iota.b load.b const.b dj.j* const.c dj.b* dj.n* dj.p dj.l* dj.c big.b dj.k jrow.a jadd.a dj.a own.a own.b own.c own.d own.e ua.a uc.a ua.b dj.f* dj.d* dj.o* uc.c ub.a* dj.g* dj.e* uc.b* ub.b* load.c load.s0a load.s0b copy.1a copy.1b uc.d* ua.c col.s0c pre.s0c uc.e ub.c* cv0.a* uc.f* cv0.b* sum.s0c rest.s0c col.s0a col.s0b s0:0-26 pre.s0a pre.s0b sum.s0a sum.s0b rest.s0b s0:26-80* load.T0a copy.1d copy.1e copy.1f copy.e1a copy.1c pick.s0a rest.s0a take.s0a* s0:166-224* s0:80-118 send.s0a pick.s0b s0:118-166 take.s0b* list.x0a pick.s0c 10:0-72* 10:72-116 lhi.x0a llo.x0a xs.x0a take.s0c* 10:116-176* 10:176-224 pick.10a send.s0b send.s0c col.s1b col.s1a col.s1c pre.s1b pre.s1a pick.10b cv0.p0a* take.10a* xg.x0a cvs.s1a cvs.s1b cvs.s1c sum.s1b rest.s1b copy.2d sum.s1a rest.s1a* s1:62-116 s1:0-62* send.10a pre.s1c sum.s1c rest.s1c s1:178-224 pick.s1a s1:116-178* take.s1a* 20:116-224* list.x1a pick.s1b 20:0-116 copy.2c copy.e2a pick.20a pick.20b lhi.x1a take.s1b llo.x1a copy.2a copy.2b send.s1a sel.c xs.x1a send.s1b col.s2b col.s2a 11:90-168 cvs.s2a pre.s2a pre.s2b sum.s2a take.20a cvs.s2b xg.x1a rest.s2a sum.s2b rest.s2b s2:46-164 11:168-224* 11:0-90* pick.11c pick.11a pick.11b s2:164-224* take.11b* s2:0-46* take.11a* copy.e4a send.20a send.11b send.11a copy.3b copy.e3a 30:102-224 30:0-102* pick.s2a list.x2a pick.30a pick.30b take.s2a 21:0-102 lhi.x2a take.30a 12:0-92 llo.x2a copy.3c copy.3d 21:102-224* 12:92-224* pick.21a pick.21b pick.12a pick.12b take.21a* wrap.p0a copy.3a send.s2a send.30a cvs.s3a xs.x2a sel.d sel.e sel.f col.s3a send.21a p0:78-224* pre.s3a sum.s3a p0:0-78 xg.x2a rest.s3a copy.4d copy.4c s3:102-224* pick.p0a tadd.p0a pick.p0b take.12a s3:0-102 31:0-102 pick.s3a tadd.p0b list.x3a take.p0a take.s3a lhi.x3a low.p0a pick.s3b 31:102-224* llo.x3a T0:0-78 take.s3b pick.31a pick.31b T0:78-224* send.12a wrap.p3a copy.4a copy.4b send.s3a send.s3b wrap.p2a take.31a* wrap.p1a send.31a 22:144-224* turn.T0a 22:0-144 turn.T0b pick.22a cvs.s4a xs.x3a cvs.s4b col.s4b take.T0a* col.s4a send.T0a 13:118-224 xg.x3a p1:0-112 pre.s4b pre.s4a pick.22b sum.s4b sum.s4a 13:0-118* take.22a* rest.s4b* send.22a pick.13a rest.s4a p1:112-224* take.13a* mend.T0a send.13a pick.p1a tadd.p1a s4:0-134* s4:134-224 pick.s4a 23:108-224* pick.23b 32:0-130 23:0-108 take.p1a* take.s4a* 32:130-224* take.23b* low.p1a 14:0-118 pick.23a 14:118-224* take.23a send.23b cast.y4a store.y4a pick.32a T1:0-116 pick.14a take.32a T1:116-224* turn.T1a turn.T1b take.14a* 33:116-224* take.T1a* send.23a 33:0-116 pick.33a pick.33b send.32a send.14a send.T1a mend.T1a p2:0-108 p2:108-224* pick.p2a take.33a* 24:132-224* 24:0-132 send.33a pick.p2b tadd.p2a tadd.p2b take.p2a take.p2b low.p2a low.p2b T2:0-106 pick.24a take.24a p3:0-100 T2:106-224* pick.T2a take.T2a send.24a send.T2a p3:100-224* pick.p3a 34:76-116* 34:0-76 34:176-224 pick.p3b pick.34a tadd.p3a tadd.p3b take.p3a take.p3b low.p3a low.p3b T3:0-64 34:116-176* take.34a* pick.34b T3:64-122* take.34b* T3:122-170* send.34a send.34b wrap.p4a T3:170-224 pick.T3a take.T3a p4:0-50 pick.T3b p4:50-112* p4:112-174* send.T3a take.T3b p4:174-224 pick.p4a tadd.p4a send.T3b take.p4a low.p4a T4:0-52 T4:52-112* pick.p4b tadd.p4b pick.T4a take.p4b low.p4b T4:112-148 T4:148-176* pick.T4b T4:176-190 T4:190-212* take.T4a* take.T4b* store.T4a store.T4b gown.T4a pick.T4c scan.T4a ends.T4a take.T4c* store.T4c'
PAR = {'chunks': [0, 576, 1312, 2048], 'first_sum': [(148, 224), (80, 148), (0, 80)], 'g0': 2048, 'tails': 'YYGY', 'gx': [1792, 1792, 1344], 'gp': 896, 'dp': 1344, 'pace': 0, 'cuts': {'s0': (26, 116), 's1': (108,), 's3': (102,), '11': (168,), '34': (112,), 'T3': (112,), 'p4': (112,), 'T4': (110, 172), '23': (108,), 'p3': (98,), 'p2': (108,)}, 'noseam': ['13', '14', '23', '24', '32', '34', 'T0', 'T2', 'T4', 'p1', 'p2', 'p3', 'p4', 's2', 's3', 's4'], 'turned': '01', 'si_cut': 80, 'col0': (0,), 'last': 210, 'lanes': {'s0a': 1, 's0b': 1, 's0c': 1}}
ORDER = 'iota.a big.b ones.a jand.a sel.a jeq.a load.a const.c dj.e dj.l dj.m own.a dj.d dj.a* dj.o* dj.g* dj.b sel.b iota.b load.b load.c load.s0a load.s0b dj.c* dj.p big.a half.a dj.j* own.b const.a pads.a dj.i own.c ua.a jrow.a uc.a own.d ua.b own.e uc.c dj.n* dj.h* dj.f* ub.a* copy.1a dj.k* uc.b* copy.1b ub.b* uc.d* jadd.a col.s0c ua.c uc.e ub.c* cv0.a* uc.f* cv0.b* pre.s0c sum.s0c col.s0a col.s0b rest.s0c const.b s0:0-26 pre.s0a sum.s0a pre.s0b sum.s0b s0:26-80* copy.1d copy.1e copy.1f load.T0a copy.e1a copy.1c pick.s0a rest.s0b rest.s0a take.s0a* s0:168-224* s0:80-118 send.s0a pick.s0b s0:118-168 take.s0b* 10:0-74* list.x0a pick.s0c 10:74-116 lhi.x0a llo.x0a xs.x0a take.s0c* 10:174-224 pick.10a send.s0b send.s0c col.s1b col.s1a pre.s1b pre.s1a 10:116-174* xg.x0a pick.10b cvs.s1b cvs.s1a cv0.p0a take.10a* sum.s1b cvs.s1c rest.s1b copy.2d sum.s1a s1:56-108 rest.s1a* s1:0-56* col.s1c wrap.p1a send.10a pre.s1c sum.s1c rest.s1c s1:180-224 pick.s1a s1:108-180* take.s1a* 20:114-224* pick.s1b list.x1a 20:0-114 copy.2c copy.e2a pick.20a pick.20b lhi.x1a take.s1b llo.x1a copy.2a copy.2b xs.x1a send.s1a send.s1b col.s2b wrap.p0a col.s2a 11:92-168 cvs.s2a 11:168-224* pick.11c pre.s2a pre.s2b sum.s2a take.20a cvs.s2b xg.x1a rest.s2a sum.s2b rest.s2b take.11b s2:34-164 11:0-92* pick.11a pick.11b s2:0-34* s2:164-224* take.11a* send.20a send.11b send.11a 30:98-224 30:0-98* pick.s2a pick.30a pick.30b list.x2a take.s2a 21:0-96 take.30a lhi.x2a 12:0-94 llo.x2a copy.3c copy.3d 21:96-224* 12:94-224* pick.21a pick.21b pick.12a pick.12b take.21a* copy.3b copy.3a send.s2a cvs.s3a xs.x2a sel.c send.30a copy.e4a p0:0-72 xg.x2a send.21a col.s3a copy.e3a sel.d wrap.p2a sel.e p0:72-224* pre.s3a sum.s3a copy.4d pick.p0a tadd.p0a pick.p0b rest.s3a take.12a s3:102-224* s3:0-102 31:0-102 pick.s3a tadd.p0b list.x3a take.p0a lhi.x3a 31:102-224* take.s3a low.p0a llo.x3a pick.s3b pick.31a pick.31b T0:78-224* take.s3b* take.31a* send.12a copy.4c copy.4a send.s3a copy.4b send.s3b send.31a 22:144-224* T0:0-78 turn.T0a 22:0-144 turn.T0b pick.22a xs.x3a 13:118-224 cvs.s4b cvs.s4a col.s4a col.s4b pre.s4b pre.s4a pick.22b sum.s4b sum.s4a 13:0-118* take.T0a* take.22a* rest.s4b* p1:112-224* send.22a pick.13a take.13a* xg.x3a p1:0-112 rest.s4a send.T0a wrap.p3a send.13a wrap.p4a sel.f mend.T0a pick.p1a s4:0-136* s4:136-224 tadd.p1a pick.s4a 23:108-224* pick.23b 32:0-136 23:0-108 take.p1a take.s4a* 32:136-224* take.23b* 14:0-116 low.p1a pick.23a 14:116-224* take.23a send.23b pick.32a T1:0-112 pick.14a take.32a T1:112-224* turn.T1a turn.T1b take.14a* 33:116-224* take.T1a* send.23a 33:0-116 pick.33a pick.33b send.32a send.14a p2:0-108 p2:108-224* pick.p2a take.33a* 24:130-224* 24:0-130 send.T1a mend.T1a send.33a pick.p2b tadd.p2a tadd.p2b take.p2a take.p2b low.p2a low.p2b T2:0-108 pick.24a take.24a p3:0-98 T2:108-224* pick.T2a take.T2a send.24a send.T2a p3:98-224* pick.p3a 34:74-112* 34:0-74 34:174-224 pick.p3b pick.34a tadd.p3a tadd.p3b take.p3a take.p3b low.p3a low.p3b T3:0-64 34:112-174* take.34a* pick.34b T3:64-112* take.34b* T3:112-170* send.34a send.34b T3:170-224 pick.T3a take.T3a p4:0-54 pick.T3b p4:54-112* p4:112-178* take.T3b send.T3a cast.y4a send.T3b p4:178-224 pick.p4a tadd.p4a store.y4a take.p4a low.p4a T4:0-52 T4:52-112* pick.p4b tadd.p4b pick.T4a take.p4b low.p4b T4:112-144 T4:144-172* pick.T4b T4:172-194 T4:194-210* take.T4a* store.T4a take.T4b* store.T4b gown.T4a scan.T4a pick.T4c take.T4c* ends.T4a store.T4c'
PAR = {'chunks': [0, 576, 1376, 2048], 'first_sum': [(156, 224), (80, 156), (0, 80)], 'g0': 2560, 'tails': 'YYYG', 'gx': [1792, 1792, 896], 'gp': 896, 'dp': 1792, 'pace': 2, 'cuts': {'s0': (26, 120), 's1': (106,), 's3': (102,), '11': (172,), '34': (112,), 'T3': (112,), 'p4': (112,), 'T4': (108, 170), '23': (108,), 'p3': (100,), 'p2': (108,), '10': (116,)}, 'noseam': ['10', '13', '14', '23', '24', '32', 'T0', 'T2', 'T3', 'T4', 'p1', 'p2', 's4'], 'turned': '01', 'si_cut': 88, 'col0': (0,), 'last': 208, 'lanes': {'s0a': 1}}
ORDER = 'load.a iota.a ones.a pads.a jand.a sel.a jeq.a dj.l* own.a iota.b sel.b load.b load.c load.s0a load.s0b own.b half.a own.c dj.k* const.a dj.o dj.e big.b own.d big.a dj.n const.c jrow.a dj.b dj.a* dj.f* dj.h* dj.j* dj.i* dj.m const.b ua.a ub.a* uc.b* dj.g uc.a dj.d* dj.p ub.b* jadd.a copy.1a copy.1b ua.b dj.c uc.c uc.d* ua.c cv0.a col.s0c* ub.c* uc.f* pre.s0c sum.s0c uc.e own.e rest.s0c cv0.b* s0:0-26 col.s0a col.s0b pre.s0a sum.s0a pre.s0b sum.s0b s0:26-80* copy.1d copy.1e copy.1f load.T0a copy.e1a copy.1c pick.s0a rest.s0b rest.s0a s0:80-120 take.s0a* s0:170-224* send.s0a pick.s0b s0:120-170 take.s0b* 10:0-74* list.x0a pick.s0c 10:74-116 lhi.x0a llo.x0a xs.x0a take.s0c* 10:116-180* 10:180-224 pick.10a send.s0b send.s0c col.s1a col.s1b take.10a* send.10a pre.s1b pre.s1a cvs.s1a cvs.s1b sum.s1a sum.s1b pick.10b rest.s1a rest.s1b cvs.s1c xg.x0a* col.s1c pre.s1c copy.2c s1:0-64* s1:64-120 sum.s1c rest.s1c take.10b copy.2a send.10b s1:168-224* pick.s1a s1:120-168 take.s1a 11:0-94* pick.s1b list.x1a 20:0-114 copy.e2a pick.11a pick.20a lhi.x1a take.s1b llo.x1a cv0.p0a 20:114-224* send.s1a copy.2b xs.x1a send.s1b col.s2a sel.c wrap.p0a sel.d col.s2b pre.s2a cvs.s2a sum.s2a pick.20b 11:94-172 rest.s2a xg.x1a cvs.s2b 11:172-224* s2:42-96 take.20a* pre.s2b pick.11b sum.s2b pick.11c take.11a s2:0-42* rest.s2b* s2:96-164 take.11b* s2:164-224* send.20a send.11a send.11b sel.e copy.3b copy.3a 30:98-224 30:0-98* pick.s2a pick.s2b list.x2a pick.30a pick.30b 21:88-224* lhi.x2a take.s2a 21:0-88 take.30a 12:0-96 pick.21a pick.21b copy.3c 12:96-224* pick.12a pick.12b send.s2a send.30a take.21a llo.x2a cvs.s3a xs.x2a p0:0-72 xg.x2a copy.e3a wrap.p1a send.21a col.s3a p0:72-224* pre.s3a sum.s3a pick.p0a tadd.p0a pick.p0b rest.s3a take.12a s3:102-224* s3:0-102 31:0-102 pick.s3a tadd.p0b list.x3a 31:102-224* take.p0a lhi.x3a take.s3a low.p0a llo.x3a T0:0-74 pick.s3b pick.31a pick.31b T0:74-224* take.s3b* take.31a* copy.4c send.12a copy.4b wrap.p3a copy.4a send.s3a send.s3b send.31a 22:144-224* turn.T0a 22:0-144 turn.T0b pick.22a xs.x3a 13:118-224 cvs.s4b cvs.s4a xg.x3a take.T0a* col.s4b send.T0a col.s4a copy.e4a pre.s4b pick.22b pre.s4a sum.s4b sum.s4a 13:0-118* rest.s4b* take.22a* p1:0-112* pick.13a take.13a* p1:112-224 rest.s4a send.22a mend.T0a send.13a pick.p1a s4:0-134* s4:134-224 tadd.p1a pick.s4a 23:108-224* pick.23b 32:0-136 23:0-108 take.p1a take.s4a* 32:136-224* take.23b* 14:0-116 low.p1a pick.23a 14:116-224* take.23a send.23b pick.32a T1:0-110 pick.14a take.32a T1:110-224* turn.T1a turn.T1b take.14a* 33:116-224* take.T1a* send.23a send.32a wrap.p2a 33:0-116 pick.33a pick.33b p2:0-108 p2:108-224* pick.p2a take.33a* send.14a wrap.p4a send.T1a cast.y4a sel.f send.33a mend.T1a 24:128-224* 24:0-128 pick.p2b tadd.p2a tadd.p2b take.p2a take.p2b low.p2a low.p2b T2:0-108 pick.24a take.24a p3:0-100 T2:108-224* pick.T2a take.T2a send.24a send.T2a p3:100-224* pick.p3a 34:72-112* 34:0-72 34:174-224 pick.p3b pick.34a tadd.p3a tadd.p3b take.p3a take.p3b low.p3a low.p3b T3:0-62 34:112-174* take.34a* pick.34b T3:62-112* take.34b* T3:112-170* send.34a send.34b T3:170-224 pick.T3a take.T3a p4:0-54 pick.T3b p4:54-112* p4:112-178* take.T3b send.T3a send.T3b p4:178-224 pick.p4a tadd.p4a store.y4a take.p4a low.p4a T4:0-54 T4:54-112* pick.p4b tadd.p4b pick.T4a take.p4b low.p4b T4:142-170 T4:112-142* pick.T4b T4:170-194 T4:194-208* take.T4a* store.T4a take.T4b* store.T4b pick.T4c take.T4c* gown.T4a scan.T4a ends.T4a store.T4c'
PAR = {'chunks': [0, 576, 1312, 2048], 'first_sum': [(148, 224), (80, 148), (0, 80)], 'g0': 1536, 'tails': 'YYGG', 'gx': [1792, 896, 1792], 'gp': 896, 'dp': 896, 'pace': 1, 'cuts': {'s0': (28, 120), 's1': (106,), 's3': (100,), '11': (172,), '34': (112,), 'T3': (112,), 'p4': (112,), 'T4': (108, 172), '23': (110,), 'p3': (100,), 'p2': (108,), '10': (116,)}, 'noseam': ['13', '14', '23', '24', '32', 'T0', 'T2', 'T3', 'p1', 'p2', 's0', 's3', 's4'], 'turned': '01', 'si_cut': 80, 'col0': (0,), 'last': 208, 'lanes': {'s0a': 1, 's0b': 1, 's0c': 1, '10a': 1}}
ORDER = 'load.a ones.a iota.a big.b const.c jand.a pads.a const.b const.a jrow.a jeq.a own.a big.a sel.a dj.o* dj.a* dj.m* dj.d* dj.p* dj.f* dj.b* dj.i own.b dj.k half.a dj.e own.c dj.n dj.c own.d dj.j own.e ua.a dj.h load.b load.s0a load.c load.s0b ub.a* uc.b* ub.b* uc.a ua.b sel.b iota.b copy.1a dj.l uc.c uc.d* cv0.a* col.s0c* pre.s0c sum.s0c jadd.a ua.c rest.s0c uc.e dj.g ub.c* uc.f* cv0.b* s0:0-28 col.s0a col.s0b copy.1b pre.s0a sum.s0a pre.s0b sum.s0b s0:28-80* copy.1d copy.1e copy.e2a copy.1f copy.1c copy.e1a pick.s0a rest.s0b rest.s0a s0:80-120 take.s0a* s0:168-224* send.s0a pick.s0b s0:120-168 take.s0b* 10:0-64* list.x0a pick.s0c 10:64-116 lhi.x0a llo.x0a xs.x0a take.s0c* 10:116-186* pick.10a send.s0b send.s0c col.s1a col.s1b col.s1c pre.s1a cvs.s1a 10:186-224 sum.s1a pre.s1b cvs.s1b rest.s1a sum.s1b rest.s1b cvs.s1c take.10a* xg.x0a* send.10a s1:0-62* s1:62-114 pre.s1c pick.10b sum.s1c rest.s1c take.10b copy.2a send.10b s1:172-224 pick.s1a s1:114-172* take.s1a 11:0-100* list.x1a pick.s1b 20:0-116 copy.2c load.T0a copy.2d pick.11a pick.20a lhi.x1a take.s1b 20:116-224* send.s1a copy.2b send.s1b llo.x1a cvs.s2a xs.x1a col.s2a sel.c wrap.p1a col.s2b sel.d pre.s2a sum.s2a 11:100-172 rest.s2a xg.x1a cvs.s2b 11:172-224* s2:40-96 pick.20b take.20a* pre.s2b pick.11b sum.s2b pick.11c take.11a s2:0-40* rest.s2b* s2:96-164 take.11b* s2:164-224* send.20a send.11a wrap.p0a send.11b copy.3a 30:98-224 30:0-98* pick.s2a pick.s2b list.x2a pick.30a pick.30b 21:88-224* take.s2a 21:0-88 pick.21a pick.21b lhi.x2a take.30a 12:0-96 copy.3b copy.3c copy.3d send.s2a send.30a take.21a send.21a cvs.s3a llo.x2a cv0.p0a xs.x2a p0:0-72 xg.x2a 12:96-224* pick.12a pick.12b sel.e col.s3a copy.e3a p0:72-224* pre.s3a sum.s3a rest.s3a pick.p0a tadd.p0a take.12a s3:100-224* s3:0-100 pick.p0b tadd.p0b pick.s3a list.x3a 31:0-104 31:104-224* take.p0a lhi.x3a low.p0a llo.x3a take.s3a T0:0-70 pick.s3b pick.31a pick.31b T0:70-224* take.s3b* take.31a* copy.4c copy.4a send.12a wrap.p3a wrap.p2a copy.4b copy.e4a copy.4d send.s3a send.s3b send.31a 22:144-224* turn.T0a 22:0-144 turn.T0b pick.22a cvs.s4a xs.x3a 13:118-224 cvs.s4b col.s4b col.s4a pre.s4b pre.s4a pick.22b xg.x3a p1:112-224 sum.s4a rest.s4a sum.s4b take.T0a* 13:0-118* take.22a* rest.s4b* p1:0-112* pick.13a take.13a* send.T0a send.22a send.13a mend.T0a sel.f pick.p1a s4:0-134* s4:134-224 tadd.p1a pick.s4a 23:110-224* pick.23b 32:0-134 take.p1a 23:0-110 take.s4a* 32:134-224* take.23b* low.p1a 14:0-110 pick.23a 14:110-224* take.23a send.23b send.23a pick.32a T1:0-118 pick.14a take.32a T1:118-224* turn.T1a turn.T1b take.14a* 33:116-224* take.T1a* send.32a send.14a send.T1a 33:0-116 pick.33a pick.33b p2:0-108 p2:108-224* pick.p2a take.33a* mend.T1a send.33a 24:128-224* 24:0-128 pick.p2b tadd.p2b tadd.p2a take.p2a take.p2b low.p2a low.p2b T2:0-108 pick.24a take.24a p3:0-100 T2:108-224* pick.T2a take.T2a send.24a wrap.p4a send.T2a p3:100-224* pick.p3a 34:74-112* 34:0-74 34:174-224 pick.p3b pick.34a tadd.p3a tadd.p3b take.p3a take.p3b low.p3a low.p3b T3:0-62 34:112-174* take.34a* pick.34b T3:62-112* take.34b* T3:112-170* cast.y4a send.34a send.34b T3:170-224 pick.T3a take.T3a p4:0-54 pick.T3b p4:54-112* p4:112-178* take.T3b send.T3a send.T3b p4:178-224 pick.p4a tadd.p4a store.y4a take.p4a low.p4a T4:0-54 T4:54-110* pick.p4b tadd.p4b pick.T4a take.p4b low.p4b T4:140-172 T4:110-140* pick.T4b T4:172-190 T4:190-208* take.T4a* take.T4b* pick.T4c gown.T4a scan.T4a store.T4a store.T4b ends.T4a take.T4c* store.T4c'
PLAN = arrange(PAR, ORDER)
SEMAPHORES = ["cV", "cS", "cP", "cG", "gone"] + PLAN["names"]


def rank_program(g, core, T, topo):
    rank = T.rank_of(core)
    if rank is None:
        return
    order, slot, last = PLAN["order"], PLAN["slot"], PAR["last"]
    Q = {"V": g.vector, "S": g.scalar, "P": g.tensor, "G": g, "Y": g.sync}
    V, S, P = g.vector, g.scalar, g.tensor

    def peer(d):
        return T.cores[(rank + d) % NR]

    def engines(o, src, dst):
        use = topo.engines(src, dst)
        return use if o["lane"] == 3 else use[o["lane"] - 1::2]

    mark, total = {}, {}
    for e in order:
        for o in order[e]:
            if o["kind"] == "send":
                mark[o["ix"]] = (o["sem"], len(engines(o, peer(-o["dist"]), core)))
            elif o["sem"]:
                mark[o["ix"]] = (o["sem"], 16)
            else:
                total["c" + e] = total.get("c" + e, 0) + 1
                mark[o["ix"]] = ("c" + e, total["c" + e])
    gone = [0]

    def plus(e, out, in_, c):
        if e == "V":
            return V.tensor_scalar(out, in_, c, None, A.add)
        return S.activation(out, in_, F.Identity, bias=c)

    def move(out, in_, n):
        return g.affine_select(out, in_, [[0, n]], A.is_ge, 0.0, 0, 0)

    def emit(o, e):
        k = o["kind"]
        t, lo, hi = o.get("t"), o.get("lo"), o.get("hi")
        Xt = T["X%d" % t] if t is not None else None
        bank = T["ps%d" % slot[o["bank"]]] if "bank" in o else None
        Gb = T["G%d" % slot[o["g"]]] if "g" in o else None
        if k in ("load", "store"):
            return Q[e].dma_start(T[o["dst"]][:, lo:hi], T[o["src"]][:, lo:hi])
        if k == "copyx":
            return Q[e].dma_start(T["X%d" % o["to"]][:, lo:hi], Xt[:, lo:hi])
        if k == "copyg":
            return move(T["X%d" % o["to"]][:, lo:hi], Xt[:, lo:hi], hi - lo)
        if k == "send":
            dst = peer(o["dist"])
            rid, pid, _ = topo.addr(dst)
            w, use = o["w"], engines(o, core, dst)
            if o["src"]:
                g.remote_dma(T[o["dst"]][:, o["d0"]:o["d0"] + w], T[o["src"]][:, o["s0"]:o["s0"] + w], T.sem[o["sem"]], T.sem["gone"],
                             pid, rid, sum(1 << x for x in use))
            else:
                c = o["c"]
                g.remote_dma_fused([RemoteDMATransfer(dst_ids=[DstId(rid=rid, pnc=pid)], dma_engine_mask=sum(1 << x for x in use[nxt::2]),
                                                      remote_sem=T.sem[o["sem"]], src=T.tout[:, c + nxt:c + nxt + w],
                                                      dst=(T.tnx if nxt else T.tin)[:, c:c + w]) for nxt in (0, 1)],
                                   local_sem=T.sem["gone"])
            gone[0] += len(use)
            return None
        if k == "mend":
            c, w = o["c"], o["w"]
            return move(T.tnx[:, c + 15:c + w:16], T.tin[:, c:c + w:16], w // 16)
        if k == "cast":
            return move(T.ysf[:, lo:hi], T.U[:, o["c"] + lo:o["c"] + hi], hi - lo)
        if k == "pads":
            return V.tensor_copy(T.tout[:, 0:8 * TW:8], T.one[:, 0:TW])
        if k == "ones":
            return V.memset(T.one[:], 1.0)
        if k == "const":
            return V.tensor_scalar(T[o["buf"]][:], T.one[:, lo:hi], o["c"], None, A.mult)
        if k == "iota":
            return g.iota(T[o["buf"]][:], o["pat"], o["base"], o["cm"])
        if k == "sel":
            w = o["which"]
            if w == "II":
                return g.affine_select(T.II[:], T.one[:], [[0, 2], [-1, 128]], A.is_equal, 0.0, 0, 1)
            if w == "EW":
                return g.affine_select(T.EW[:], T.one[:, 0:144], [[-16, 9], [128, 16]], A.is_equal, 0.0, 16, 1)
            if w == "run":
                return g.affine_select(T.run[:], T.one[:], [[0, 16], [1, 16]], A.not_equal, 0.0, 0, 0)
            if w == "T1":
                return g.affine_select(T.TT[:], T.II[:], [[0, 2], [-1, 128]], A.not_equal, 1.0, -1, 1)
            if w == "T2":
                return g.affine_select(T.TT[:, 15:256:16], T.TT[:, 15:256:16], [[0, 2], [-16, 8]], A.not_equal, 0.0, -16, 1)
            return g.affine_select(T.TT[:, 15:256:16], T.TT[:, 15:256:16], [[0, 2], [-16, 8]], A.not_equal, 1.0, 0, 1)
        if k == "jand":
            return V.tensor_scalar(T.jc[:], T.ja[:], 15, None, A.bitwise_and)
        if k == "jeq":
            return V.tensor_scalar(T.mk[:], T.jc[:], 0.0, None, A.is_equal)
        if k == "own":
            w = o["w"]
            return V.tensor_copy(T.own[:, w:2 * w], T.own[:, 0:w]) if w else V.tensor_copy(T.own[:, 0:16], T.mk[:])
        if k == "dj":
            j = o["j"]
            if e == "V":
                return V.tensor_scalar(T.D[:, 128 * j:128 * j + 128], T.II[:, 0:128], T.mk[:, j:j + 1], None, A.mult)
            return S.activation(T.D[:, 128 * j:128 * j + 128], T.II[:, 0:128], F.Identity, scale=T.mk[:, j:j + 1])
        if k == "jrow":
            return V.tensor_scalar(T.jr[:], T.jc[:], 16.0, 7.5, A.mult, A.add)
        if k == "jadd":
            return V.tensor_scalar(T.jd[:], T.jb[:], T.jr[:, 0:1], None, A.add)
        if k == "cv0":
            return plus(e, T[o["dst"]][:, lo:hi], T[o["src"]][:, lo:hi], -2048.0)
        if k == "ua":
            return V.tensor_scalar(T.X0[:, lo:hi], T.pw[:, lo:hi], W - 1, None, A.bitwise_and)
        if k == "ub":
            return S.activation(T.X0[:, H + lo:H + hi], T.pw[:, lo:hi], F.Identity, bias=-(2.0 ** 23 - 2048.5) / W, scale=1.0 / W)
        if k == "uc":
            return plus(e, T.X0[:, lo:hi], T.X0[:, lo:hi], -2047.0)
        if k == "wrap":
            return move(Xt[:, W:W + 1], Xt[:, 0:1], 1)
        if k == "cvs":
            c = (L_S * RO + t) * I
            return V.tensor_scalar(T.s16[:, t * I + lo:t * I + hi], T.L[:, c + lo:c + hi], -2048.0, None, A.add)
        if k == "col":
            if e != "G":
                return plus(e, T.col[:, t * I + lo:t * I + hi], Xt[:, 16 * lo + t:16 * hi:16], 0.0)
            return move(T.col[:, t * I + lo:t * I + hi], Xt[:, 16 * lo + t:16 * hi:16], hi - lo)
        if k == "big":
            return V.memset(T.cM[:, lo:lo + I], o["c"])
        if k == "half":
            return V.tensor_scalar(T.NH[:], T.II[:], -0.5, None, A.mult)
        if k == "pre":
            P.matmul(bank[:, lo:hi], T.one[:, 0:128], T.cN[:, lo:hi], True, False)
            return P.matmul(bank[:, lo:hi], T.NH[:, 0:128], T.col[:, t * I + lo:t * I + hi], False, False)
        if k == "sum":
            sh = 80 if t else 0
            P.matmul(bank[:, lo:hi], T.NH[:, sh:sh + 128], T.s16[:, t * I + lo:t * I + hi], False, False)
            P.matmul(bank[:, lo:hi], T.one[:, 0:128], T.cM[:, lo:hi], False, False)
            P.matmul(bank[:, lo:hi], T.one[:, 0:128], T.cM[:, I + lo:I + hi], False, False)
            P.matmul(bank[:, lo:hi], T.II[:, 0:128], T.col[:, t * I + lo:t * I + hi], False, False)
            return P.matmul(bank[:, lo:hi], T.II[:, sh:sh + 128], T.s16[:, t * I + lo:t * I + hi], False, True)
        if k in ("take", "rest"):
            return plus(e, T[o["dst"]][:, o["d0"] + lo:o["d0"] + hi], bank[:, lo:hi], o["c"])
        if k == "low":
            c = (U_T * RO + t) * I
            return V.tensor_tensor(T.U[:, c + lo:c + hi], bank[:, lo:hi], T.hT[:, t * I + lo:t * I + hi], A.subtract)
        if k == "gath":
            win = Xt[:, 0:o["width"]].indirect(T[o["obuf"]][:, o["o0"] + lo:o["o0"] + hi])
            return plus(e, T["G%d" % slot[o["virt"][0]]][:, 16 * lo:16 * hi], win, -1.0)
        if k == "gown":
            c = (U_T * RO + t) * I
            return V.tensor_tensor(T.gm[:, 0:o["n"]], Xt[:, 0:W].indirect(T.U[:, c + last:c + I]), T.own[:, 0:o["n"]], A.mult)
        if k == "scan":
            n = 2 * o["n"]
            return V.tensor_tensor_scan(T.gs[:, 0:n], T.run[:, 0:n], T.gm[:, 0:n], 0.0, A.mult, A.add)
        if k == "ends":
            return V.tensor_scalar(T.ytf[:, last:I], T.gs[:, 15:16 * o["n"]:16], 2047.0, None, A.add)
        if k == "pick":
            if o["extra"]:
                P.matmul(bank[:, lo:hi], T.one[:, 0:128], T.cT[:, lo:hi], True, False)
            for j in range(16):
                r = P.matmul(bank[:, lo:hi], T.D[:, 128 * j:128 * j + 128], Gb[:, 16 * lo + j:16 * hi:16],
                             j == 0 and not o["extra"], j == 15 and not o["extra"])
            return r
        if k == "turn":
            j = o["j"]
            for a in range(16):
                r = P.matmul(bank[:, o["c"] + a:o["c"] + 128:16], Gb[:, 16 * TB * j + a:16 * (TB * j + 128):16],
                             T.II[:, 80 + a:208:16], True, True)
            return r
        if k == "tadd":
            if not o["sub"]:
                sh = 80 if t else 0
                return P.matmul(bank[:, lo:hi], T.TT[:, sh:sh + 128], T[o["src"]][:, o["c"] + lo:o["c"] + hi], False, True)
            for (a, b, j, c) in o["sub"]:
                for nxt in (0, 1):
                    r = P.matmul(bank[:, a:b], (T.tnx if nxt else T.tin)[:, c:c + 128], T.II[:, a - TB * j:b - TB * j],
                                 False, nxt == 1 and b == hi)
            return r
        c = 16 * t
        if k == "list":
            P.matmul(bank[:, 0:14], T.one[:, 0:128], T.cl[:, 0:14], True, False)
            for a in range(16):
                r = P.matmul(bank[:, 0:14], T.EW[:, 16 - a:144 - a], Gb[:, 16 * a:XE:256], False, a == 15)
            return r
        if k == "lhi":
            return V.tensor_tensor(T.hl[:, c:c + 14], bank[:, 0:14], T.jd[:, 0:14], A.subtract)
        if k == "llo":
            return V.tensor_tensor(T.lx[:, c:c + 14], bank[:, 0:14], T.hl[:, c:c + 14], A.subtract)
        if k == "xg":
            return plus(e, T["X%d" % (t + 1)][:, t:XE:16], Xt[:, 0:XE].indirect(T.lx[:, c:c + 14]), 0.0)
        return V.tensor_copy(T["X%d" % (t + 1)][:, 0:XE].indirect(T.lx[:, c:c + 14]), Xt[:, t:XE:16])

    for e in order:
        seen = {}
        for o in order[e]:
            need = {}
            for d in o["deps"]:
                s, c = mark[d]
                if e == "P" and s == "cP":
                    continue
                need[s] = max(need.get(s, 0), c)
            for s in sorted(need):
                if seen.get(s, 0) < need[s]:
                    Q[e].wait_ge(T.sem[s], need[s])
                    seen[s] = need[s]
            r = emit(o, e)
            if r is not None:
                s, c = mark[o["ix"]]
                r.then_inc(T.sem[s], 16 if o["sem"] else 1)
    for o in order["Y"]:
        if o["kind"] == "store":
            g.sync.wait_ge(T.sem[o["sem"]], 16)
    for s in sorted(total):
        g.wait_ge(T.sem[s], total[s])
    g.wait_ge(T.sem["gone"], gone[0])
